import numpy as np
import ml_dtypes


def mxq(x, axis, fmt="e4m3"):
    dtype, down = {"e4m3": (ml_dtypes.float8_e4m3fn, 7), "e5m2": (ml_dtypes.float8_e5m2, 14)}[fmt]
    v = np.moveaxis(np.asarray(x, np.float32).astype(ml_dtypes.bfloat16).astype(np.float64), axis, -1)
    blocks = v.reshape(v.shape[:-1] + (-1, 32))
    amax = np.abs(blocks).max(-1, keepdims=True)
    byte = np.maximum(np.where(amax > 0, np.frexp(amax)[1] - 1 + 127, 0) - down, 1)
    scale = np.exp2(byte - 127.0)
    codes = (blocks / scale).astype(np.float32).astype(dtype).astype(np.float64)
    return np.moveaxis((codes * scale).reshape(v.shape), -1, axis)


WIDE = False


def mx_kscale(k):
    if not WIDE:
        return np.ones(k)
    levels = np.array([10, -10, 5, -5, 0])
    if k % 512:
        return np.exp2(np.random.permutation(np.resize(levels, k // 32))).repeat(32)
    a = np.empty((k // 512, 16))
    for p in range(k // 512):
        a[p, :8] = np.random.permutation(np.resize(levels, 8))
        for g in range(8):
            far = levels[np.abs(levels - a[p, g]) >= 10]
            a[p, g + 8] = far[np.random.randint(len(far))]
    return np.exp2(a.ravel()).repeat(32)


def f64(x):
    return np.asarray(x).astype(np.float64)


def striped(idx):
    return np.tile(idx.reshape(-1, 16).T, (8, 1)).astype(np.uint16)


def unstriped(offs):
    return offs[:16].T.reshape(-1).astype(np.int64)


E2M1 = np.array([0.0, 0.5, 1.0, 1.5, 2.0, 3.0, 4.0, 6.0, -0.0, -0.5, -1.0, -1.5, -2.0, -3.0, -4.0, -6.0])


def pack_weight(w, fmt):
    k, n = w.shape
    w = f64(np.asarray(w, np.float32).astype(ml_dtypes.bfloat16)).reshape(k // 32, 32, n)
    amax = np.abs(w).max(1)
    if fmt == "e4m3":
        byte = np.frexp(amax)[1] - 1 + 127 - 7
    else:
        mant, ex = np.frexp(amax / 6.0)
        byte = np.where(mant > 0.5, ex, ex - 1) + 127
    byte = np.clip(np.where(amax > 0, byte, 1), 1, 254)
    scaled = (w * np.exp2(127.0 - byte)[:, None, :]).reshape(k, n).astype(np.float32)
    by_word = np.ascontiguousarray(scaled.reshape(k // 512, 128, 4, n).transpose(0, 1, 3, 2))
    if fmt == "e4m3":
        words = by_word.astype(ml_dtypes.float8_e4m3fn).view(np.uint8)
    else:
        c = by_word.astype(ml_dtypes.float4_e2m1fn).view(np.uint8) & 0xF
        words = (c[..., 0::2] | (c[..., 1::2] << 4)).reshape(k // 512, 128, 2 * n)
    return np.ascontiguousarray(words), np.ascontiguousarray(byte.astype(np.uint8).reshape(k // 512, 16, n))


def unpack_weight(words, scales, fmt):
    g, _, n = scales.shape
    words = np.ascontiguousarray(words).reshape(g, 128, n, -1)
    if fmt == "e4m3":
        vals = words.view(ml_dtypes.float8_e4m3fn).astype(np.float64)
    else:
        nib = np.empty((g, 128, n, 4), np.uint8)
        nib[..., 0::2] = words & 0xF
        nib[..., 1::2] = words >> 4
        vals = E2M1[nib]
    vals = vals * np.repeat(np.exp2(scales.astype(np.float64) - 127.0), 8, axis=1)[..., None]
    return vals.transpose(0, 1, 3, 2).reshape(g * 512, n)


def gelu(v):
    return 0.5 * v * (1.0 + np.tanh(np.sqrt(2.0 / np.pi) * (v + 0.044715 * v**3)))


K, H, T, S, T2 = 1024, 512, 2048, 1024, 2048

def setup_inputs():
    n = np.random.standard_normal
    s = mx_kscale(K)[:, None]
    u = mx_kscale(H)[:, None]
    tab_words, tab_scales = pack_weight(n((K, T)) * s, "e4m3")
    w1_words, w1_scales = pack_weight(n((K, H)) / np.sqrt(K) / s, "e2m1")
    return {
        "tab_words": tab_words, "tab_scales": tab_scales,
        "w1_words": w1_words, "w1_scales": w1_scales,
        "xT": (np.round(16 * n((K, T2))) / 16 * s).astype(np.float32),
        "w2": (n((K, H)) / np.sqrt(2 * K) / s).astype(np.float32),
        "w3": (n((H, H)) / np.sqrt(H) / u).astype(np.float32),
        "lam": np.random.uniform(0.2, 0.8, H).astype(np.float32),
        "gain": (np.random.uniform(0.7, 2.0, H) * u[:, 0]).astype(np.float32),
        "offs": striped(np.random.permutation(T)[:S]),
        "offs2": striped(np.random.permutation(T2)[:S]),
        "offs3": striped(np.random.permutation(T2)[:S]),
    }

def reference(tab_words, tab_scales, w1_words, w1_scales, xT, w2, w3, lam, gain, offs, offs2, offs3):
    v = unpack_weight(tab_words, tab_scales, "e4m3")[:, unstriped(offs)]
    w1 = unpack_weight(w1_words, w1_scales, "e2m1")
    x = f64(xT)[:, unstriped(offs2)] - f64(xT)[:, unstriped(offs3)]
    a = w1.T @ v
    b = mxq(f64(w2), 0, "e4m3").T @ mxq(x, 0, "e4m3")
    z = f64(gain)[:, None] * (b + f64(lam)[:, None] * (a - b))
    y = mxq(f64(w3), 0, "e4m3").T @ mxq(z, 0, "e4m3")
    return np.minimum(y, a)

@@ -1,0 +1,260 @@
+from contextlib import ExitStack
+
+import concourse.mybir as mybir
+
+K, H, T, S = 1024, 512, 2048, 1024
+FLOPS = 2 * K * H * S * 2 + 2 * H * H * S
+
+F32 = mybir.dt.float32
+BF16 = mybir.dt.bfloat16
+I32 = mybir.dt.int32
+U32 = mybir.dt.uint32
+U16 = mybir.dt.uint16
+U8 = mybir.dt.uint8
+E4M3 = mybir.dt.float8_e4m3fn_x4
+E2M1 = mybir.dt.float4_e2m1fn_x4
+ALU = mybir.AluOpType
+ACT = mybir.ActivationFunctionType
+
+P = 128
+PACK = 4
+PASSES = K // (P * PACK)
+HALF = 512
+CHUNK = 256
+
+
+def tile_list_storm_index_cap_kernel(
+    tc, tab_words, tab_scales, w1_words, w1_scales, xT, w2, w3, lam, gain, offs, offs2, offs3, out
+):
+    nc = tc.nc
+    with ExitStack() as ctx:
+        lists = ctx.enter_context(tc.tile_pool(name="lists", bufs=1))
+        keep = ctx.enter_context(tc.tile_pool(name="keep", bufs=1))
+        ring = ctx.enter_context(tc.tile_pool(name="ring", bufs=2))
+        stores = ctx.enter_context(tc.tile_pool(name="stores", bufs=4))
+        psum = ctx.enter_context(tc.psum_pool(name="psum", bufs=4))
+
+        list1 = lists.tile([P, S // 16], U16, name="list1")
+        list2 = lists.tile([P, S // 16], U16, name="list2")
+        list3 = lists.tile([P, S // 16], U16, name="list3")
+
+        tab_s = keep.tile([P, T], U8, name="tab_s")
+        w1_s = keep.tile([P, PASSES, H], U8, name="w1_s")
+        v_s1 = keep.tile([P, S], U8, name="v_s1", align_bytes=64)
+        nc.vector.memset(tab_s[:].bitcast(I32), 0)
+        nc.vector.memset(w1_s[:].rearrange("p a c -> p (a c)").bitcast(I32), 0)
+        nc.vector.memset(v_s1[:].bitcast(I32), 0)
+
+        planes = [keep.tile([P, T], F32, name=f"plane{n}") for n in range(PASSES * PACK)]
+        tab_w = [keep.tile([P, T], I32, name=f"tab_w{a}") for a in range(PASSES)]
+        w1_w = keep.tile([P, PASSES, H // 2], I32, name="w1_w")
+        lam_t = keep.tile([P, PACK], F32, name="lam_t")
+        gain_t = keep.tile([P, PACK], F32, name="gain_t")
+        x_rows = xT.rearrange("(a p i) t -> a i p t", a=PASSES, i=PACK)
+
+        def load_plane(n):
+            nc.sync.dma_start(planes[n][:], x_rows[n // PACK, n % PACK])
+
+        def load_tab(a):
+            nc.sync.dma_start(tab_w[a][:], tab_words[a].rearrange("p t i -> p (t i)").bitcast(I32))
+
+        def load_weight(rows):
+            raw = ring.tile([P, PACK, H], F32, name="w_raw")
+            nc.sync.dma_start(raw[:], rows.rearrange("(p j) c -> p j c", j=PACK))
+            return raw
+
+        nc.sync.dma_start(list1[:], offs)
+        nc.sync.dma_start(list3[:], offs3)
+        nc.sync.dma_start(list2[:], offs2)
+        load_plane(0)
+        for q in range(4):
+            nc.scalar.dma_start(
+                tab_s[32 * q : 32 * q + 8, :].bitcast(I32), tab_scales[:, 4 * q : 4 * q + 4, :].bitcast(I32)
+            )
+        load_plane(1)
+        nc.sync.dma_start(w1_w[:], w1_words.rearrange("a p b -> p a b").bitcast(I32))
+        for q in range(4):
+            nc.scalar.dma_start(
+                w1_s[32 * q : 32 * q + 4, :, :].bitcast(I32),
+                w1_scales[:, 4 * q : 4 * q + 4, :].rearrange("a r c -> r a c").bitcast(I32),
+            )
+        nc.scalar.dma_start(lam_t[:], lam.rearrange("(p t) -> p t", t=PACK))
+        nc.scalar.dma_start(gain_t[:], gain.rearrange("(p t) -> p t", t=PACK))
+        load_tab(0)
+        load_plane(2)
+        load_tab(1)
+        w2_raw = [load_weight(w2[0:512, :])]
+        load_plane(3)
+        load_plane(4)
+        w2_raw.append(load_weight(w2[512:1024, :]))
+        load_plane(5)
+        load_plane(6)
+        load_plane(7)
+        w3_raw = load_weight(w3)
+
+        v_s0 = keep.tile([P, S], U8, name="v_s0", align_bytes=64)
+        nc.vector.tensor_copy(v_s0[:], tab_s[:].indirect(list1[:]))
+        for q in range(4):
+            nc.scalar.dma_start(
+                v_s1[32 * q : 32 * q + 4, :].bitcast(I32), v_s0[32 * q + 4 : 32 * q + 8, :].bitcast(I32)
+            )
+        v_s = [v_s0, v_s1]
+
+        c_a = keep.tile([P, PACK], F32, name="c_a")
+        c_b = keep.tile([P, PACK], F32, name="c_b")
+        rest = keep.tile([P, PACK], F32, name="rest")
+        nc.gpsimd.tensor_tensor(c_a[:], gain_t[:], lam_t[:], ALU.mult)
+        nc.gpsimd.tensor_scalar(rest[:], lam_t[:], -1.0, 1.0, ALU.mult, ALU.add)
+        nc.gpsimd.tensor_tensor(c_b[:], gain_t[:], rest[:], ALU.mult)
+
+        def difference(a, i, j0, width, dest):
+            window = planes[PACK * a + i]
+            cols = slice(j0 // 16, (j0 + width) // 16)
+            picked = ring.tile([P, width], F32, name=f"picked{i}")
+            nc.vector.tensor_copy(picked[:], window[:].indirect(list3[:, cols]))
+            nc.vector.tensor_tensor(dest[:, i, :], window[:].indirect(list2[:, cols]), picked[:], ALU.subtract)
+
+        def interleave(src, width, name):
+            grouped = ring.tile([P, width * PACK], BF16, name=name, align_bytes=64)
+            nc.scalar.copy(
+                grouped[:].rearrange("p (c i t) -> p c t i", i=4, t=PACK),
+                src[:].rearrange("p t (c i) -> p c t i", i=4),
+            )
+            return grouped
+
+        def quantize_weight(raw, name):
+            grouped = ring.tile([P, H * PACK], BF16, name="w_grouped", align_bytes=64)
+            nc.scalar.copy(
+                grouped[:].rearrange("p (t m j) -> p m j t", t=PACK, j=PACK),
+                raw[:].rearrange("p j (m t) -> p m j t", t=PACK),
+            )
+            codes = keep.tile([P, H], U32, name=f"{name}_codes", align_bytes=64)
+            scales = keep.tile([P, H], U8, name=f"{name}_scales", align_bytes=64)
+            nc.vector.quantize_mx(codes[:].bitcast(E4M3), scales[:], grouped[:])
+            return codes, scales
+
+        def quantize(grouped, width, pool, name):
+            codes = pool.tile([P, width], U32, name=f"{name}_codes", align_bytes=64)
+            scales = pool.tile([P, width], U8, name=f"{name}_scales", align_bytes=64)
+            nc.vector.quantize_mx(codes[:].bitcast(E4M3), scales[:], grouped[:])
+            return codes, scales
+
+        x0 = [ring.tile([P, PACK, HALF], F32, name="x_planes") for h in range(2)]
+        for i in range(2):
+            for h in range(2):
+                difference(0, i, h * HALF, HALF, x0[h])
+
+        w1_p = keep.tile([P, PASSES, H * 2], U8, name="w1_p", align_bytes=64)
+        w1_ps = keep.tile([P, PASSES, H], U8, name="w1_ps", align_bytes=64)
+        nc.vector.tensor_copy(
+            w1_p[:].bitcast(U16).rearrange("p a (t m) -> p a t m", t=PACK),
+            w1_w[:].bitcast(U16).rearrange("p a (m t) -> p a t m", t=PACK),
+        )
+        nc.vector.tensor_copy(
+            w1_ps[:].rearrange("p a (t m) -> p a t m", t=PACK),
+            w1_s[:].rearrange("p a (m t) -> p a t m", t=PACK),
+        )
+
+        v_w = [keep.tile([P, S], U32, name=f"v_w{a}", align_bytes=64) for a in range(PASSES)]
+        nc.vector.tensor_copy(v_w[0][:], tab_w[0][:].bitcast(U32).indirect(list1[:]))
+        for h in range(2):
+            difference(0, 2, h * HALF, HALF, x0[h])
+        nc.vector.tensor_copy(v_w[1][:], tab_w[1][:].bitcast(U32).indirect(list1[:]))
+
+        a_raw = keep.tile([P, PACK, S], F32, name="a_raw")
+        a_scaled = keep.tile([P, PACK, S], F32, name="a_scaled")
+        for h in range(2):
+            cols = slice(h * HALF, (h + 1) * HALF)
+            for t in range(PACK):
+                acc = psum.tile([P, HALF], F32, name="acc_ay")
+                for a in range(PASSES):
+                    nc.tensor.matmul_mx(
+                        acc[:],
+                        lhsT=w1_p[:, a, 2 * P * t : 2 * P * (t + 1)].bitcast(E2M1),
+                        lhsT_scale=w1_ps[:, a, P * t : P * (t + 1)],
+                        rhs=v_w[a][:, cols].bitcast(E4M3),
+                        rhs_scale=v_s[a][:, cols],
+                        start=(a == 0),
+                        stop=(a == PASSES - 1),
+                    )
+                nc.scalar.copy(a_raw[:, t, cols], acc[:])
+                nc.scalar.activation(a_scaled[:, t, cols], acc[:], ACT.Copy, scale=c_a[:, t : t + 1])
+
+        w2_q = [quantize_weight(w2_raw[0], "w2a")]
+        for h in range(2):
+            difference(0, 3, h * HALF, HALF, x0[h])
+        x0_grouped = [interleave(x0[h], HALF, "x_grouped") for h in range(2)]
+
+        chunks = S // CHUNK
+        x1 = [ring.tile([P, PACK, CHUNK], F32, name="x_planes") for c in range(2)]
+        for c in range(2):
+            difference(1, 0, c * CHUNK, CHUNK, x1[c])
+        x0_q = [quantize(x0_grouped[h], HALF, keep, f"x0_{h}") for h in range(2)]
+        w2_q.append(quantize_weight(w2_raw[1], "w2b"))
+        for i in range(1, PACK):
+            for c in range(2):
+                difference(1, i, c * CHUNK, CHUNK, x1[c])
+        w3_q = quantize_weight(w3_raw, "w3")
+
+        out_rows = out.rearrange("(p t) j -> p t j", t=PACK)
+
+        def product_b(c):
+            x1_q = quantize(interleave(x1[c], CHUNK, "x_grouped"), CHUNK, ring, "x1")
+            h, off = divmod(c * CHUNK, HALF)
+            operands = [
+                (x0_q[h][0][:, off : off + CHUNK], x0_q[h][1][:, off : off + CHUNK]),
+                (x1_q[0][:], x1_q[1][:]),
+            ]
+            banks = []
+            for pair in range(2):
+                acc = psum.tile([P, 2, CHUNK], F32, name="acc_b")
+                for u in range(2):
+                    t = 2 * pair + u
+                    for a in range(PASSES):
+                        nc.tensor.matmul_mx(
+                            acc[:, u, :],
+                            lhsT=w2_q[a][0][:, P * t : P * (t + 1)].bitcast(E4M3),
+                            lhsT_scale=w2_q[a][1][:, P * t : P * (t + 1)],
+                            rhs=operands[a][0].bitcast(E4M3),
+                            rhs_scale=operands[a][1],
+                            start=(a == 0),
+                            stop=(a == PASSES - 1),
+                        )
+                banks.append(acc)
+            return banks
+
+        def blend(c, banks):
+            cols = slice(c * CHUNK, (c + 1) * CHUNK)
+            z = ring.tile([P, PACK, CHUNK], BF16, name="z_planes")
+            for t in range(PACK):
+                nc.vector.scalar_tensor_tensor(
+                    z[:, t, :], banks[t // 2][:, t % 2, :], c_b[:, t : t + 1], a_scaled[:, t, cols], ALU.mult, ALU.add
+                )
+            return interleave(z, CHUNK, "z_grouped")
+
+        def finish(c, z_grouped):
+            cols = slice(c * CHUNK, (c + 1) * CHUNK)
+            z_q = quantize(z_grouped, CHUNK, ring, "z")
+            for pair in range(2):
+                acc = psum.tile([P, 2, CHUNK], F32, name="acc_ay")
+                for u in range(2):
+                    t = 2 * pair + u
+                    nc.tensor.matmul_mx(
+                        acc[:, u, :],
+                        lhsT=w3_q[0][:, P * t : P * (t + 1)].bitcast(E4M3),
+                        lhsT_scale=w3_q[1][:, P * t : P * (t + 1)],
+                        rhs=z_q[0][:].bitcast(E4M3),
+                        rhs_scale=z_q[1][:],
+                        start=True,
+                        stop=True,
+                    )
+                result = stores.tile([P, 2, CHUNK], F32, name="result")
+                nc.vector.tensor_tensor(result[:], acc[:], a_raw[:, 2 * pair : 2 * pair + 2, cols], ALU.min)
+                nc.sync.dma_start(out_rows[:, 2 * pair : 2 * pair + 2, cols], result[:])
+
+        for c in range(chunks):
+            if c >= 2:
+                x1.append(ring.tile([P, PACK, CHUNK], F32, name="x_planes"))
+                for i in range(PACK):
+                    difference(1, i, c * CHUNK, CHUNK, x1[c])
+            finish(c, blend(c, product_b(c)))

@@ -1,6 +1,7 @@
 from contextlib import ExitStack
 
 import concourse.mybir as mybir
+from concourse.masks import make_identity
 
 K, H, T, S = 1024, 512, 2048, 1024
 FLOPS = 2 * K * H * S * 2 + 2 * H * H * S
@@ -21,6 +22,7 @@ PACK = 4
 PASSES = K // (P * PACK)
 HALF = 512
 CHUNK = 256
+SLOTS = 6
 
 
 def tile_list_storm_index_cap_kernel(
@@ -32,7 +34,9 @@ def tile_list_storm_index_cap_kernel(
         keep = ctx.enter_context(tc.tile_pool(name="keep", bufs=1))
         ring = ctx.enter_context(tc.tile_pool(name="ring", bufs=2))
         stores = ctx.enter_context(tc.tile_pool(name="stores", bufs=4))
-        psum = ctx.enter_context(tc.psum_pool(name="psum", bufs=4))
+        psum_turn = ctx.enter_context(tc.psum_pool(name="psum_turn", bufs=2))
+        psum_b = ctx.enter_context(tc.psum_pool(name="psum_b", bufs=4))
+        psum_ay = ctx.enter_context(tc.psum_pool(name="psum_ay", bufs=2))
 
         list1 = lists.tile([P, S // 16], U16, name="list1")
         list2 = lists.tile([P, S // 16], U16, name="list2")
@@ -41,7 +45,7 @@ def tile_list_storm_index_cap_kernel(
         tab_s = keep.tile([P, T], U8, name="tab_s")
         w1_s = keep.tile([P, PASSES, H], U8, name="w1_s")
         v_s1 = keep.tile([P, S], U8, name="v_s1", align_bytes=64)
-        nc.vector.memset(tab_s[:].bitcast(I32), 0)
+        nc.gpsimd.memset(tab_s[:].bitcast(I32), 0)
         nc.vector.memset(w1_s[:].rearrange("p a c -> p (a c)").bitcast(I32), 0)
         nc.vector.memset(v_s1[:].bitcast(I32), 0)
 
@@ -50,10 +54,11 @@ def tile_list_storm_index_cap_kernel(
         w1_w = keep.tile([P, PASSES, H // 2], I32, name="w1_w")
         lam_t = keep.tile([P, PACK], F32, name="lam_t")
         gain_t = keep.tile([P, PACK], F32, name="gain_t")
-        x_rows = xT.rearrange("(a p i) t -> a i p t", a=PASSES, i=PACK)
+        ident = keep.tile([P, P], F32, name="ident")
+        make_identity(nc, ident[:])
 
         def load_plane(n):
-            nc.sync.dma_start(planes[n][:], x_rows[n // PACK, n % PACK])
+            nc.sync.dma_start(planes[n][:], xT[P * n : P * (n + 1), :])
 
         def load_tab(a):
             nc.sync.dma_start(tab_w[a][:], tab_words[a].rearrange("p t i -> p (t i)").bitcast(I32))
@@ -66,11 +71,11 @@ def tile_list_storm_index_cap_kernel(
         nc.sync.dma_start(list1[:], offs)
         nc.sync.dma_start(list3[:], offs3)
         nc.sync.dma_start(list2[:], offs2)
-        load_plane(0)
         for q in range(4):
-            nc.scalar.dma_start(
+            nc.sync.dma_start(
                 tab_s[32 * q : 32 * q + 8, :].bitcast(I32), tab_scales[:, 4 * q : 4 * q + 4, :].bitcast(I32)
             )
+        load_plane(0)
         load_plane(1)
         nc.sync.dma_start(w1_w[:], w1_words.rearrange("a p b -> p a b").bitcast(I32))
         for q in range(4):
@@ -81,16 +86,10 @@ def tile_list_storm_index_cap_kernel(
         nc.scalar.dma_start(lam_t[:], lam.rearrange("(p t) -> p t", t=PACK))
         nc.scalar.dma_start(gain_t[:], gain.rearrange("(p t) -> p t", t=PACK))
         load_tab(0)
-        load_plane(2)
         load_tab(1)
-        w2_raw = [load_weight(w2[0:512, :])]
-        load_plane(3)
-        load_plane(4)
-        w2_raw.append(load_weight(w2[512:1024, :]))
-        load_plane(5)
-        load_plane(6)
-        load_plane(7)
-        w3_raw = load_weight(w3)
+        for n in (2, 4, 5, 6, 3, 7):
+            load_plane(n)
+        w2_raw = [load_weight(w2[0:512, :]), load_weight(w2[512:1024, :])]
 
         v_s0 = keep.tile([P, S], U8, name="v_s0", align_bytes=64)
         nc.vector.tensor_copy(v_s0[:], tab_s[:].indirect(list1[:]))
@@ -107,12 +106,54 @@ def tile_list_storm_index_cap_kernel(
         nc.gpsimd.tensor_scalar(rest[:], lam_t[:], -1.0, 1.0, ALU.mult, ALU.add)
         nc.gpsimd.tensor_tensor(c_b[:], gain_t[:], rest[:], ALU.mult)
 
-        def difference(a, i, j0, width, dest):
-            window = planes[PACK * a + i]
-            cols = slice(j0 // 16, (j0 + width) // 16)
-            picked = ring.tile([P, width], F32, name=f"picked{i}")
-            nc.vector.tensor_copy(picked[:], window[:].indirect(list3[:, cols]))
-            nc.vector.tensor_tensor(dest[:, i, :], window[:].indirect(list2[:, cols]), picked[:], ALU.subtract)
+        slots = []
+
+        def slot(dtype, width):
+            tile = keep.tile([P, width], dtype, name=f"picked{len(slots) % SLOTS}", align_bytes=64)
+            slots.append(tile)
+            return tile
+
+        def pick_minus(n, h):
+            minus = slot(F32, HALF)
+            cols = slice(h * HALF // 16, (h + 1) * HALF // 16)
+            nc.vector.tensor_scalar(minus[:], planes[n][:].indirect(list3[:, cols]), -1.0, 0.0, ALU.mult, ALU.add)
+            return minus
+
+        def difference(n, j0, width, minus, turned, plus=None):
+            if plus is None:
+                plus = slot(F32, width)[:]
+            nc.vector.tensor_copy(plus, planes[n][:].indirect(list2[:, j0 // 16 : (j0 + width) // 16]))
+            acc = psum_turn.tile([P, width // P, P], F32, name="turn")
+            off = j0 % HALF
+            for g in range(width // P):
+                nc.tensor.matmul(
+                    acc[:, g, :], minus[:, off + P * g : off + P * (g + 1)], ident[:], start=True, stop=False, is_transpose=True
+                )
+                nc.tensor.matmul(
+                    acc[:, g, :], plus[:, P * g : P * (g + 1)], ident[:], start=False, stop=True, is_transpose=True
+                )
+            nc.scalar.copy(
+                turned[:].rearrange("j (g u c p e) -> j c u g p e", u=2, c=PACK, p=32, e=2)[:, n % PACK],
+                acc[:].rearrange("j g (p u e) -> j u g p e", u=2, e=2),
+            )
+
+        def turn_back(turned, width):
+            grouped = ring.tile([P, width * PACK], BF16, name="x_grouped", align_bytes=64)
+            words = turned[:].bitcast(F32)
+            for pair in range(width // CHUNK):
+                acc = psum_turn.tile([P, 2, 2, P], F32, name="turn")
+                for g in range(2):
+                    for u in range(2):
+                        first = ((2 * pair + g) * 2 + u) * P
+                        nc.tensor.transpose(acc[:, g, u, :], words[:, first : first + P], ident[:])
+                nc.scalar.copy(
+                    grouped[:].bitcast(F32)[:, pair * 512 : (pair + 1) * 512].rearrange("p (g j u) -> p g j u", g=2, u=2),
+                    acc[:].rearrange("p g u j -> p g j u"),
+                )
+            return grouped
+
+        def turned_tile(width):
+            return ring.tile([P, width * PACK], BF16, name="x_turned", align_bytes=64)
 
         def interleave(src, width, name):
             grouped = ring.tile([P, width * PACK], BF16, name=name, align_bytes=64)
@@ -139,10 +180,14 @@ def tile_list_storm_index_cap_kernel(
             nc.vector.quantize_mx(codes[:].bitcast(E4M3), scales[:], grouped[:])
             return codes, scales
 
-        x0 = [ring.tile([P, PACK, HALF], F32, name="x_planes") for h in range(2)]
-        for i in range(2):
+        x0 = [turned_tile(HALF) for h in range(2)]
+
+        def whole_plane(n):
             for h in range(2):
-                difference(0, i, h * HALF, HALF, x0[h])
+                difference(n, h * HALF, HALF, pick_minus(n, h), x0[h])
+
+        whole_plane(0)
+        whole_plane(1)
 
         w1_p = keep.tile([P, PASSES, H * 2], U8, name="w1_p", align_bytes=64)
         w1_ps = keep.tile([P, PASSES, H], U8, name="w1_ps", align_bytes=64)
@@ -155,24 +200,26 @@ def tile_list_storm_index_cap_kernel(
             w1_s[:].rearrange("p a (m t) -> p a t m", t=PACK),
         )
 
-        v_w = [keep.tile([P, S], U32, name=f"v_w{a}", align_bytes=64) for a in range(PASSES)]
-        nc.vector.tensor_copy(v_w[0][:], tab_w[0][:].bitcast(U32).indirect(list1[:]))
-        for h in range(2):
-            difference(0, 2, h * HALF, HALF, x0[h])
-        nc.vector.tensor_copy(v_w[1][:], tab_w[1][:].bitcast(U32).indirect(list1[:]))
-
         a_raw = keep.tile([P, PACK, S], F32, name="a_raw")
         a_scaled = keep.tile([P, PACK, S], F32, name="a_scaled")
-        for h in range(2):
+
+        def product_a(h):
             cols = slice(h * HALF, (h + 1) * HALF)
+            v_w = []
+            for a in range(PASSES):
+                picked = slot(U32, HALF)
+                nc.vector.tensor_copy(
+                    picked[:], tab_w[a][:].bitcast(U32).indirect(list1[:, h * HALF // 16 : (h + 1) * HALF // 16])
+                )
+                v_w.append(picked)
             for t in range(PACK):
-                acc = psum.tile([P, HALF], F32, name="acc_ay")
+                acc = psum_ay.tile([P, HALF], F32, name="acc_ay")
                 for a in range(PASSES):
                     nc.tensor.matmul_mx(
                         acc[:],
                         lhsT=w1_p[:, a, 2 * P * t : 2 * P * (t + 1)].bitcast(E2M1),
                         lhsT_scale=w1_ps[:, a, P * t : P * (t + 1)],
-                        rhs=v_w[a][:, cols].bitcast(E4M3),
+                        rhs=v_w[a][:].bitcast(E4M3),
                         rhs_scale=v_s[a][:, cols],
                         start=(a == 0),
                         stop=(a == PASSES - 1),
@@ -180,34 +227,44 @@ def tile_list_storm_index_cap_kernel(
                 nc.scalar.copy(a_raw[:, t, cols], acc[:])
                 nc.scalar.activation(a_scaled[:, t, cols], acc[:], ACT.Copy, scale=c_a[:, t : t + 1])
 
-        w2_q = [quantize_weight(w2_raw[0], "w2a")]
-        for h in range(2):
-            difference(0, 3, h * HALF, HALF, x0[h])
-        x0_grouped = [interleave(x0[h], HALF, "x_grouped") for h in range(2)]
+        product_a(0)
+        whole_plane(2)
+        product_a(1)
+        whole_plane(3)
+        x0_grouped = [turn_back(x0[h], HALF) for h in range(2)]
 
-        chunks = S // CHUNK
-        x1 = [ring.tile([P, PACK, CHUNK], F32, name="x_planes") for c in range(2)]
-        for c in range(2):
-            difference(1, 0, c * CHUNK, CHUNK, x1[c])
+        x1_first = turned_tile(HALF)
+        difference(4, 0, HALF, pick_minus(4, 0), x1_first)
         x0_q = [quantize(x0_grouped[h], HALF, keep, f"x0_{h}") for h in range(2)]
-        w2_q.append(quantize_weight(w2_raw[1], "w2b"))
-        for i in range(1, PACK):
-            for c in range(2):
-                difference(1, i, c * CHUNK, CHUNK, x1[c])
+        for n in range(5, 8):
+            difference(n, 0, HALF, pick_minus(n, 0), x1_first)
+        w2_q = [quantize_weight(w2_raw[a], f"w2_{a}") for a in range(PASSES)]
+        w3_raw = load_weight(w3)
+        x1_q = [quantize(turn_back(x1_first, HALF), HALF, keep, "x1_first")]
         w3_q = quantize_weight(w3_raw, "w3")
+        minus_last = [pick_minus(n, 1) for n in range(4, 8)]
+        free_slots = [(len(slots) + k) % SLOTS for k in range(2)]
 
         out_rows = out.rearrange("(p t) j -> p t j", t=PACK)
 
-        def product_b(c):
-            x1_q = quantize(interleave(x1[c], CHUNK, "x_grouped"), CHUNK, ring, "x1")
+        def last_differences(c):
+            turned = turned_tile(CHUNK)
+            for k in range(2):
+                plus = keep.tile([P, 2, CHUNK], F32, name=f"picked{free_slots[k]}", align_bytes=64)
+                for u in range(2):
+                    n = 4 + 2 * k + u
+                    difference(n, c * CHUNK, CHUNK, minus_last[n - 4], turned, plus[:, u, :])
+            return turned
+
+        def product_b(c, x1_codes, x1_scales):
             h, off = divmod(c * CHUNK, HALF)
             operands = [
                 (x0_q[h][0][:, off : off + CHUNK], x0_q[h][1][:, off : off + CHUNK]),
-                (x1_q[0][:], x1_q[1][:]),
+                (x1_codes, x1_scales),
             ]
             banks = []
             for pair in range(2):
-                acc = psum.tile([P, 2, CHUNK], F32, name="acc_b")
+                acc = psum_b.tile([P, 2, CHUNK], F32, name="acc_b")
                 for u in range(2):
                     t = 2 * pair + u
                     for a in range(PASSES):
@@ -236,7 +293,7 @@ def tile_list_storm_index_cap_kernel(
             cols = slice(c * CHUNK, (c + 1) * CHUNK)
             z_q = quantize(z_grouped, CHUNK, ring, "z")
             for pair in range(2):
-                acc = psum.tile([P, 2, CHUNK], F32, name="acc_ay")
+                acc = psum_ay.tile([P, 2, CHUNK], F32, name="acc_ay")
                 for u in range(2):
                     t = 2 * pair + u
                     nc.tensor.matmul_mx(
@@ -252,9 +309,16 @@ def tile_list_storm_index_cap_kernel(
                 nc.vector.tensor_tensor(result[:], acc[:], a_raw[:, 2 * pair : 2 * pair + 2, cols], ALU.min)
                 nc.sync.dma_start(out_rows[:, 2 * pair : 2 * pair + 2, cols], result[:])
 
-        for c in range(chunks):
-            if c >= 2:
-                x1.append(ring.tile([P, PACK, CHUNK], F32, name="x_planes"))
-                for i in range(PACK):
-                    difference(1, i, c * CHUNK, CHUNK, x1[c])
-            finish(c, blend(c, product_b(c)))
+        banks = [
+            product_b(c, x1_q[0][0][:, c * CHUNK : (c + 1) * CHUNK], x1_q[0][1][:, c * CHUNK : (c + 1) * CHUNK])
+            for c in range(2)
+        ]
+        turned = [last_differences(c) for c in (2, 3)]
+        z_grouped = [blend(0, banks[0])]
+        for c in (2, 3):
+            codes, scales = quantize(turn_back(turned[c - 2], CHUNK), CHUNK, ring, "x1")
+            banks.append(product_b(c, codes[:], scales[:]))
+        for c in range(1, 4):
+            z_grouped.append(blend(c, banks[c]))
+            finish(c - 1, z_grouped[c - 1])
+        finish(3, z_grouped[3])

@@ -1,7 +1,6 @@
 from contextlib import ExitStack
 
 import concourse.mybir as mybir
-from concourse.masks import make_identity
 
 K, H, T, S = 1024, 512, 2048, 1024
 FLOPS = 2 * K * H * S * 2 + 2 * H * H * S
@@ -22,7 +21,7 @@ PACK = 4
 PASSES = K // (P * PACK)
 HALF = 512
 CHUNK = 256
-SLOTS = 6
+SLOTS = 3
 
 
 def tile_list_storm_index_cap_kernel(
@@ -33,10 +32,7 @@ def tile_list_storm_index_cap_kernel(
         lists = ctx.enter_context(tc.tile_pool(name="lists", bufs=1))
         keep = ctx.enter_context(tc.tile_pool(name="keep", bufs=1))
         ring = ctx.enter_context(tc.tile_pool(name="ring", bufs=2))
-        stores = ctx.enter_context(tc.tile_pool(name="stores", bufs=4))
-        psum_turn = ctx.enter_context(tc.psum_pool(name="psum_turn", bufs=2))
-        psum_b = ctx.enter_context(tc.psum_pool(name="psum_b", bufs=4))
-        psum_ay = ctx.enter_context(tc.psum_pool(name="psum_ay", bufs=2))
+        psum_acc = ctx.enter_context(tc.psum_pool(name="psum_acc", bufs=8))
 
         list1 = lists.tile([P, S // 16], U16, name="list1")
         list2 = lists.tile([P, S // 16], U16, name="list2")
@@ -46,7 +42,7 @@ def tile_list_storm_index_cap_kernel(
         w1_s = keep.tile([P, PASSES, H], U8, name="w1_s")
         v_s1 = keep.tile([P, S], U8, name="v_s1", align_bytes=64)
         nc.gpsimd.memset(tab_s[:].bitcast(I32), 0)
-        nc.vector.memset(w1_s[:].rearrange("p a c -> p (a c)").bitcast(I32), 0)
+        nc.gpsimd.memset(w1_s[:].rearrange("p a c -> p (a c)").bitcast(I32), 0)
         nc.vector.memset(v_s1[:].bitcast(I32), 0)
 
         planes = [keep.tile([P, T], F32, name=f"plane{n}") for n in range(PASSES * PACK)]
@@ -54,50 +50,50 @@ def tile_list_storm_index_cap_kernel(
         w1_w = keep.tile([P, PASSES, H // 2], I32, name="w1_w")
         lam_t = keep.tile([P, PACK], F32, name="lam_t")
         gain_t = keep.tile([P, PACK], F32, name="gain_t")
-        ident = keep.tile([P, P], F32, name="ident")
-        make_identity(nc, ident[:])
+        x_rows = xT.rearrange("(a p i) t -> a i p t", a=PASSES, i=PACK)
 
         def load_plane(n):
-            nc.sync.dma_start(planes[n][:], xT[P * n : P * (n + 1), :])
+            nc.sync.dma_start(planes[n][:], x_rows[n // PACK, n % PACK])
 
         def load_tab(a):
             nc.sync.dma_start(tab_w[a][:], tab_words[a].rearrange("p t i -> p (t i)").bitcast(I32))
 
-        def load_weight(rows):
-            raw = ring.tile([P, PACK, H], F32, name="w_raw")
+        def load_weight(rows, name):
+            raw = keep.tile([P, PACK, H], F32, name=name)
             nc.sync.dma_start(raw[:], rows.rearrange("(p j) c -> p j c", j=PACK))
             return raw
 
         nc.sync.dma_start(list1[:], offs)
-        nc.sync.dma_start(list3[:], offs3)
-        nc.sync.dma_start(list2[:], offs2)
         for q in range(4):
             nc.sync.dma_start(
                 tab_s[32 * q : 32 * q + 8, :].bitcast(I32), tab_scales[:, 4 * q : 4 * q + 4, :].bitcast(I32)
             )
         load_plane(0)
-        load_plane(1)
-        nc.sync.dma_start(w1_w[:], w1_words.rearrange("a p b -> p a b").bitcast(I32))
-        for q in range(4):
-            nc.scalar.dma_start(
-                w1_s[32 * q : 32 * q + 4, :, :].bitcast(I32),
-                w1_scales[:, 4 * q : 4 * q + 4, :].rearrange("a r c -> r a c").bitcast(I32),
-            )
-        nc.scalar.dma_start(lam_t[:], lam.rearrange("(p t) -> p t", t=PACK))
-        nc.scalar.dma_start(gain_t[:], gain.rearrange("(p t) -> p t", t=PACK))
-        load_tab(0)
-        load_tab(1)
-        for n in (2, 4, 5, 6, 3, 7):
-            load_plane(n)
-        w2_raw = [load_weight(w2[0:512, :]), load_weight(w2[512:1024, :])]
+        nc.sync.dma_start(list3[:], offs3)
+        nc.sync.dma_start(list2[:], offs2)
 
         v_s0 = keep.tile([P, S], U8, name="v_s0", align_bytes=64)
         nc.vector.tensor_copy(v_s0[:], tab_s[:].indirect(list1[:]))
         for q in range(4):
-            nc.scalar.dma_start(
+            nc.sync.dma_start(
                 v_s1[32 * q : 32 * q + 4, :].bitcast(I32), v_s0[32 * q + 4 : 32 * q + 8, :].bitcast(I32)
             )
         v_s = [v_s0, v_s1]
+
+        load_plane(1)
+        nc.sync.dma_start(w1_w[:], w1_words.rearrange("a p b -> p a b").bitcast(I32))
+        for q in range(4):
+            nc.sync.dma_start(
+                w1_s[32 * q : 32 * q + 4, :, :].bitcast(I32),
+                w1_scales[:, 4 * q : 4 * q + 4, :].rearrange("a r c -> r a c").bitcast(I32),
+            )
+        nc.sync.dma_start(lam_t[:], lam.rearrange("(p t) -> p t", t=PACK))
+        nc.sync.dma_start(gain_t[:], gain.rearrange("(p t) -> p t", t=PACK))
+        load_tab(0)
+        load_tab(1)
+        for n in (2, 4, 5, 6, 7, 3):
+            load_plane(n)
+        w2_raw = [load_weight(w2[512 * a : 512 * (a + 1), :], f"w2_raw{a}") for a in range(PASSES)]
 
         c_a = keep.tile([P, PACK], F32, name="c_a")
         c_b = keep.tile([P, PACK], F32, name="c_b")
@@ -108,58 +104,23 @@ def tile_list_storm_index_cap_kernel(
 
         slots = []
 
-        def slot(dtype, width):
-            tile = keep.tile([P, width], dtype, name=f"picked{len(slots) % SLOTS}", align_bytes=64)
-            slots.append(tile)
-            return tile
-
-        def pick_minus(n, h):
-            minus = slot(F32, HALF)
+        def difference(n, h, dest, name=None):
+            if name is None:
+                name = f"picked{len(slots) % SLOTS}"
+                slots.append(name)
+            picked = keep.tile([P, HALF], F32, name=name, align_bytes=64)
             cols = slice(h * HALF // 16, (h + 1) * HALF // 16)
-            nc.vector.tensor_scalar(minus[:], planes[n][:].indirect(list3[:, cols]), -1.0, 0.0, ALU.mult, ALU.add)
-            return minus
+            nc.vector.tensor_copy(picked[:], planes[n][:].indirect(list3[:, cols]))
+            nc.vector.tensor_tensor(dest[:, n % PACK, :], planes[n][:].indirect(list2[:, cols]), picked[:], ALU.subtract)
 
-        def difference(n, j0, width, minus, turned, plus=None):
-            if plus is None:
-                plus = slot(F32, width)[:]
-            nc.vector.tensor_copy(plus, planes[n][:].indirect(list2[:, j0 // 16 : (j0 + width) // 16]))
-            acc = psum_turn.tile([P, width // P, P], F32, name="turn")
-            off = j0 % HALF
-            for g in range(width // P):
-                nc.tensor.matmul(
-                    acc[:, g, :], minus[:, off + P * g : off + P * (g + 1)], ident[:], start=True, stop=False, is_transpose=True
-                )
-                nc.tensor.matmul(
-                    acc[:, g, :], plus[:, P * g : P * (g + 1)], ident[:], start=False, stop=True, is_transpose=True
-                )
-            nc.scalar.copy(
-                turned[:].rearrange("j (g u c p e) -> j c u g p e", u=2, c=PACK, p=32, e=2)[:, n % PACK],
-                acc[:].rearrange("j g (p u e) -> j u g p e", u=2, e=2),
-            )
+        def x_tile():
+            return ring.tile([P, PACK, HALF], F32, name="x_planes")
 
-        def turn_back(turned, width):
-            grouped = ring.tile([P, width * PACK], BF16, name="x_grouped", align_bytes=64)
-            words = turned[:].bitcast(F32)
-            for pair in range(width // CHUNK):
-                acc = psum_turn.tile([P, 2, 2, P], F32, name="turn")
-                for g in range(2):
-                    for u in range(2):
-                        first = ((2 * pair + g) * 2 + u) * P
-                        nc.tensor.transpose(acc[:, g, u, :], words[:, first : first + P], ident[:])
-                nc.scalar.copy(
-                    grouped[:].bitcast(F32)[:, pair * 512 : (pair + 1) * 512].rearrange("p (g j u) -> p g j u", g=2, u=2),
-                    acc[:].rearrange("p g u j -> p g j u"),
-                )
-            return grouped
-
-        def turned_tile(width):
-            return ring.tile([P, width * PACK], BF16, name="x_turned", align_bytes=64)
-
-        def interleave(src, width, name):
-            grouped = ring.tile([P, width * PACK], BF16, name=name, align_bytes=64)
+        def interleave(src, width, pool, name):
+            grouped = pool.tile([P, width * PACK], BF16, name=name, align_bytes=64)
             nc.scalar.copy(
                 grouped[:].rearrange("p (c i t) -> p c t i", i=4, t=PACK),
-                src[:].rearrange("p t (c i) -> p c t i", i=4),
+                src.rearrange("p t (c i) -> p c t i", i=4),
             )
             return grouped
 
@@ -180,11 +141,11 @@ def tile_list_storm_index_cap_kernel(
             nc.vector.quantize_mx(codes[:].bitcast(E4M3), scales[:], grouped[:])
             return codes, scales
 
-        x0 = [turned_tile(HALF) for h in range(2)]
+        x0 = [x_tile() for h in range(2)]
 
         def whole_plane(n):
             for h in range(2):
-                difference(n, h * HALF, HALF, pick_minus(n, h), x0[h])
+                difference(n, h, x0[h])
 
         whole_plane(0)
         whole_plane(1)
@@ -203,23 +164,20 @@ def tile_list_storm_index_cap_kernel(
         a_raw = keep.tile([P, PACK, S], F32, name="a_raw")
         a_scaled = keep.tile([P, PACK, S], F32, name="a_scaled")
 
+        v_w = [keep.tile([P, S], U32, name=f"v_w{a}", align_bytes=64) for a in range(PASSES)]
+        for a in range(PASSES):
+            nc.vector.tensor_copy(v_w[a][:], tab_w[a][:].bitcast(U32).indirect(list1[:]))
+
         def product_a(h):
             cols = slice(h * HALF, (h + 1) * HALF)
-            v_w = []
-            for a in range(PASSES):
-                picked = slot(U32, HALF)
-                nc.vector.tensor_copy(
-                    picked[:], tab_w[a][:].bitcast(U32).indirect(list1[:, h * HALF // 16 : (h + 1) * HALF // 16])
-                )
-                v_w.append(picked)
             for t in range(PACK):
-                acc = psum_ay.tile([P, HALF], F32, name="acc_ay")
+                acc = psum_acc.tile([P, HALF], F32, name="acc")
                 for a in range(PASSES):
                     nc.tensor.matmul_mx(
                         acc[:],
                         lhsT=w1_p[:, a, 2 * P * t : 2 * P * (t + 1)].bitcast(E2M1),
                         lhsT_scale=w1_ps[:, a, P * t : P * (t + 1)],
-                        rhs=v_w[a][:].bitcast(E4M3),
+                        rhs=v_w[a][:, cols].bitcast(E4M3),
                         rhs_scale=v_s[a][:, cols],
                         start=(a == 0),
                         stop=(a == PASSES - 1),
@@ -228,33 +186,26 @@ def tile_list_storm_index_cap_kernel(
                 nc.scalar.activation(a_scaled[:, t, cols], acc[:], ACT.Copy, scale=c_a[:, t : t + 1])
 
         product_a(0)
-        whole_plane(2)
         product_a(1)
+        w3_raw = load_weight(w3, "tab_w0")
+        whole_plane(2)
         whole_plane(3)
-        x0_grouped = [turn_back(x0[h], HALF) for h in range(2)]
+        x0_q = [quantize(interleave(x0[h][:], HALF, ring, "x_grouped"), HALF, keep, f"x0_{h}") for h in range(2)]
 
-        x1_first = turned_tile(HALF)
-        difference(4, 0, HALF, pick_minus(4, 0), x1_first)
-        x0_q = [quantize(x0_grouped[h], HALF, keep, f"x0_{h}") for h in range(2)]
-        for n in range(5, 8):
-            difference(n, 0, HALF, pick_minus(n, 0), x1_first)
+        x1 = [x_tile()]
+        for n in range(4, 8):
+            difference(n, 0, x1[0])
         w2_q = [quantize_weight(w2_raw[a], f"w2_{a}") for a in range(PASSES)]
-        w3_raw = load_weight(w3)
-        x1_q = [quantize(turn_back(x1_first, HALF), HALF, keep, "x1_first")]
+
+        def quantize_x1(c, name):
+            off = c * CHUNK % HALF
+            grouped = interleave(x1[c * CHUNK // HALF][:, :, off : off + CHUNK], CHUNK, keep, name)
+            return quantize(grouped, CHUNK, keep, f"x1_{c}")
+
+        x1_q = [quantize_x1(c, f"x1_grouped{c}") for c in range(2)]
         w3_q = quantize_weight(w3_raw, "w3")
-        minus_last = [pick_minus(n, 1) for n in range(4, 8)]
-        free_slots = [(len(slots) + k) % SLOTS for k in range(2)]
 
         out_rows = out.rearrange("(p t) j -> p t j", t=PACK)
-
-        def last_differences(c):
-            turned = turned_tile(CHUNK)
-            for k in range(2):
-                plus = keep.tile([P, 2, CHUNK], F32, name=f"picked{free_slots[k]}", align_bytes=64)
-                for u in range(2):
-                    n = 4 + 2 * k + u
-                    difference(n, c * CHUNK, CHUNK, minus_last[n - 4], turned, plus[:, u, :])
-            return turned
 
         def product_b(c, x1_codes, x1_scales):
             h, off = divmod(c * CHUNK, HALF)
@@ -264,7 +215,7 @@ def tile_list_storm_index_cap_kernel(
             ]
             banks = []
             for pair in range(2):
-                acc = psum_b.tile([P, 2, CHUNK], F32, name="acc_b")
+                acc = psum_acc.tile([P, 2, CHUNK], F32, name="acc")
                 for u in range(2):
                     t = 2 * pair + u
                     for a in range(PASSES):
@@ -287,13 +238,12 @@ def tile_list_storm_index_cap_kernel(
                 nc.vector.scalar_tensor_tensor(
                     z[:, t, :], banks[t // 2][:, t % 2, :], c_b[:, t : t + 1], a_scaled[:, t, cols], ALU.mult, ALU.add
                 )
-            return interleave(z, CHUNK, "z_grouped")
+            return interleave(z[:], CHUNK, ring, "z_grouped")
 
-        def finish(c, z_grouped):
+        def finish(c, z_q):
             cols = slice(c * CHUNK, (c + 1) * CHUNK)
-            z_q = quantize(z_grouped, CHUNK, ring, "z")
             for pair in range(2):
-                acc = psum_ay.tile([P, 2, CHUNK], F32, name="acc_ay")
+                acc = psum_acc.tile([P, 2, CHUNK], F32, name="acc")
                 for u in range(2):
                     t = 2 * pair + u
                     nc.tensor.matmul_mx(
@@ -305,20 +255,17 @@ def tile_list_storm_index_cap_kernel(
                         start=True,
                         stop=True,
                     )
-                result = stores.tile([P, 2, CHUNK], F32, name="result")
-                nc.vector.tensor_tensor(result[:], acc[:], a_raw[:, 2 * pair : 2 * pair + 2, cols], ALU.min)
-                nc.sync.dma_start(out_rows[:, 2 * pair : 2 * pair + 2, cols], result[:])
+                result = a_scaled[:, 2 * pair : 2 * pair + 2, cols]
+                nc.vector.tensor_tensor(result, acc[:], a_raw[:, 2 * pair : 2 * pair + 2, cols], ALU.min)
+                nc.sync.dma_start(out_rows[:, 2 * pair : 2 * pair + 2, cols], result)
 
-        banks = [
-            product_b(c, x1_q[0][0][:, c * CHUNK : (c + 1) * CHUNK], x1_q[0][1][:, c * CHUNK : (c + 1) * CHUNK])
-            for c in range(2)
-        ]
-        turned = [last_differences(c) for c in (2, 3)]
-        z_grouped = [blend(0, banks[0])]
+        banks = [product_b(c, x1_q[c][0][:], x1_q[c][1][:]) for c in range(2)]
+        x1.append(x_tile())
+        for n in range(4, 8):
+            difference(n, 1, x1[1], "x1_grouped1" if n == 6 else None)
         for c in (2, 3):
-            codes, scales = quantize(turn_back(turned[c - 2], CHUNK), CHUNK, ring, "x1")
+            codes, scales = quantize_x1(c, f"x1_grouped{c}")
             banks.append(product_b(c, codes[:], scales[:]))
-        for c in range(1, 4):
-            z_grouped.append(blend(c, banks[c]))
-            finish(c - 1, z_grouped[c - 1])
-        finish(3, z_grouped[3])
+        z_q = [quantize(blend(c, banks[c]), CHUNK, keep, f"z{c}") for c in range(4)]
+        for c in range(4):
+            finish(c, z_q[c])

@@ -18,10 +18,14 @@ ACT = mybir.ActivationFunctionType
 
 P = 128
 PACK = 4
-PASSES = K // (P * PACK)
+K_PASS = P * PACK
+PASSES = K // K_PASS
+QUADRANTS = 4
+STRIPE = 16
 HALF = 512
 CHUNK = 256
-SLOTS = 3
+RUN = 4
+PICK_TILES = 3
 
 
 def tile_list_storm_index_cap_kernel(
@@ -32,84 +36,89 @@ def tile_list_storm_index_cap_kernel(
         lists = ctx.enter_context(tc.tile_pool(name="lists", bufs=1))
         keep = ctx.enter_context(tc.tile_pool(name="keep", bufs=1))
         ring = ctx.enter_context(tc.tile_pool(name="ring", bufs=2))
-        psum_acc = ctx.enter_context(tc.psum_pool(name="psum_acc", bufs=8))
+        psum = ctx.enter_context(tc.psum_pool(name="psum", bufs=8))
 
-        list1 = lists.tile([P, S // 16], U16, name="list1")
-        list2 = lists.tile([P, S // 16], U16, name="list2")
-        list3 = lists.tile([P, S // 16], U16, name="list3")
+        list1 = lists.tile([P, S // STRIPE], U16, name="list1")
+        list2 = lists.tile([P, S // STRIPE], U16, name="list2")
+        list3 = lists.tile([P, S // STRIPE], U16, name="list3")
 
         tab_s = keep.tile([P, T], U8, name="tab_s")
         w1_s = keep.tile([P, PASSES, H], U8, name="w1_s")
-        v_s1 = keep.tile([P, S], U8, name="v_s1", align_bytes=64)
-        nc.gpsimd.memset(tab_s[:].bitcast(I32), 0)
-        nc.gpsimd.memset(w1_s[:].rearrange("p a c -> p (a c)").bitcast(I32), 0)
-        nc.vector.memset(v_s1[:].bitcast(I32), 0)
+        v_s = keep.tile([P, PASSES, S], U8, name="v_s", align_bytes=64)
+        nc.gpsimd.memset(tab_s[32:64, :].bitcast(I32), 0)
+        nc.gpsimd.memset(tab_s[64:128, :].bitcast(I32), 0)
+        nc.gpsimd.memset(w1_s[:].rearrange("p s c -> p (s c)").bitcast(I32), 0)
+        nc.vector.memset(v_s[:].rearrange("p s j -> p (s j)").bitcast(I32), 0)
 
         planes = [keep.tile([P, T], F32, name=f"plane{n}") for n in range(PASSES * PACK)]
-        tab_w = [keep.tile([P, T], I32, name=f"tab_w{a}") for a in range(PASSES)]
+        tab_w = [keep.tile([P, T], I32, name=f"tab_w{s}") for s in range(PASSES)]
         w1_w = keep.tile([P, PASSES, H // 2], I32, name="w1_w")
         lam_t = keep.tile([P, PACK], F32, name="lam_t")
         gain_t = keep.tile([P, PACK], F32, name="gain_t")
-        x_rows = xT.rearrange("(a p i) t -> a i p t", a=PASSES, i=PACK)
+        x_rows = xT.rearrange("(s p i) t -> s i p t", s=PASSES, i=PACK)
 
         def load_plane(n):
             nc.sync.dma_start(planes[n][:], x_rows[n // PACK, n % PACK])
 
-        def load_tab(a):
-            nc.sync.dma_start(tab_w[a][:], tab_words[a].rearrange("p t i -> p (t i)").bitcast(I32))
+        def load_tab(s):
+            nc.sync.dma_start(tab_w[s][:], tab_words[s].rearrange("p t i -> p (t i)").bitcast(I32))
 
         def load_weight(rows, name):
             raw = keep.tile([P, PACK, H], F32, name=name)
-            nc.sync.dma_start(raw[:], rows.rearrange("(p j) c -> p j c", j=PACK))
+            nc.sync.dma_start(raw[:], rows.rearrange("(p i) c -> p i c", i=PACK))
             return raw
 
-        nc.sync.dma_start(list1[:], offs)
-        for q in range(4):
+        def load_w1_scales(q):
             nc.sync.dma_start(
-                tab_s[32 * q : 32 * q + 8, :].bitcast(I32), tab_scales[:, 4 * q : 4 * q + 4, :].bitcast(I32)
+                w1_s[32 * q : 32 * q + 4, :, :].bitcast(I32),
+                w1_scales[:, 4 * q : 4 * q + 4, :].rearrange("s r c -> r s c").bitcast(I32),
             )
+
+        nc.sync.dma_start(list1[:], offs)
+        nc.sync.dma_start(tab_s[0:32, :].bitcast(I32), tab_scales.rearrange("s g t -> (s g) t").bitcast(I32))
         load_plane(0)
         nc.sync.dma_start(list3[:], offs3)
         nc.sync.dma_start(list2[:], offs2)
 
-        v_s0 = keep.tile([P, S], U8, name="v_s0", align_bytes=64)
-        nc.vector.tensor_copy(v_s0[:], tab_s[:].indirect(list1[:]))
-        for q in range(4):
-            nc.sync.dma_start(
-                v_s1[32 * q : 32 * q + 4, :].bitcast(I32), v_s0[32 * q + 4 : 32 * q + 8, :].bitcast(I32)
-            )
-        v_s = [v_s0, v_s1]
+        v_rows = keep.tile([P, S], U8, name="v_rows")
+        nc.vector.tensor_copy(v_rows[:], tab_s[:].indirect(list1[:]))
+
+        def place_v_scales(s, q):
+            first = 4 * (QUADRANTS * s + q)
+            nc.sync.dma_start(v_s[32 * q : 32 * q + 4, s, :].bitcast(I32), v_rows[first : first + 4, :].bitcast(I32))
 
         load_plane(1)
-        nc.sync.dma_start(w1_w[:], w1_words.rearrange("a p b -> p a b").bitcast(I32))
-        for q in range(4):
-            nc.sync.dma_start(
-                w1_s[32 * q : 32 * q + 4, :, :].bitcast(I32),
-                w1_scales[:, 4 * q : 4 * q + 4, :].rearrange("a r c -> r a c").bitcast(I32),
-            )
         nc.sync.dma_start(lam_t[:], lam.rearrange("(p t) -> p t", t=PACK))
         nc.sync.dma_start(gain_t[:], gain.rearrange("(p t) -> p t", t=PACK))
-        load_tab(0)
-        load_tab(1)
-        for n in (2, 4, 5, 6, 7, 3):
+        nc.sync.dma_start(w1_w[:], w1_words.rearrange("s p b -> p s b").bitcast(I32))
+        for s in range(PASSES):
+            load_w1_scales(2 * s)
+            load_tab(s)
+            load_w1_scales(2 * s + 1)
+        for s in range(PASSES):
+            load_plane(2 + 2 * s)
+            for q in range(QUADRANTS):
+                place_v_scales(s, q)
+        for n in (5, 3, 6, 7):
             load_plane(n)
-        w2_raw = [load_weight(w2[512 * a : 512 * (a + 1), :], f"w2_raw{a}") for a in range(PASSES)]
+        w2_raw = [load_weight(w2[K_PASS * s : K_PASS * (s + 1), :], f"w2_raw{s}") for s in range(PASSES)]
 
-        c_a = keep.tile([P, PACK], F32, name="c_a")
-        c_b = keep.tile([P, PACK], F32, name="c_b")
+        factor_a = keep.tile([P, PACK], F32, name="factor_a")
+        factor_b = keep.tile([P, PACK], F32, name="factor_b")
         rest = keep.tile([P, PACK], F32, name="rest")
-        nc.gpsimd.tensor_tensor(c_a[:], gain_t[:], lam_t[:], ALU.mult)
+        nc.gpsimd.tensor_tensor(factor_a[:], gain_t[:], lam_t[:], ALU.mult)
         nc.gpsimd.tensor_scalar(rest[:], lam_t[:], -1.0, 1.0, ALU.mult, ALU.add)
-        nc.gpsimd.tensor_tensor(c_b[:], gain_t[:], rest[:], ALU.mult)
+        nc.gpsimd.tensor_tensor(factor_b[:], gain_t[:], rest[:], ALU.mult)
 
-        slots = []
+        picks = []
 
-        def difference(n, h, dest, name=None):
-            if name is None:
-                name = f"picked{len(slots) % SLOTS}"
-                slots.append(name)
-            picked = keep.tile([P, HALF], F32, name=name, align_bytes=64)
-            cols = slice(h * HALF // 16, (h + 1) * HALF // 16)
+        def next_pick_tile():
+            picks.append(f"picked{len(picks) % PICK_TILES}")
+            return picks[-1]
+
+        def difference(n, h, dest, pick_tile):
+            picked = keep.tile([P, HALF], F32, name=pick_tile, align_bytes=64)
+            cols = slice(h * HALF // STRIPE, (h + 1) * HALF // STRIPE)
             nc.vector.tensor_copy(picked[:], planes[n][:].indirect(list3[:, cols]))
             nc.vector.tensor_tensor(dest[:, n % PACK, :], planes[n][:].indirect(list2[:, cols]), picked[:], ALU.subtract)
 
@@ -119,139 +128,135 @@ def tile_list_storm_index_cap_kernel(
         def interleave(src, width, pool, name):
             grouped = pool.tile([P, width * PACK], BF16, name=name, align_bytes=64)
             nc.scalar.copy(
-                grouped[:].rearrange("p (c i t) -> p c t i", i=4, t=PACK),
-                src.rearrange("p t (c i) -> p c t i", i=4),
+                grouped[:].rearrange("p (c e i) -> p c i e", e=RUN, i=PACK),
+                src.rearrange("p i (c e) -> p c i e", e=RUN),
             )
             return grouped
+
+        def quantize(grouped, width, name):
+            codes = keep.tile([P, width], U32, name=f"{name}_codes", align_bytes=64)
+            scales = keep.tile([P, width], U8, name=f"{name}_scales", align_bytes=64)
+            nc.vector.quantize_mx(codes[:].bitcast(E4M3), scales[:], grouped[:])
+            return codes, scales
 
         def quantize_weight(raw, name):
             grouped = ring.tile([P, H * PACK], BF16, name="w_grouped", align_bytes=64)
             nc.scalar.copy(
-                grouped[:].rearrange("p (t m j) -> p m j t", t=PACK, j=PACK),
-                raw[:].rearrange("p j (m t) -> p m j t", t=PACK),
+                grouped[:].rearrange("p (t m i) -> p m i t", t=PACK, i=PACK),
+                raw[:].rearrange("p i (m t) -> p m i t", t=PACK),
             )
-            codes = keep.tile([P, H], U32, name=f"{name}_codes", align_bytes=64)
-            scales = keep.tile([P, H], U8, name=f"{name}_scales", align_bytes=64)
-            nc.vector.quantize_mx(codes[:].bitcast(E4M3), scales[:], grouped[:])
-            return codes, scales
-
-        def quantize(grouped, width, pool, name):
-            codes = pool.tile([P, width], U32, name=f"{name}_codes", align_bytes=64)
-            scales = pool.tile([P, width], U8, name=f"{name}_scales", align_bytes=64)
-            nc.vector.quantize_mx(codes[:].bitcast(E4M3), scales[:], grouped[:])
-            return codes, scales
+            return quantize(grouped, H, name)
 
         x0 = [x_tile() for h in range(2)]
 
-        def whole_plane(n):
+        def both_halves(n):
             for h in range(2):
-                difference(n, h, x0[h])
+                difference(n, h, x0[h], next_pick_tile())
 
-        whole_plane(0)
-        whole_plane(1)
+        both_halves(0)
+        both_halves(1)
 
-        w1_p = keep.tile([P, PASSES, H * 2], U8, name="w1_p", align_bytes=64)
-        w1_ps = keep.tile([P, PASSES, H], U8, name="w1_ps", align_bytes=64)
+        w1_codes = keep.tile([P, PASSES, H * 2], U8, name="w1_codes", align_bytes=64)
+        w1_planes = keep.tile([P, PASSES, H], U8, name="w1_planes", align_bytes=64)
         nc.vector.tensor_copy(
-            w1_p[:].bitcast(U16).rearrange("p a (t m) -> p a t m", t=PACK),
-            w1_w[:].bitcast(U16).rearrange("p a (m t) -> p a t m", t=PACK),
+            w1_codes[:].bitcast(U16).rearrange("p s (t m) -> p s t m", t=PACK),
+            w1_w[:].bitcast(U16).rearrange("p s (m t) -> p s t m", t=PACK),
         )
         nc.vector.tensor_copy(
-            w1_ps[:].rearrange("p a (t m) -> p a t m", t=PACK),
-            w1_s[:].rearrange("p a (m t) -> p a t m", t=PACK),
+            w1_planes[:].rearrange("p s (t m) -> p s t m", t=PACK),
+            w1_s[:].rearrange("p s (m t) -> p s t m", t=PACK),
         )
 
         a_raw = keep.tile([P, PACK, S], F32, name="a_raw")
         a_scaled = keep.tile([P, PACK, S], F32, name="a_scaled")
 
-        v_w = [keep.tile([P, S], U32, name=f"v_w{a}", align_bytes=64) for a in range(PASSES)]
-        for a in range(PASSES):
-            nc.vector.tensor_copy(v_w[a][:], tab_w[a][:].bitcast(U32).indirect(list1[:]))
+        v_w = [keep.tile([P, S], U32, name=f"v_w{s}", align_bytes=64) for s in range(PASSES)]
+        for s in range(PASSES):
+            nc.vector.tensor_copy(v_w[s][:], tab_w[s][:].bitcast(U32).indirect(list1[:]))
 
-        def product_a(h):
+        for h in range(2):
             cols = slice(h * HALF, (h + 1) * HALF)
             for t in range(PACK):
-                acc = psum_acc.tile([P, HALF], F32, name="acc")
-                for a in range(PASSES):
+                acc = psum.tile([P, HALF], F32, name="acc")
+                for s in range(PASSES):
                     nc.tensor.matmul_mx(
                         acc[:],
-                        lhsT=w1_p[:, a, 2 * P * t : 2 * P * (t + 1)].bitcast(E2M1),
-                        lhsT_scale=w1_ps[:, a, P * t : P * (t + 1)],
-                        rhs=v_w[a][:, cols].bitcast(E4M3),
-                        rhs_scale=v_s[a][:, cols],
-                        start=(a == 0),
-                        stop=(a == PASSES - 1),
+                        lhsT=w1_codes[:, s, 2 * P * t : 2 * P * (t + 1)].bitcast(E2M1),
+                        lhsT_scale=w1_planes[:, s, P * t : P * (t + 1)],
+                        rhs=v_w[s][:, cols].bitcast(E4M3),
+                        rhs_scale=v_s[:, s, cols],
+                        start=(s == 0),
+                        stop=(s == PASSES - 1),
                     )
                 nc.scalar.copy(a_raw[:, t, cols], acc[:])
-                nc.scalar.activation(a_scaled[:, t, cols], acc[:], ACT.Copy, scale=c_a[:, t : t + 1])
+                nc.scalar.activation(a_scaled[:, t, cols], acc[:], ACT.Copy, scale=factor_a[:, t : t + 1])
 
-        product_a(0)
-        product_a(1)
         w3_raw = load_weight(w3, "tab_w0")
-        whole_plane(2)
-        whole_plane(3)
-        x0_q = [quantize(interleave(x0[h][:], HALF, ring, "x_grouped"), HALF, keep, f"x0_{h}") for h in range(2)]
+        both_halves(2)
+        both_halves(3)
+        x0_q = [quantize(interleave(x0[h][:], HALF, ring, "x_grouped"), HALF, f"x0_{h}") for h in range(2)]
 
+        pass1_planes = range(PACK, 2 * PACK)
         x1 = [x_tile()]
-        for n in range(4, 8):
-            difference(n, 0, x1[0])
-        w2_q = [quantize_weight(w2_raw[a], f"w2_{a}") for a in range(PASSES)]
+        for n in pass1_planes:
+            difference(n, 0, x1[0], next_pick_tile())
+        w2_q = [quantize_weight(w2_raw[s], f"w2_{s}") for s in range(PASSES)]
 
-        def quantize_x1(c, name):
-            off = c * CHUNK % HALF
-            grouped = interleave(x1[c * CHUNK // HALF][:, :, off : off + CHUNK], CHUNK, keep, name)
-            return quantize(grouped, CHUNK, keep, f"x1_{c}")
+        def quantize_x1(c):
+            h, off = divmod(c * CHUNK, HALF)
+            grouped = interleave(x1[h][:, :, off : off + CHUNK], CHUNK, keep, f"x1_grouped{c}")
+            return quantize(grouped, CHUNK, f"x1_{c}")
 
-        x1_q = [quantize_x1(c, f"x1_grouped{c}") for c in range(2)]
+        x1_q = [quantize_x1(c) for c in range(2)]
         w3_q = quantize_weight(w3_raw, "w3")
 
         out_rows = out.rearrange("(p t) j -> p t j", t=PACK)
 
-        def product_b(c, x1_codes, x1_scales):
+        def product_b(c, x1_chunk):
             h, off = divmod(c * CHUNK, HALF)
             operands = [
                 (x0_q[h][0][:, off : off + CHUNK], x0_q[h][1][:, off : off + CHUNK]),
-                (x1_codes, x1_scales),
+                (x1_chunk[0][:], x1_chunk[1][:]),
             ]
             banks = []
             for pair in range(2):
-                acc = psum_acc.tile([P, 2, CHUNK], F32, name="acc")
+                acc = psum.tile([P, 2, CHUNK], F32, name="acc")
                 for u in range(2):
                     t = 2 * pair + u
-                    for a in range(PASSES):
+                    for s in range(PASSES):
                         nc.tensor.matmul_mx(
                             acc[:, u, :],
-                            lhsT=w2_q[a][0][:, P * t : P * (t + 1)].bitcast(E4M3),
-                            lhsT_scale=w2_q[a][1][:, P * t : P * (t + 1)],
-                            rhs=operands[a][0].bitcast(E4M3),
-                            rhs_scale=operands[a][1],
-                            start=(a == 0),
-                            stop=(a == PASSES - 1),
+                            lhsT=w2_q[s][0][:, P * t : P * (t + 1)].bitcast(E4M3),
+                            lhsT_scale=w2_q[s][1][:, P * t : P * (t + 1)],
+                            rhs=operands[s][0].bitcast(E4M3),
+                            rhs_scale=operands[s][1],
+                            start=(s == 0),
+                            stop=(s == PASSES - 1),
                         )
                 banks.append(acc)
             return banks
 
         def blend(c, banks):
             cols = slice(c * CHUNK, (c + 1) * CHUNK)
-            z = ring.tile([P, PACK, CHUNK], BF16, name="z_planes")
+            z = ring.tile([P, PACK, CHUNK], BF16, name="z_slices")
             for t in range(PACK):
                 nc.vector.scalar_tensor_tensor(
-                    z[:, t, :], banks[t // 2][:, t % 2, :], c_b[:, t : t + 1], a_scaled[:, t, cols], ALU.mult, ALU.add
+                    z[:, t, :], banks[t // 2][:, t % 2, :], factor_b[:, t : t + 1], a_scaled[:, t, cols], ALU.mult, ALU.add
                 )
             return interleave(z[:], CHUNK, ring, "z_grouped")
 
-        def finish(c, z_q):
+        def finish(c, z_chunk):
             cols = slice(c * CHUNK, (c + 1) * CHUNK)
             for pair in range(2):
-                acc = psum_acc.tile([P, 2, CHUNK], F32, name="acc")
+                acc = psum.tile([P, 2, CHUNK], F32, name="acc")
                 for u in range(2):
                     t = 2 * pair + u
                     nc.tensor.matmul_mx(
                         acc[:, u, :],
                         lhsT=w3_q[0][:, P * t : P * (t + 1)].bitcast(E4M3),
                         lhsT_scale=w3_q[1][:, P * t : P * (t + 1)],
-                        rhs=z_q[0][:].bitcast(E4M3),
-                        rhs_scale=z_q[1][:],
+                        rhs=z_chunk[0][:].bitcast(E4M3),
+                        rhs_scale=z_chunk[1][:],
                         start=True,
                         stop=True,
                     )
@@ -259,13 +264,14 @@ def tile_list_storm_index_cap_kernel(
                 nc.vector.tensor_tensor(result, acc[:], a_raw[:, 2 * pair : 2 * pair + 2, cols], ALU.min)
                 nc.sync.dma_start(out_rows[:, 2 * pair : 2 * pair + 2, cols], result)
 
-        banks = [product_b(c, x1_q[c][0][:], x1_q[c][1][:]) for c in range(2)]
+        b_banks = [product_b(c, x1_q[c]) for c in range(2)]
+
+        late_plane = pass1_planes[2]
         x1.append(x_tile())
-        for n in range(4, 8):
-            difference(n, 1, x1[1], "x1_grouped1" if n == 6 else None)
+        for n in pass1_planes:
+            difference(n, 1, x1[1], "x1_grouped1" if n == late_plane else next_pick_tile())
         for c in (2, 3):
-            codes, scales = quantize_x1(c, f"x1_grouped{c}")
-            banks.append(product_b(c, codes[:], scales[:]))
-        z_q = [quantize(blend(c, banks[c]), CHUNK, keep, f"z{c}") for c in range(4)]
-        for c in range(4):
+            b_banks.append(product_b(c, quantize_x1(c)))
+        z_q = [quantize(blend(c, b_banks[c]), CHUNK, f"z{c}") for c in range(S // CHUNK)]
+        for c in range(S // CHUNK):
             finish(c, z_q[c])

@@ -1,6 +1,7 @@
 from contextlib import ExitStack
 
 import concourse.mybir as mybir
+from concourse.masks import make_identity
 
 K, H, T, S = 1024, 512, 2048, 1024
 FLOPS = 2 * K * H * S * 2 + 2 * H * H * S
@@ -21,11 +22,15 @@ PACK = 4
 K_PASS = P * PACK
 PASSES = K // K_PASS
 QUADRANTS = 4
+SLICES = H // P
 STRIPE = 16
 HALF = 512
-CHUNK = 256
+BANK = 512
 RUN = 4
 PICK_TILES = 3
+CHUNK = 256
+CHUNKS = [CHUNK] * (S // CHUNK)
+LANE_BYTES = SLICES * CHUNK * 4
 
 
 def tile_list_storm_index_cap_kernel(
@@ -36,25 +41,28 @@ def tile_list_storm_index_cap_kernel(
         lists = ctx.enter_context(tc.tile_pool(name="lists", bufs=1))
         keep = ctx.enter_context(tc.tile_pool(name="keep", bufs=1))
         ring = ctx.enter_context(tc.tile_pool(name="ring", bufs=2))
-        psum = ctx.enter_context(tc.psum_pool(name="psum", bufs=8))
+        lanes = ctx.enter_context(tc.tile_pool(name="lanes", bufs=1))
+        psum = ctx.enter_context(tc.psum_pool(name="psum", bufs=2))
 
         list1 = lists.tile([P, S // STRIPE], U16, name="list1")
         list2 = lists.tile([P, S // STRIPE], U16, name="list2")
         list3 = lists.tile([P, S // STRIPE], U16, name="list3")
 
         tab_s = keep.tile([P, T], U8, name="tab_s")
-        w1_s = keep.tile([P, PASSES, H], U8, name="w1_s")
+        w1_s = keep.tile([P, PASSES, H], U8, name="w1_s", align_bytes=64)
         v_s = keep.tile([P, PASSES, S], U8, name="v_s", align_bytes=64)
         nc.gpsimd.memset(tab_s[32:64, :].bitcast(I32), 0)
         nc.gpsimd.memset(tab_s[64:128, :].bitcast(I32), 0)
+        nc.gpsimd.memset(v_s[:].rearrange("p s j -> p (s j)").bitcast(I32), 0)
         nc.gpsimd.memset(w1_s[:].rearrange("p s c -> p (s c)").bitcast(I32), 0)
-        nc.vector.memset(v_s[:].rearrange("p s j -> p (s j)").bitcast(I32), 0)
+        ident = keep.tile([P, P], F32, name="ident")
+        make_identity(nc, ident[:])
 
         planes = [keep.tile([P, T], F32, name=f"plane{n}") for n in range(PASSES * PACK)]
         tab_w = [keep.tile([P, T], I32, name=f"tab_w{s}") for s in range(PASSES)]
-        w1_w = keep.tile([P, PASSES, H // 2], I32, name="w1_w")
-        lam_t = keep.tile([P, PACK], F32, name="lam_t")
-        gain_t = keep.tile([P, PACK], F32, name="gain_t")
+        w1_w = keep.tile([P, PASSES, 2 * H], U8, name="w1_w", align_bytes=64)
+        lam_t = keep.tile([P, SLICES], F32, name="lam_t")
+        gain_t = keep.tile([P, SLICES], F32, name="gain_t")
         x_rows = xT.rearrange("(s p i) t -> s i p t", s=PASSES, i=PACK)
 
         def load_plane(n):
@@ -74,6 +82,10 @@ def tile_list_storm_index_cap_kernel(
                 w1_scales[:, 4 * q : 4 * q + 4, :].rearrange("s r c -> r s c").bitcast(I32),
             )
 
+        def load_channels(dest, vec):
+            with nc.allow_non_contiguous_dma("one factor a channel, one channel a partition"):
+                nc.sync.dma_start(dest[:], vec.rearrange("(q p) -> p q", p=P))
+
         nc.sync.dma_start(list1[:], offs)
         nc.sync.dma_start(tab_s[0:32, :].bitcast(I32), tab_scales.rearrange("s g t -> (s g) t").bitcast(I32))
         load_plane(0)
@@ -87,43 +99,43 @@ def tile_list_storm_index_cap_kernel(
             first = 4 * (QUADRANTS * s + q)
             nc.sync.dma_start(v_s[32 * q : 32 * q + 4, s, :].bitcast(I32), v_rows[first : first + 4, :].bitcast(I32))
 
+        load_tab(0)
+        nc.sync.dma_start(w1_w[:].bitcast(I32), w1_words.rearrange("s p b -> p s b").bitcast(I32))
+        load_w1_scales(0)
+        load_channels(lam_t, lam)
+        load_tab(1)
+        load_w1_scales(1)
+        load_w1_scales(2)
+        load_channels(gain_t, gain)
         load_plane(1)
-        nc.sync.dma_start(lam_t[:], lam.rearrange("(p t) -> p t", t=PACK))
-        nc.sync.dma_start(gain_t[:], gain.rearrange("(p t) -> p t", t=PACK))
-        nc.sync.dma_start(w1_w[:], w1_words.rearrange("s p b -> p s b").bitcast(I32))
-        for s in range(PASSES):
-            load_w1_scales(2 * s)
-            load_tab(s)
-            load_w1_scales(2 * s + 1)
-        for s in range(PASSES):
-            load_plane(2 + 2 * s)
-            for q in range(QUADRANTS):
-                place_v_scales(s, q)
-        for n in (5, 3, 6, 7):
+        load_w1_scales(3)
+        place_v_scales(0, 0)
+        w2_raw = [load_weight(w2[0:K_PASS, :], "w2_raw0")]
+        place_v_scales(0, 1)
+        place_v_scales(0, 2)
+        load_plane(2)
+        place_v_scales(0, 3)
+        place_v_scales(1, 0)
+        w2_raw.append(load_weight(w2[K_PASS:K, :], "w2_raw1"))
+        place_v_scales(1, 1)
+        place_v_scales(1, 2)
+        load_plane(4)
+        place_v_scales(1, 3)
+        load_plane(3)
+        for n in (5, 6, 7):
             load_plane(n)
-        w2_raw = [load_weight(w2[K_PASS * s : K_PASS * (s + 1), :], f"w2_raw{s}") for s in range(PASSES)]
 
-        factor_a = keep.tile([P, PACK], F32, name="factor_a")
-        factor_b = keep.tile([P, PACK], F32, name="factor_b")
-        rest = keep.tile([P, PACK], F32, name="rest")
+        factor_a = keep.tile([P, SLICES], F32, name="factor_a")
+        factor_b = keep.tile([P, SLICES], F32, name="factor_b")
+        rest = keep.tile([P, SLICES], F32, name="rest")
         nc.gpsimd.tensor_tensor(factor_a[:], gain_t[:], lam_t[:], ALU.mult)
         nc.gpsimd.tensor_scalar(rest[:], lam_t[:], -1.0, 1.0, ALU.mult, ALU.add)
         nc.gpsimd.tensor_tensor(factor_b[:], gain_t[:], rest[:], ALU.mult)
 
-        picks = []
-
-        def next_pick_tile():
-            picks.append(f"picked{len(picks) % PICK_TILES}")
-            return picks[-1]
-
-        def difference(n, h, dest, pick_tile):
-            picked = keep.tile([P, HALF], F32, name=pick_tile, align_bytes=64)
-            cols = slice(h * HALF // STRIPE, (h + 1) * HALF // STRIPE)
-            nc.vector.tensor_copy(picked[:], planes[n][:].indirect(list3[:, cols]))
-            nc.vector.tensor_tensor(dest[:, n % PACK, :], planes[n][:].indirect(list2[:, cols]), picked[:], ALU.subtract)
-
-        def x_tile():
-            return ring.tile([P, PACK, HALF], F32, name="x_planes")
+        def difference(n, first, width, dest, picked):
+            cols = slice(first // STRIPE, (first + width) // STRIPE)
+            nc.vector.tensor_copy(picked, planes[n][:].indirect(list3[:, cols]))
+            nc.vector.tensor_tensor(dest[:, n % PACK, :], planes[n][:].indirect(list2[:, cols]), picked, ALU.subtract)
 
         def interleave(src, width, pool, name):
             grouped = pool.tile([P, width * PACK], BF16, name=name, align_bytes=64)
@@ -139,139 +151,162 @@ def tile_list_storm_index_cap_kernel(
             nc.vector.quantize_mx(codes[:].bitcast(E4M3), scales[:], grouped[:])
             return codes, scales
 
-        def quantize_weight(raw, name):
-            grouped = ring.tile([P, H * PACK], BF16, name="w_grouped", align_bytes=64)
-            nc.scalar.copy(
-                grouped[:].rearrange("p (t m i) -> p m i t", t=PACK, i=PACK),
-                raw[:].rearrange("p i (m t) -> p m i t", t=PACK),
-            )
-            return quantize(grouped, H, name)
-
-        x0 = [x_tile() for h in range(2)]
+        x0 = [keep.tile([P, PACK, HALF], F32, name=f"x_planes{h}") for h in range(2)]
+        picks = []
 
         def both_halves(n):
             for h in range(2):
-                difference(n, h, x0[h], next_pick_tile())
+                picked = keep.tile([P, HALF], F32, name=f"picked{len(picks) % PICK_TILES}", align_bytes=64)
+                picks.append(picked)
+                difference(n, h * HALF, HALF, x0[h], picked[:])
 
         both_halves(0)
-        both_halves(1)
 
-        w1_codes = keep.tile([P, PASSES, H * 2], U8, name="w1_codes", align_bytes=64)
-        w1_planes = keep.tile([P, PASSES, H], U8, name="w1_planes", align_bytes=64)
-        nc.vector.tensor_copy(
-            w1_codes[:].bitcast(U16).rearrange("p s (t m) -> p s t m", t=PACK),
-            w1_w[:].bitcast(U16).rearrange("p s (m t) -> p s t m", t=PACK),
-        )
-        nc.vector.tensor_copy(
-            w1_planes[:].rearrange("p s (t m) -> p s t m", t=PACK),
-            w1_s[:].rearrange("p s (m t) -> p s t m", t=PACK),
-        )
-
-        a_raw = keep.tile([P, PACK, S], F32, name="a_raw")
-        a_scaled = keep.tile([P, PACK, S], F32, name="a_scaled")
-
+        a_raw = keep.tile([P, SLICES, S], F32, name="a_raw")
+        a_scaled = keep.tile([P, SLICES, S], F32, name="a_scaled")
         v_w = [keep.tile([P, S], U32, name=f"v_w{s}", align_bytes=64) for s in range(PASSES)]
         for s in range(PASSES):
             nc.vector.tensor_copy(v_w[s][:], tab_w[s][:].bitcast(U32).indirect(list1[:]))
 
         for h in range(2):
             cols = slice(h * HALF, (h + 1) * HALF)
-            for t in range(PACK):
-                acc = psum.tile([P, HALF], F32, name="acc")
+            for q in range(SLICES):
+                acc = psum.tile([P, HALF], F32, name="acc", bufs=3)
                 for s in range(PASSES):
                     nc.tensor.matmul_mx(
                         acc[:],
-                        lhsT=w1_codes[:, s, 2 * P * t : 2 * P * (t + 1)].bitcast(E2M1),
-                        lhsT_scale=w1_planes[:, s, P * t : P * (t + 1)],
+                        lhsT=w1_w[:, s, 2 * P * q : 2 * P * (q + 1)].bitcast(E2M1),
+                        lhsT_scale=w1_s[:, s, P * q : P * (q + 1)],
                         rhs=v_w[s][:, cols].bitcast(E4M3),
                         rhs_scale=v_s[:, s, cols],
                         start=(s == 0),
                         stop=(s == PASSES - 1),
                     )
-                nc.scalar.copy(a_raw[:, t, cols], acc[:])
-                nc.scalar.activation(a_scaled[:, t, cols], acc[:], ACT.Copy, scale=factor_a[:, t : t + 1])
+                nc.scalar.copy(a_raw[:, q, cols], acc[:])
+                nc.scalar.activation(a_scaled[:, q, cols], acc[:], ACT.Copy, scale=factor_a[:, q : q + 1])
 
         w3_raw = load_weight(w3, "tab_w0")
+        both_halves(1)
+        w2_q = [quantize(interleave(w2_raw[s][:], H, ring, "grouped"), H, f"w2_{s}") for s in range(PASSES)]
         both_halves(2)
         both_halves(3)
-        x0_q = [quantize(interleave(x0[h][:], HALF, ring, "x_grouped"), HALF, f"x0_{h}") for h in range(2)]
+        x0_q = [quantize(interleave(x0[h][:], HALF, ring, "grouped"), HALF, f"x0_{h}") for h in range(2)]
 
-        pass1_planes = range(PACK, 2 * PACK)
-        x1 = [x_tile()]
-        for n in pass1_planes:
-            difference(n, 0, x1[0], next_pick_tile())
-        w2_q = [quantize_weight(w2_raw[s], f"w2_{s}") for s in range(PASSES)]
+        z_codes = keep.tile([P, S], U32, name="z_codes", align_bytes=64)
+        z_scales = keep.tile([P, S], U8, name="z_scales", align_bytes=64)
 
-        def quantize_x1(c):
-            h, off = divmod(c * CHUNK, HALF)
-            grouped = interleave(x1[h][:, :, off : off + CHUNK], CHUNK, keep, f"x1_grouped{c}")
-            return quantize(grouped, CHUNK, f"x1_{c}")
+        def lane_tile(lane, shape, dtype, name, start=0):
+            return lanes.tile(shape, dtype, name=name, align_bytes=64, offset=(lane % 2) * LANE_BYTES + start)
 
-        x1_q = [quantize_x1(c) for c in range(2)]
-        w3_q = quantize_weight(w3_raw, "w3")
+        x1 = []
 
-        out_rows = out.rearrange("(p t) j -> p t j", t=PACK)
+        def gather_pair(c, pair):
+            if pair == 0:
+                x1.append(keep.tile([P, PACK, CHUNK], F32, name="x_planes1" if c % 2 else "x_chunk"))
+            for u in range(2):
+                picked = lane_tile(c + pair, [P, CHUNK], F32, f"pick{c}_{pair}_{u}", u * CHUNK * 4)
+                difference(PACK + 2 * pair + u, c * CHUNK, CHUNK, x1[c], picked[:])
 
-        def product_b(c, x1_chunk):
-            h, off = divmod(c * CHUNK, HALF)
+        def round_chunk(c):
+            grouped = lane_tile(c, [P, CHUNK * PACK], BF16, f"x1_grouped{c}")
+            nc.scalar.copy(
+                grouped[:].rearrange("p (c e i) -> p c i e", e=RUN, i=PACK),
+                x1[c][:].rearrange("p i (c e) -> p c i e", e=RUN),
+            )
+            return grouped
+
+        def blend_chunk(c, first, width, x1_q):
+            h, off = divmod(first, HALF)
             operands = [
-                (x0_q[h][0][:, off : off + CHUNK], x0_q[h][1][:, off : off + CHUNK]),
-                (x1_chunk[0][:], x1_chunk[1][:]),
+                (x0_q[h][0][:, off : off + width], x0_q[h][1][:, off : off + width]),
+                (x1_q[0][:], x1_q[1][:]),
             ]
-            banks = []
-            for pair in range(2):
-                acc = psum.tile([P, 2, CHUNK], F32, name="acc")
-                for u in range(2):
-                    t = 2 * pair + u
-                    for s in range(PASSES):
-                        nc.tensor.matmul_mx(
-                            acc[:, u, :],
-                            lhsT=w2_q[s][0][:, P * t : P * (t + 1)].bitcast(E4M3),
-                            lhsT_scale=w2_q[s][1][:, P * t : P * (t + 1)],
-                            rhs=operands[s][0].bitcast(E4M3),
-                            rhs_scale=operands[s][1],
-                            start=(s == 0),
-                            stop=(s == PASSES - 1),
+            b_scaled = lane_tile(c + 1, [P, SLICES, width], F32, f"b_scaled{c}")
+            per_bank = BANK // width
+            for q in range(SLICES):
+                if q % per_bank == 0:
+                    acc = psum.tile([P, per_bank, width], F32, name="acc", bufs=3)
+                for s in range(PASSES):
+                    nc.tensor.matmul_mx(
+                        acc[:, q % per_bank, :],
+                        lhsT=w2_q[s][0][:, P * q : P * (q + 1)].bitcast(E4M3),
+                        lhsT_scale=w2_q[s][1][:, P * q : P * (q + 1)],
+                        rhs=operands[s][0].bitcast(E4M3),
+                        rhs_scale=operands[s][1],
+                        start=(s == 0),
+                        stop=(s == PASSES - 1),
+                    )
+                if q % per_bank == per_bank - 1:
+                    for u in range(per_bank):
+                        qq = q - per_bank + 1 + u
+                        nc.scalar.activation(b_scaled[:, qq, :], acc[:, u, :], ACT.Copy, scale=factor_b[:, qq : qq + 1])
+            blocks = width // P
+            words = psum.tile([P, 2, width], F32, name="words", bufs=1)
+            for j in range(blocks):
+                turned = psum.tile([P, H], F32, name="turned", bufs=2)
+                terms = [a_scaled[:, :, first + j * P : first + (j + 1) * P], b_scaled[:, :, j * P : (j + 1) * P]]
+                for n, term in enumerate(terms):
+                    for q in range(SLICES):
+                        nc.tensor.matmul(
+                            turned[:, q * P : (q + 1) * P],
+                            lhsT=term[:, q, :],
+                            rhs=ident[:],
+                            is_transpose=True,
+                            start=(n == 0 and q == 0),
+                            stop=(n == 1 and q == SLICES - 1),
                         )
-                banks.append(acc)
-            return banks
-
-        def blend(c, banks):
-            cols = slice(c * CHUNK, (c + 1) * CHUNK)
-            z = ring.tile([P, PACK, CHUNK], BF16, name="z_slices")
-            for t in range(PACK):
-                nc.vector.scalar_tensor_tensor(
-                    z[:, t, :], banks[t // 2][:, t % 2, :], factor_b[:, t : t + 1], a_scaled[:, t, cols], ALU.mult, ALU.add
+                rounded = ring.tile([P, H], BF16, name="rounded")
+                nc.scalar.copy(
+                    rounded[:].rearrange("j (u p e) -> j u p e", u=2, e=2),
+                    turned[:].rearrange("j (p u e) -> j u p e", u=2, e=2),
                 )
-            return interleave(z[:], CHUNK, ring, "z_grouped")
-
-        def finish(c, z_chunk):
-            cols = slice(c * CHUNK, (c + 1) * CHUNK)
-            for pair in range(2):
-                acc = psum.tile([P, 2, CHUNK], F32, name="acc")
                 for u in range(2):
-                    t = 2 * pair + u
+                    nc.tensor.transpose(
+                        words[:, u, j * P : (j + 1) * P], rounded[:].bitcast(F32)[:, u * P : (u + 1) * P], ident[:]
+                    )
+            grouped = ring.tile([P, width * PACK], BF16, name="z_grouped", align_bytes=64)
+            nc.scalar.copy(
+                grouped[:].bitcast(F32).rearrange("p (j u) -> p j u", u=2), words[:].rearrange("p u j -> p j u")
+            )
+            cols = slice(first, first + width)
+            nc.vector.quantize_mx(z_codes[:, cols].bitcast(E4M3), z_scales[:, cols], grouped[:])
+
+        gather_pair(0, 0)
+        for c in range(len(CHUNKS)):
+            gather_pair(c, 1)
+            grouped = round_chunk(c)
+            if c + 1 < len(CHUNKS):
+                gather_pair(c + 1, 0)
+            blend_chunk(c, c * CHUNK, CHUNK, quantize(grouped, CHUNK, f"x1_{c}"))
+            if c == 0:
+                w3_q = quantize(interleave(w3_raw[:], H, ring, "grouped"), H, "w3")
+
+        out_rows = out.rearrange("(q p) j -> p q j", p=P)
+        results = [keep.tile([P, SLICES, HALF], F32, name=f"plane{6 + h}") for h in range(2)]
+
+        def finish(first, width):
+            cols = slice(first, first + width)
+            h, off = divmod(first, HALF)
+            per_bank = BANK // width
+            for q0 in range(0, SLICES, per_bank):
+                acc = psum.tile([P, per_bank, width], F32, name="scores", bufs=2)
+                for u in range(per_bank):
+                    q = q0 + u
                     nc.tensor.matmul_mx(
                         acc[:, u, :],
-                        lhsT=w3_q[0][:, P * t : P * (t + 1)].bitcast(E4M3),
-                        lhsT_scale=w3_q[1][:, P * t : P * (t + 1)],
-                        rhs=z_chunk[0][:].bitcast(E4M3),
-                        rhs_scale=z_chunk[1][:],
+                        lhsT=w3_q[0][:, P * q : P * (q + 1)].bitcast(E4M3),
+                        lhsT_scale=w3_q[1][:, P * q : P * (q + 1)],
+                        rhs=z_codes[:, cols].bitcast(E4M3),
+                        rhs_scale=z_scales[:, cols],
                         start=True,
                         stop=True,
                     )
-                result = a_scaled[:, 2 * pair : 2 * pair + 2, cols]
-                nc.vector.tensor_tensor(result, acc[:], a_raw[:, 2 * pair : 2 * pair + 2, cols], ALU.min)
-                nc.sync.dma_start(out_rows[:, 2 * pair : 2 * pair + 2, cols], result)
+                result = results[h][:, q0 : q0 + per_bank, off : off + width]
+                nc.vector.tensor_tensor(result, acc[:], a_raw[:, q0 : q0 + per_bank, cols], ALU.min)
+                nc.sync.dma_start(out_rows[:, q0 : q0 + per_bank, cols], result)
 
-        b_banks = [product_b(c, x1_q[c]) for c in range(2)]
-
-        late_plane = pass1_planes[2]
-        x1.append(x_tile())
-        for n in pass1_planes:
-            difference(n, 1, x1[1], "x1_grouped1" if n == late_plane else next_pick_tile())
-        for c in (2, 3):
-            b_banks.append(product_b(c, quantize_x1(c)))
-        z_q = [quantize(blend(c, b_banks[c]), CHUNK, f"z{c}") for c in range(S // CHUNK)]
-        for c in range(S // CHUNK):
-            finish(c, z_q[c])
+        finish(0, HALF)
+        first = HALF
+        for width in CHUNKS[2:]:
+            finish(first, width)
+            first = first + width

@@ -29,8 +29,8 @@ BANK = 512
 RUN = 4
 PICK_TILES = 3
 CHUNK = 256
-CHUNKS = [CHUNK] * (S // CHUNK)
-LANE_BYTES = SLICES * CHUNK * 4
+ACC_BANKS = 4
+TURN_BANKS = 3
 
 
 def tile_list_storm_index_cap_kernel(
@@ -59,8 +59,8 @@ def tile_list_storm_index_cap_kernel(
         make_identity(nc, ident[:])
 
         planes = [keep.tile([P, T], F32, name=f"plane{n}") for n in range(PASSES * PACK)]
-        tab_w = [keep.tile([P, T], I32, name=f"tab_w{s}") for s in range(PASSES)]
-        w1_w = keep.tile([P, PASSES, 2 * H], U8, name="w1_w", align_bytes=64)
+        tab_w = [keep.tile([P, T], I32, name=f"tab_w{s}", align_bytes=64) for s in range(PASSES)]
+        w1_w = keep.tile([P, PASSES, H // 2], I32, name="w1_w")
         lam_t = keep.tile([P, SLICES], F32, name="lam_t")
         gain_t = keep.tile([P, SLICES], F32, name="gain_t")
         x_rows = xT.rearrange("(s p i) t -> s i p t", s=PASSES, i=PACK)
@@ -72,7 +72,7 @@ def tile_list_storm_index_cap_kernel(
             nc.sync.dma_start(tab_w[s][:], tab_words[s].rearrange("p t i -> p (t i)").bitcast(I32))
 
         def load_weight(rows, name):
-            raw = keep.tile([P, PACK, H], F32, name=name)
+            raw = keep.tile([P, PACK, H], F32, name=name, align_bytes=64)
             nc.sync.dma_start(raw[:], rows.rearrange("(p i) c -> p i c", i=PACK))
             return raw
 
@@ -83,8 +83,7 @@ def tile_list_storm_index_cap_kernel(
             )
 
         def load_channels(dest, vec):
-            with nc.allow_non_contiguous_dma("one factor a channel, one channel a partition"):
-                nc.sync.dma_start(dest[:], vec.rearrange("(q p) -> p q", p=P))
+            nc.sync.dma_start(dest[:], vec.rearrange("(p t) -> p t", t=SLICES))
 
         nc.sync.dma_start(list1[:], offs)
         nc.sync.dma_start(tab_s[0:32, :].bitcast(I32), tab_scales.rearrange("s g t -> (s g) t").bitcast(I32))
@@ -100,29 +99,23 @@ def tile_list_storm_index_cap_kernel(
             nc.sync.dma_start(v_s[32 * q : 32 * q + 4, s, :].bitcast(I32), v_rows[first : first + 4, :].bitcast(I32))
 
         load_tab(0)
-        nc.sync.dma_start(w1_w[:].bitcast(I32), w1_words.rearrange("s p b -> p s b").bitcast(I32))
+        nc.sync.dma_start(w1_w[:], w1_words.rearrange("s p b -> p s b").bitcast(I32))
         load_w1_scales(0)
+        load_w1_scales(1)
         load_channels(lam_t, lam)
         load_tab(1)
-        load_w1_scales(1)
         load_w1_scales(2)
+        load_w1_scales(3)
         load_channels(gain_t, gain)
         load_plane(1)
-        load_w1_scales(3)
-        place_v_scales(0, 0)
+        for q in range(QUADRANTS):
+            place_v_scales(0, q)
         w2_raw = [load_weight(w2[0:K_PASS, :], "w2_raw0")]
-        place_v_scales(0, 1)
-        place_v_scales(0, 2)
+        for q in range(QUADRANTS):
+            place_v_scales(1, q)
         load_plane(2)
-        place_v_scales(0, 3)
-        place_v_scales(1, 0)
         w2_raw.append(load_weight(w2[K_PASS:K, :], "w2_raw1"))
-        place_v_scales(1, 1)
-        place_v_scales(1, 2)
-        load_plane(4)
-        place_v_scales(1, 3)
-        load_plane(3)
-        for n in (5, 6, 7):
+        for n in (3, 4, 5, 6, 7):
             load_plane(n)
 
         factor_a = keep.tile([P, SLICES], F32, name="factor_a")
@@ -132,17 +125,28 @@ def tile_list_storm_index_cap_kernel(
         nc.gpsimd.tensor_scalar(rest[:], lam_t[:], -1.0, 1.0, ALU.mult, ALU.add)
         nc.gpsimd.tensor_tensor(factor_b[:], gain_t[:], rest[:], ALU.mult)
 
+        def entries(first, width):
+            return slice(first // STRIPE, (first + width) // STRIPE)
+
+        def pick(n, first, width, picked):
+            nc.vector.tensor_copy(picked, planes[n][:].indirect(list3[:, entries(first, width)]))
+
+        def subtract(n, first, width, dest, picked):
+            nc.vector.tensor_tensor(dest, planes[n][:].indirect(list2[:, entries(first, width)]), picked, ALU.subtract)
+
         def difference(n, first, width, dest, picked):
-            cols = slice(first // STRIPE, (first + width) // STRIPE)
-            nc.vector.tensor_copy(picked, planes[n][:].indirect(list3[:, cols]))
-            nc.vector.tensor_tensor(dest[:, n % PACK, :], planes[n][:].indirect(list2[:, cols]), picked, ALU.subtract)
+            pick(n, first, width, picked)
+            subtract(n, first, width, dest[:, n % PACK, :], picked)
+
+        def interleave_into(grouped, src):
+            nc.scalar.copy(
+                grouped.rearrange("p (c e i) -> p c i e", e=RUN, i=PACK),
+                src.rearrange("p i (c e) -> p c i e", e=RUN),
+            )
 
         def interleave(src, width, pool, name):
             grouped = pool.tile([P, width * PACK], BF16, name=name, align_bytes=64)
-            nc.scalar.copy(
-                grouped[:].rearrange("p (c e i) -> p c i e", e=RUN, i=PACK),
-                src.rearrange("p i (c e) -> p c i e", e=RUN),
-            )
+            interleave_into(grouped[:], src)
             return grouped
 
         def quantize(grouped, width, name):
@@ -151,16 +155,38 @@ def tile_list_storm_index_cap_kernel(
             nc.vector.quantize_mx(codes[:].bitcast(E4M3), scales[:], grouped[:])
             return codes, scales
 
-        x0 = [keep.tile([P, PACK, HALF], F32, name=f"x_planes{h}") for h in range(2)]
+        def round_weight(raw, pool, name):
+            grouped = pool.tile([P, H * PACK], BF16, name=name, align_bytes=64)
+            nc.scalar.copy(
+                grouped[:].rearrange("p (t m i) -> p m i t", t=SLICES, i=PACK),
+                raw[:].rearrange("p i (m t) -> p m i t", t=SLICES),
+            )
+            return grouped
+
+        x0 = [keep.tile([P, PACK, HALF], F32, name=f"x_planes{h}", align_bytes=64) for h in range(2)]
         picks = []
+
+        def pick_tile(width):
+            picks.append(keep.tile([P, width], F32, name=f"picked{len(picks) % PICK_TILES}", align_bytes=64))
+            return picks[-1]
 
         def both_halves(n):
             for h in range(2):
-                picked = keep.tile([P, HALF], F32, name=f"picked{len(picks) % PICK_TILES}", align_bytes=64)
-                picks.append(picked)
-                difference(n, h * HALF, HALF, x0[h], picked[:])
+                difference(n, h * HALF, HALF, x0[h], pick_tile(HALF)[:])
 
-        both_halves(0)
+        difference(0, 0, HALF, x0[0], pick_tile(HALF)[:])
+        difference(0, HALF, HALF, x0[1], keep.tile([P, HALF], F32, name="w1_codes", align_bytes=64)[:])
+
+        w1_codes = keep.tile([P, PASSES, H * 2], U8, name="w1_codes", align_bytes=64)
+        w1_planes = keep.tile([P, PASSES, H], U8, name="w1_planes", align_bytes=64)
+        nc.gpsimd.tensor_copy(
+            w1_codes[:].rearrange("p s (t m b) -> p s t m b", t=SLICES, b=2),
+            w1_w[:].bitcast(U8).rearrange("p s (m t b) -> p s t m b", t=SLICES, b=2),
+        )
+        nc.gpsimd.tensor_copy(
+            w1_planes[:].rearrange("p s (t m) -> p s t m", t=SLICES),
+            w1_s[:].rearrange("p s (m t) -> p s t m", t=SLICES),
+        )
 
         a_raw = keep.tile([P, SLICES, S], F32, name="a_raw")
         a_scaled = keep.tile([P, SLICES, S], F32, name="a_scaled")
@@ -171,12 +197,12 @@ def tile_list_storm_index_cap_kernel(
         for h in range(2):
             cols = slice(h * HALF, (h + 1) * HALF)
             for q in range(SLICES):
-                acc = psum.tile([P, HALF], F32, name="acc", bufs=3)
+                acc = psum.tile([P, HALF], F32, name="acc", bufs=ACC_BANKS)
                 for s in range(PASSES):
                     nc.tensor.matmul_mx(
                         acc[:],
-                        lhsT=w1_w[:, s, 2 * P * q : 2 * P * (q + 1)].bitcast(E2M1),
-                        lhsT_scale=w1_s[:, s, P * q : P * (q + 1)],
+                        lhsT=w1_codes[:, s, 2 * P * q : 2 * P * (q + 1)].bitcast(E2M1),
+                        lhsT_scale=w1_planes[:, s, P * q : P * (q + 1)],
                         rhs=v_w[s][:, cols].bitcast(E4M3),
                         rhs_scale=v_s[:, s, cols],
                         start=(s == 0),
@@ -187,63 +213,73 @@ def tile_list_storm_index_cap_kernel(
 
         w3_raw = load_weight(w3, "tab_w0")
         both_halves(1)
-        w2_q = [quantize(interleave(w2_raw[s][:], H, ring, "grouped"), H, f"w2_{s}") for s in range(PASSES)]
+        w2_q = [quantize(round_weight(w2_raw[s], keep, f"w2_grouped{s}"), H, f"w2_{s}") for s in range(PASSES)]
         both_halves(2)
         both_halves(3)
-        x0_q = [quantize(interleave(x0[h][:], HALF, ring, "grouped"), HALF, f"x0_{h}") for h in range(2)]
+        x0_grouped = [
+            keep.tile([P, HALF * PACK], BF16, name="w2_grouped0", align_bytes=64),
+            lanes.tile([P, HALF * PACK], BF16, name="x0_grouped1", align_bytes=64, offset=0),
+        ]
+        x0_q = []
+        for h in range(2):
+            interleave_into(x0_grouped[h][:], x0[h][:])
+            x0_q.append(quantize(x0_grouped[h], HALF, f"x0_{h}"))
 
         z_codes = keep.tile([P, S], U32, name="z_codes", align_bytes=64)
         z_scales = keep.tile([P, S], U8, name="z_scales", align_bytes=64)
 
-        def lane_tile(lane, shape, dtype, name, start=0):
-            return lanes.tile(shape, dtype, name=name, align_bytes=64, offset=(lane % 2) * LANE_BYTES + start)
-
-        x1 = []
-
-        def gather_pair(c, pair):
-            if pair == 0:
-                x1.append(keep.tile([P, PACK, CHUNK], F32, name="x_planes1" if c % 2 else "x_chunk"))
+        def gather_pair(h, pair, dest):
+            if h == 0 and pair == 0:
+                both = keep.tile([P, 2, HALF], F32, name="w2_grouped1", align_bytes=64)
+            taken = []
             for u in range(2):
-                picked = lane_tile(c + pair, [P, CHUNK], F32, f"pick{c}_{pair}_{u}", u * CHUNK * 4)
-                difference(PACK + 2 * pair + u, c * CHUNK, CHUNK, x1[c], picked[:])
+                if h == 0 and pair == 0:
+                    picked = both[:, u, :]
+                elif h == 1 and u == 1:
+                    picked = keep.tile([P, HALF], F32, name="x1_grouped0", align_bytes=64)[:]
+                else:
+                    picked = lanes.tile(
+                        [P, HALF], F32, name=f"pick{h}_{pair}_{u}", align_bytes=64, offset=(u + h) * HALF * 4
+                    )[:]
+                pick(PACK + 2 * pair + u, h * HALF, HALF, picked)
+                taken.append(picked)
+            width = CHUNK if h == 1 and pair == 1 else HALF
+            for off in range(0, HALF, width):
+                for u in range(2):
+                    i = 2 * pair + u
+                    part = slice(off, off + width)
+                    subtract(PACK + i, h * HALF + off, width, dest[:, i, part], taken[u][:, part])
 
-        def round_chunk(c):
-            grouped = lane_tile(c, [P, CHUNK * PACK], BF16, f"x1_grouped{c}")
-            nc.scalar.copy(
-                grouped[:].rearrange("p (c e i) -> p c i e", e=RUN, i=PACK),
-                x1[c][:].rearrange("p i (c e) -> p c i e", e=RUN),
-            )
-            return grouped
-
-        def blend_chunk(c, first, width, x1_q):
-            h, off = divmod(first, HALF)
+        def product_b(c, x1_q):
+            h, off = divmod(c * CHUNK, HALF)
             operands = [
-                (x0_q[h][0][:, off : off + width], x0_q[h][1][:, off : off + width]),
+                (x0_q[h][0][:, off : off + CHUNK], x0_q[h][1][:, off : off + CHUNK]),
                 (x1_q[0][:], x1_q[1][:]),
             ]
-            b_scaled = lane_tile(c + 1, [P, SLICES, width], F32, f"b_scaled{c}")
-            per_bank = BANK // width
-            for q in range(SLICES):
-                if q % per_bank == 0:
-                    acc = psum.tile([P, per_bank, width], F32, name="acc", bufs=3)
-                for s in range(PASSES):
+            banks = [psum.tile([P, 2, CHUNK], F32, name="acc", bufs=ACC_BANKS) for pair in range(2)]
+            for s in range(PASSES):
+                for q in range(SLICES):
                     nc.tensor.matmul_mx(
-                        acc[:, q % per_bank, :],
+                        banks[q // 2][:, q % 2, :],
                         lhsT=w2_q[s][0][:, P * q : P * (q + 1)].bitcast(E4M3),
                         lhsT_scale=w2_q[s][1][:, P * q : P * (q + 1)],
                         rhs=operands[s][0].bitcast(E4M3),
                         rhs_scale=operands[s][1],
-                        start=(s == 0),
-                        stop=(s == PASSES - 1),
+                        start=(s == 0 and q % 2 == 0),
+                        stop=(s == PASSES - 1 and q % 2 == 1),
                     )
-                if q % per_bank == per_bank - 1:
-                    for u in range(per_bank):
-                        qq = q - per_bank + 1 + u
-                        nc.scalar.activation(b_scaled[:, qq, :], acc[:, u, :], ACT.Copy, scale=factor_b[:, qq : qq + 1])
-            blocks = width // P
-            words = psum.tile([P, 2, width], F32, name="words", bufs=1)
-            for j in range(blocks):
-                turned = psum.tile([P, H], F32, name="turned", bufs=2)
+            return banks
+
+        def blend_turned(c, banks):
+            first = c * CHUNK
+            b_scaled = keep.tile([P, SLICES, CHUNK], F32, name=f"w2_raw{c % 2}", align_bytes=64)
+            for q in range(SLICES):
+                nc.scalar.activation(
+                    b_scaled[:, q, :], banks[q // 2][:, q % 2, :], ACT.Copy, scale=factor_b[:, q : q + 1]
+                )
+            words = psum.tile([P, 2, CHUNK], F32, name="words", bufs=1)
+            for j in range(CHUNK // P):
+                turned = psum.tile([P, H], F32, name="turned", bufs=TURN_BANKS)
                 terms = [a_scaled[:, :, first + j * P : first + (j + 1) * P], b_scaled[:, :, j * P : (j + 1) * P]]
                 for n, term in enumerate(terms):
                     for q in range(SLICES):
@@ -258,30 +294,63 @@ def tile_list_storm_index_cap_kernel(
                 rounded = ring.tile([P, H], BF16, name="rounded")
                 nc.scalar.copy(
                     rounded[:].rearrange("j (u p e) -> j u p e", u=2, e=2),
-                    turned[:].rearrange("j (p u e) -> j u p e", u=2, e=2),
+                    turned[:].rearrange("j (u e p) -> j u p e", u=2, e=2),
                 )
                 for u in range(2):
                     nc.tensor.transpose(
                         words[:, u, j * P : (j + 1) * P], rounded[:].bitcast(F32)[:, u * P : (u + 1) * P], ident[:]
                     )
-            grouped = ring.tile([P, width * PACK], BF16, name="z_grouped", align_bytes=64)
+            grouped = ring.tile([P, CHUNK * PACK], BF16, name="z_grouped", align_bytes=64)
             nc.scalar.copy(
                 grouped[:].bitcast(F32).rearrange("p (j u) -> p j u", u=2), words[:].rearrange("p u j -> p j u")
             )
+            return grouped
+
+        def blend_direct(c, banks):
+            cols = slice(c * CHUNK, (c + 1) * CHUNK)
+            z = ring.tile([P, SLICES, CHUNK], BF16, name="z_slices")
+            for q in range(SLICES):
+                nc.vector.scalar_tensor_tensor(
+                    z[:, q, :], banks[q // 2][:, q % 2, :], factor_b[:, q : q + 1], a_scaled[:, q, cols], ALU.mult, ALU.add
+                )
+            return z
+
+        def quantize_x1(c, grouped):
+            codes = keep.tile([P, CHUNK], U32, name=f"x1_codes{c}", align_bytes=64)
+            scales = keep.tile([P, CHUNK], U8, name=f"x1_scales{c}", align_bytes=64)
+            nc.vector.quantize_mx(codes[:].bitcast(E4M3), scales[:], grouped)
+            return codes, scales
+
+        def quantize_z(first, width, z_grouped):
             cols = slice(first, first + width)
-            nc.vector.quantize_mx(z_codes[:, cols].bitcast(E4M3), z_scales[:, cols], grouped[:])
+            nc.vector.quantize_mx(z_codes[:, cols].bitcast(E4M3), z_scales[:, cols], z_grouped[:])
 
-        gather_pair(0, 0)
-        for c in range(len(CHUNKS)):
-            gather_pair(c, 1)
-            grouped = round_chunk(c)
-            if c + 1 < len(CHUNKS):
-                gather_pair(c + 1, 0)
-            blend_chunk(c, c * CHUNK, CHUNK, quantize(grouped, CHUNK, f"x1_{c}"))
-            if c == 0:
-                w3_q = quantize(interleave(w3_raw[:], H, ring, "grouped"), H, "w3")
+        x1 = [keep.tile([P, PACK, HALF], F32, name="x_planes2")]
+        for pair in range(2):
+            gather_pair(0, pair, x1[0])
+        x1_q = []
+        for c, name in enumerate(("x1_grouped0", "x_planes1")):
+            grouped = interleave(x1[0][:, :, c * CHUNK : (c + 1) * CHUNK], CHUNK, keep, name)
+            x1_q.append(quantize_x1(c, grouped[:]))
+        for c in range(2):
+            quantize_z(c * CHUNK, CHUNK, blend_turned(c, product_b(c, x1_q[c])))
+        w3_q = quantize(round_weight(w3_raw, keep, "tab_w1"), H, "w3")
+        x1.append(keep.tile([P, PACK, HALF], F32, name="x_planes1", align_bytes=64))
+        for pair in range(2):
+            gather_pair(1, pair, x1[1])
+        banks = []
+        last_grouped = keep.tile([P, 2, CHUNK * PACK], BF16, name="w2_raw1", align_bytes=64)
+        for c in (2, 3):
+            interleave_into(last_grouped[:, c - 2, :], x1[1][:, :, (c - 2) * CHUNK : (c - 1) * CHUNK])
+            banks.append(product_b(c, quantize_x1(c, last_grouped[:, c - 2, :])))
+        for c in (2, 3):
+            z = blend_direct(c, banks[c - 2])
+            width = P if c == 3 else CHUNK
+            for off in range(0, CHUNK, width):
+                z_grouped = interleave(z[:, :, off : off + width], width, ring, "z_grouped")
+                quantize_z(c * CHUNK + off, width, z_grouped)
 
-        out_rows = out.rearrange("(q p) j -> p q j", p=P)
+        out_rows = out.rearrange("(p q) j -> p q j", q=SLICES)
         results = [keep.tile([P, SLICES, HALF], F32, name=f"plane{6 + h}") for h in range(2)]
 
         def finish(first, width):
@@ -289,7 +358,7 @@ def tile_list_storm_index_cap_kernel(
             h, off = divmod(first, HALF)
             per_bank = BANK // width
             for q0 in range(0, SLICES, per_bank):
-                acc = psum.tile([P, per_bank, width], F32, name="scores", bufs=2)
+                acc = psum.tile([P, per_bank, width], F32, name="turned", bufs=TURN_BANKS)
                 for u in range(per_bank):
                     q = q0 + u
                     nc.tensor.matmul_mx(
@@ -305,8 +374,7 @@ def tile_list_storm_index_cap_kernel(
                 nc.vector.tensor_tensor(result, acc[:], a_raw[:, q0 : q0 + per_bank, cols], ALU.min)
                 nc.sync.dma_start(out_rows[:, q0 : q0 + per_bank, cols], result)
 
-        finish(0, HALF)
-        first = HALF
-        for width in CHUNKS[2:]:
-            finish(first, width)
-            first = first + width
+        for first in range(0, S - CHUNK, CHUNK):
+            finish(first, CHUNK)
+        for first in range(S - CHUNK, S, P):
+            finish(first, P)

@@ -29,8 +29,8 @@ BANK = 512
 RUN = 4
 PICK_TILES = 3
 CHUNK = 256
-ACC_BANKS = 4
-TURN_BANKS = 3
+B_BANKS = [0, 2, 2, 4]
+SLOT = HALF * 4
 
 
 def tile_list_storm_index_cap_kernel(
@@ -42,7 +42,7 @@ def tile_list_storm_index_cap_kernel(
         keep = ctx.enter_context(tc.tile_pool(name="keep", bufs=1))
         ring = ctx.enter_context(tc.tile_pool(name="ring", bufs=2))
         lanes = ctx.enter_context(tc.tile_pool(name="lanes", bufs=1))
-        psum = ctx.enter_context(tc.psum_pool(name="psum", bufs=2))
+        psum = ctx.enter_context(tc.psum_pool(name="psum", bufs=1))
 
         list1 = lists.tile([P, S // STRIPE], U16, name="list1")
         list2 = lists.tile([P, S // STRIPE], U16, name="list2")
@@ -188,8 +188,11 @@ def tile_list_storm_index_cap_kernel(
             w1_s[:].rearrange("p s (m t) -> p s t m", t=SLICES),
         )
 
+        def bank(n, shape):
+            return psum.tile(shape, F32, name=f"bank{n}")
+
         a_raw = keep.tile([P, SLICES, S], F32, name="a_raw")
-        a_scaled = keep.tile([P, SLICES, S], F32, name="a_scaled")
+        a_scaled = [keep.tile([P, SLICES, HALF], F32, name=f"a_scaled{h}") for h in range(2)]
         v_w = [keep.tile([P, S], U32, name=f"v_w{s}", align_bytes=64) for s in range(PASSES)]
         for s in range(PASSES):
             nc.vector.tensor_copy(v_w[s][:], tab_w[s][:].bitcast(U32).indirect(list1[:]))
@@ -197,7 +200,7 @@ def tile_list_storm_index_cap_kernel(
         for h in range(2):
             cols = slice(h * HALF, (h + 1) * HALF)
             for q in range(SLICES):
-                acc = psum.tile([P, HALF], F32, name="acc", bufs=ACC_BANKS)
+                acc = bank(q, [P, HALF])
                 for s in range(PASSES):
                     nc.tensor.matmul_mx(
                         acc[:],
@@ -209,7 +212,7 @@ def tile_list_storm_index_cap_kernel(
                         stop=(s == PASSES - 1),
                     )
                 nc.scalar.copy(a_raw[:, q, cols], acc[:])
-                nc.scalar.activation(a_scaled[:, q, cols], acc[:], ACT.Copy, scale=factor_a[:, q : q + 1])
+                nc.scalar.activation(a_scaled[h][:, q, :], acc[:], ACT.Copy, scale=factor_a[:, q : q + 1])
 
         w3_raw = load_weight(w3, "tab_w0")
         both_halves(1)
@@ -217,15 +220,13 @@ def tile_list_storm_index_cap_kernel(
         both_halves(2)
         both_halves(3)
         x0_grouped = [
+            lanes.tile([P, HALF * PACK], BF16, name="x0_grouped0", align_bytes=64, offset=0),
             keep.tile([P, HALF * PACK], BF16, name="w2_grouped0", align_bytes=64),
-            lanes.tile([P, HALF * PACK], BF16, name="x0_grouped1", align_bytes=64, offset=0),
         ]
-        x0_q = []
         for h in range(2):
             interleave_into(x0_grouped[h][:], x0[h][:])
-            x0_q.append(quantize(x0_grouped[h], HALF, f"x0_{h}"))
+        x0_q = [quantize(x0_grouped[0], HALF, "x0_0")]
 
-        z_codes = keep.tile([P, S], U32, name="z_codes", align_bytes=64)
         z_scales = keep.tile([P, S], U8, name="z_scales", align_bytes=64)
 
         def gather_pair(h, pair, dest):
@@ -239,7 +240,7 @@ def tile_list_storm_index_cap_kernel(
                     picked = keep.tile([P, HALF], F32, name="x1_grouped0", align_bytes=64)[:]
                 else:
                     picked = lanes.tile(
-                        [P, HALF], F32, name=f"pick{h}_{pair}_{u}", align_bytes=64, offset=(u + h) * HALF * 4
+                        [P, HALF], F32, name=f"pick{h}_{pair}_{u}", align_bytes=64, offset=SLOT // 2 if h else u * SLOT
                     )[:]
                 pick(PACK + 2 * pair + u, h * HALF, HALF, picked)
                 taken.append(picked)
@@ -256,7 +257,7 @@ def tile_list_storm_index_cap_kernel(
                 (x0_q[h][0][:, off : off + CHUNK], x0_q[h][1][:, off : off + CHUNK]),
                 (x1_q[0][:], x1_q[1][:]),
             ]
-            banks = [psum.tile([P, 2, CHUNK], F32, name="acc", bufs=ACC_BANKS) for pair in range(2)]
+            banks = [bank(B_BANKS[c] + pair, [P, 2, CHUNK]) for pair in range(2)]
             for s in range(PASSES):
                 for q in range(SLICES):
                     nc.tensor.matmul_mx(
@@ -270,17 +271,17 @@ def tile_list_storm_index_cap_kernel(
                     )
             return banks
 
-        def blend_turned(c, banks):
+        def blend_turned(c, banks, grouped):
             first = c * CHUNK
             b_scaled = keep.tile([P, SLICES, CHUNK], F32, name=f"w2_raw{c % 2}", align_bytes=64)
             for q in range(SLICES):
                 nc.scalar.activation(
                     b_scaled[:, q, :], banks[q // 2][:, q % 2, :], ACT.Copy, scale=factor_b[:, q : q + 1]
                 )
-            words = psum.tile([P, 2, CHUNK], F32, name="words", bufs=1)
+            words = bank(c, [P, 2, CHUNK])
             for j in range(CHUNK // P):
-                turned = psum.tile([P, H], F32, name="turned", bufs=TURN_BANKS)
-                terms = [a_scaled[:, :, first + j * P : first + (j + 1) * P], b_scaled[:, :, j * P : (j + 1) * P]]
+                turned = bank(4 + 2 * c + j, [P, H])
+                terms = [a_scaled[0][:, :, first + j * P : first + (j + 1) * P], b_scaled[:, :, j * P : (j + 1) * P]]
                 for n, term in enumerate(terms):
                     for q in range(SLICES):
                         nc.tensor.matmul(
@@ -300,18 +301,14 @@ def tile_list_storm_index_cap_kernel(
                     nc.tensor.transpose(
                         words[:, u, j * P : (j + 1) * P], rounded[:].bitcast(F32)[:, u * P : (u + 1) * P], ident[:]
                     )
-            grouped = ring.tile([P, CHUNK * PACK], BF16, name="z_grouped", align_bytes=64)
-            nc.scalar.copy(
-                grouped[:].bitcast(F32).rearrange("p (j u) -> p j u", u=2), words[:].rearrange("p u j -> p j u")
-            )
-            return grouped
+            nc.scalar.copy(grouped.rearrange("p (j u) -> p j u", u=2), words[:].rearrange("p u j -> p j u"))
 
         def blend_direct(c, banks):
-            cols = slice(c * CHUNK, (c + 1) * CHUNK)
+            cols = slice(c * CHUNK - HALF, (c + 1) * CHUNK - HALF)
             z = ring.tile([P, SLICES, CHUNK], BF16, name="z_slices")
             for q in range(SLICES):
                 nc.vector.scalar_tensor_tensor(
-                    z[:, q, :], banks[q // 2][:, q % 2, :], factor_b[:, q : q + 1], a_scaled[:, q, cols], ALU.mult, ALU.add
+                    z[:, q, :], banks[q // 2][:, q % 2, :], factor_b[:, q : q + 1], a_scaled[1][:, q, cols], ALU.mult, ALU.add
                 )
             return z
 
@@ -323,18 +320,27 @@ def tile_list_storm_index_cap_kernel(
 
         def quantize_z(first, width, z_grouped):
             cols = slice(first, first + width)
-            nc.vector.quantize_mx(z_codes[:, cols].bitcast(E4M3), z_scales[:, cols], z_grouped[:])
+            nc.vector.quantize_mx(z_codes[:, cols].bitcast(E4M3), z_scales[:, cols], z_grouped)
 
         x1 = [keep.tile([P, PACK, HALF], F32, name="x_planes2")]
         for pair in range(2):
             gather_pair(0, pair, x1[0])
+        x0_q.append(
+            (
+                lanes.tile([P, HALF], U32, name="x0_1_codes", align_bytes=64, offset=3 * SLOT // 2),
+                keep.tile([P, HALF], U8, name="x0_1_scales", align_bytes=64),
+            )
+        )
+        nc.vector.quantize_mx(x0_q[1][0][:].bitcast(E4M3), x0_q[1][1][:], x0_grouped[1][:])
         x1_q = []
         for c, name in enumerate(("x1_grouped0", "x_planes1")):
             grouped = interleave(x1[0][:, :, c * CHUNK : (c + 1) * CHUNK], CHUNK, keep, name)
             x1_q.append(quantize_x1(c, grouped[:]))
+        z_words = keep.tile([P, 2 * HALF], F32, name="z_words", align_bytes=64)
+        first_banks = [product_b(c, x1_q[c]) for c in range(2)]
         for c in range(2):
-            quantize_z(c * CHUNK, CHUNK, blend_turned(c, product_b(c, x1_q[c])))
-        w3_q = quantize(round_weight(w3_raw, keep, "tab_w1"), H, "w3")
+            blend_turned(c, first_banks[c], z_words[:, 2 * CHUNK * c : 2 * CHUNK * (c + 1)])
+        w3_grouped = round_weight(w3_raw, keep, "tab_w1")
         x1.append(keep.tile([P, PACK, HALF], F32, name="x_planes1", align_bytes=64))
         for pair in range(2):
             gather_pair(1, pair, x1[1])
@@ -343,22 +349,28 @@ def tile_list_storm_index_cap_kernel(
         for c in (2, 3):
             interleave_into(last_grouped[:, c - 2, :], x1[1][:, :, (c - 2) * CHUNK : (c - 1) * CHUNK])
             banks.append(product_b(c, quantize_x1(c, last_grouped[:, c - 2, :])))
+        w3_q = (
+            lanes.tile([P, H], U32, name="w3_codes", align_bytes=64, offset=SLOT // 2),
+            keep.tile([P, H], U8, name="w3_scales", align_bytes=64),
+        )
+        nc.vector.quantize_mx(w3_q[0][:].bitcast(E4M3), w3_q[1][:], w3_grouped[:])
+        z_codes = keep.tile([P, S], U32, name="w2_raw1", align_bytes=64)
+        quantize_z(0, HALF, z_words[:].bitcast(BF16))
         for c in (2, 3):
-            z = blend_direct(c, banks[c - 2])
-            width = P if c == 3 else CHUNK
-            for off in range(0, CHUNK, width):
-                z_grouped = interleave(z[:, :, off : off + width], width, ring, "z_grouped")
-                quantize_z(c * CHUNK + off, width, z_grouped)
+            quantize_z(c * CHUNK, CHUNK, interleave(blend_direct(c, banks[c - 2])[:], CHUNK, ring, "z_last")[:])
 
         out_rows = out.rearrange("(p q) j -> p q j", q=SLICES)
-        results = [keep.tile([P, SLICES, HALF], F32, name=f"plane{6 + h}") for h in range(2)]
+        results = [keep.tile([P, SLICES, HALF], F32, name=f"a_scaled{1 - h}") for h in range(2)]
 
         def finish(first, width):
             cols = slice(first, first + width)
             h, off = divmod(first, HALF)
             per_bank = BANK // width
             for q0 in range(0, SLICES, per_bank):
-                acc = psum.tile([P, per_bank, width], F32, name="turned", bufs=TURN_BANKS)
+                if h == 1:
+                    acc = bank(B_BANKS[first // CHUNK] + q0 // 2, [P, per_bank, width])
+                else:
+                    acc = bank((6 + q0) % 8, [P, per_bank, width])
                 for u in range(per_bank):
                     q = q0 + u
                     nc.tensor.matmul_mx(
@@ -374,7 +386,6 @@ def tile_list_storm_index_cap_kernel(
                 nc.vector.tensor_tensor(result, acc[:], a_raw[:, q0 : q0 + per_bank, cols], ALU.min)
                 nc.sync.dma_start(out_rows[:, q0 : q0 + per_bank, cols], result)
 
-        for first in range(0, S - CHUNK, CHUNK):
+        finish(0, HALF)
+        for first in range(HALF, S, CHUNK):
             finish(first, CHUNK)
-        for first in range(S - CHUNK, S, P):
-            finish(first, P)

@@ -27,10 +27,8 @@ STRIPE = 16
 HALF = 512
 BANK = 512
 RUN = 4
-PICK_TILES = 3
 CHUNK = 256
-B_BANKS = [0, 2, 2, 4]
-SLOT = HALF * 4
+KIB = 1024
 
 
 def tile_list_storm_index_cap_kernel(
@@ -43,6 +41,12 @@ def tile_list_storm_index_cap_kernel(
         ring = ctx.enter_context(tc.tile_pool(name="ring", bufs=2))
         lanes = ctx.enter_context(tc.tile_pool(name="lanes", bufs=1))
         psum = ctx.enter_context(tc.psum_pool(name="psum", bufs=1))
+
+        def lane(name, shape, dtype, kib):
+            return lanes.tile(shape, dtype, name=name, align_bytes=64, offset=int(kib * KIB))
+
+        W2_RAW, RING, W1_SLOT, PAIR, X0, LAST, W2_GROUPED, A0 = (0, 8), (16, 18), 20, 22, 26, 42, (46, 50), 54
+        CODES, X1 = 62, 66
 
         list1 = lists.tile([P, S // STRIPE], U16, name="list1")
         list2 = lists.tile([P, S // STRIPE], U16, name="list2")
@@ -71,10 +75,8 @@ def tile_list_storm_index_cap_kernel(
         def load_tab(s):
             nc.sync.dma_start(tab_w[s][:], tab_words[s].rearrange("p t i -> p (t i)").bitcast(I32))
 
-        def load_weight(rows, name):
-            raw = keep.tile([P, PACK, H], F32, name=name, align_bytes=64)
+        def load_weight(raw, rows):
             nc.sync.dma_start(raw[:], rows.rearrange("(p i) c -> p i c", i=PACK))
-            return raw
 
         def load_w1_scales(q):
             nc.sync.dma_start(
@@ -98,6 +100,7 @@ def tile_list_storm_index_cap_kernel(
             first = 4 * (QUADRANTS * s + q)
             nc.sync.dma_start(v_s[32 * q : 32 * q + 4, s, :].bitcast(I32), v_rows[first : first + 4, :].bitcast(I32))
 
+        w2_raw = [lane(f"w2_raw{s}", [P, PACK, H], F32, W2_RAW[s]) for s in range(PASSES)]
         load_tab(0)
         nc.sync.dma_start(w1_w[:], w1_words.rearrange("s p b -> p s b").bitcast(I32))
         load_w1_scales(0)
@@ -110,13 +113,12 @@ def tile_list_storm_index_cap_kernel(
         load_plane(1)
         for q in range(QUADRANTS):
             place_v_scales(0, q)
-        w2_raw = [load_weight(w2[0:K_PASS, :], "w2_raw0")]
+        load_weight(w2_raw[0], w2[0:K_PASS, :])
         for q in range(QUADRANTS):
             place_v_scales(1, q)
         load_plane(2)
-        w2_raw.append(load_weight(w2[K_PASS:K, :], "w2_raw1"))
-        for n in (3, 4, 5, 6, 7):
-            load_plane(n)
+        load_weight(w2_raw[1], w2[K_PASS:K, :])
+        load_plane(3)
 
         factor_a = keep.tile([P, SLICES], F32, name="factor_a")
         factor_b = keep.tile([P, SLICES], F32, name="factor_b")
@@ -128,15 +130,13 @@ def tile_list_storm_index_cap_kernel(
         def entries(first, width):
             return slice(first // STRIPE, (first + width) // STRIPE)
 
-        def pick(n, first, width, picked):
-            nc.vector.tensor_copy(picked, planes[n][:].indirect(list3[:, entries(first, width)]))
+        def pick(n, first, width, kib):
+            picked = lane(f"pick{n}_{first}", [P, width], F32, kib)
+            nc.vector.tensor_copy(picked[:], planes[n][:].indirect(list3[:, entries(first, width)]))
+            return picked
 
         def subtract(n, first, width, dest, picked):
             nc.vector.tensor_tensor(dest, planes[n][:].indirect(list2[:, entries(first, width)]), picked, ALU.subtract)
-
-        def difference(n, first, width, dest, picked):
-            pick(n, first, width, picked)
-            subtract(n, first, width, dest[:, n % PACK, :], picked)
 
         def interleave_into(grouped, src):
             nc.scalar.copy(
@@ -144,40 +144,31 @@ def tile_list_storm_index_cap_kernel(
                 src.rearrange("p i (c e) -> p c i e", e=RUN),
             )
 
-        def interleave(src, width, pool, name):
-            grouped = pool.tile([P, width * PACK], BF16, name=name, align_bytes=64)
-            interleave_into(grouped[:], src)
-            return grouped
-
-        def quantize(grouped, width, name):
-            codes = keep.tile([P, width], U32, name=f"{name}_codes", align_bytes=64)
+        def quantize(grouped, width, name, kib=None):
+            if kib is None:
+                codes = keep.tile([P, width], U32, name=f"{name}_codes", align_bytes=64)
+            else:
+                codes = lane(f"{name}_codes", [P, width], U32, kib)
             scales = keep.tile([P, width], U8, name=f"{name}_scales", align_bytes=64)
-            nc.vector.quantize_mx(codes[:].bitcast(E4M3), scales[:], grouped[:])
+            nc.vector.quantize_mx(codes[:].bitcast(E4M3), scales[:], grouped)
             return codes, scales
 
-        def round_weight(raw, pool, name):
-            grouped = pool.tile([P, H * PACK], BF16, name=name, align_bytes=64)
+        def round_weight(grouped, raw):
             nc.scalar.copy(
                 grouped[:].rearrange("p (t m i) -> p m i t", t=SLICES, i=PACK),
                 raw[:].rearrange("p i (m t) -> p m i t", t=SLICES),
             )
-            return grouped
 
-        x0 = [keep.tile([P, PACK, HALF], F32, name=f"x_planes{h}", align_bytes=64) for h in range(2)]
-        picks = []
+        x0 = lane("x0", [P, PACK, S], F32, X0)
 
-        def pick_tile(width):
-            picks.append(keep.tile([P, width], F32, name=f"picked{len(picks) % PICK_TILES}", align_bytes=64))
-            return picks[-1]
-
-        def both_halves(n):
+        def both_halves(n, slots):
+            taken = [pick(n, h * HALF, HALF, slots[h]) for h in range(2)]
             for h in range(2):
-                difference(n, h * HALF, HALF, x0[h], pick_tile(HALF)[:])
+                subtract(n, h * HALF, HALF, x0[:, n, h * HALF : (h + 1) * HALF], taken[h][:])
 
-        difference(0, 0, HALF, x0[0], pick_tile(HALF)[:])
-        difference(0, HALF, HALF, x0[1], keep.tile([P, HALF], F32, name="w1_codes", align_bytes=64)[:])
+        both_halves(0, (RING[0], W1_SLOT))
 
-        w1_codes = keep.tile([P, PASSES, H * 2], U8, name="w1_codes", align_bytes=64)
+        w1_codes = lane("w1_codes", [P, PASSES, H * 2], U8, W1_SLOT)
         w1_planes = keep.tile([P, PASSES, H], U8, name="w1_planes", align_bytes=64)
         nc.gpsimd.tensor_copy(
             w1_codes[:].rearrange("p s (t m b) -> p s t m b", t=SLICES, b=2),
@@ -191,14 +182,22 @@ def tile_list_storm_index_cap_kernel(
         def bank(n, shape):
             return psum.tile(shape, F32, name=f"bank{n}")
 
-        a_raw = keep.tile([P, SLICES, S], F32, name="a_raw")
-        a_scaled = [keep.tile([P, SLICES, HALF], F32, name=f"a_scaled{h}") for h in range(2)]
         v_w = [keep.tile([P, S], U32, name=f"v_w{s}", align_bytes=64) for s in range(PASSES)]
         for s in range(PASSES):
             nc.vector.tensor_copy(v_w[s][:], tab_w[s][:].bitcast(U32).indirect(list1[:]))
 
+        w3_raw = keep.tile([P, PACK, H], F32, name="tab_w0", align_bytes=64)
+        load_weight(w3_raw, w3)
+        for n in range(PACK, 2 * PACK):
+            load_plane(n)
+
+        w2_grouped = [lane(f"w2_grouped{s}", [P, H * PACK], BF16, W2_GROUPED[s]) for s in range(PASSES)]
+        for s in range(PASSES):
+            round_weight(w2_grouped[s], w2_raw[s])
+
+        a_raw = keep.tile([P, SLICES, S], F32, name="a_raw")
+        a_scaled0 = lane("a_scaled0", [P, SLICES, HALF], F32, A0)
         for h in range(2):
-            cols = slice(h * HALF, (h + 1) * HALF)
             for q in range(SLICES):
                 acc = bank(q, [P, HALF])
                 for s in range(PASSES):
@@ -206,58 +205,54 @@ def tile_list_storm_index_cap_kernel(
                         acc[:],
                         lhsT=w1_codes[:, s, 2 * P * q : 2 * P * (q + 1)].bitcast(E2M1),
                         lhsT_scale=w1_planes[:, s, P * q : P * (q + 1)],
-                        rhs=v_w[s][:, cols].bitcast(E4M3),
-                        rhs_scale=v_s[:, s, cols],
+                        rhs=v_w[s][:, (1 - h) * HALF : (2 - h) * HALF].bitcast(E4M3),
+                        rhs_scale=v_s[:, s, (1 - h) * HALF : (2 - h) * HALF],
                         start=(s == 0),
                         stop=(s == PASSES - 1),
                     )
-                nc.scalar.copy(a_raw[:, q, cols], acc[:])
-                nc.scalar.activation(a_scaled[h][:, q, :], acc[:], ACT.Copy, scale=factor_a[:, q : q + 1])
+                nc.scalar.copy(a_raw[:, q, (1 - h) * HALF : (2 - h) * HALF], acc[:])
+                if h == 1:
+                    nc.scalar.activation(a_scaled0[:, q, :], acc[:], ACT.Copy, scale=factor_a[:, q : q + 1])
 
-        w3_raw = load_weight(w3, "tab_w0")
-        both_halves(1)
-        w2_q = [quantize(round_weight(w2_raw[s], keep, f"w2_grouped{s}"), H, f"w2_{s}") for s in range(PASSES)]
-        both_halves(2)
-        both_halves(3)
+        both_halves(1, (RING[1], RING[0]))
+        w2_q = []
+        a_scaled1 = []
+        for s in range(PASSES):
+            n = 2 + s
+            picked = pick(n, 0, S, W2_RAW[s])
+            w2_q.append(quantize(w2_grouped[s][:], H, f"w2_{s}"))
+            subtract(n, 0, S, x0[:, n, :], picked[:])
+            for u in range(2):
+                q = 2 * s + u
+                a_scaled1.append(lane(f"a_scaled1_{q}", [P, HALF], F32, W2_RAW[s] + 2 * u))
+                nc.gpsimd.tensor_scalar(
+                    a_scaled1[q][:], a_raw[:, q, HALF:S], factor_a[:, q : q + 1], 0.0, ALU.mult, ALU.add
+                )
+
+        w3_grouped = keep.tile([P, H * PACK], BF16, name="tab_w1", align_bytes=64)
+        round_weight(w3_grouped, w3_raw)
         x0_grouped = [
-            lanes.tile([P, HALF * PACK], BF16, name="x0_grouped0", align_bytes=64, offset=0),
-            keep.tile([P, HALF * PACK], BF16, name="w2_grouped0", align_bytes=64),
+            keep.tile([P, HALF * PACK], BF16, name="x0_grouped0", align_bytes=64),
+            lane("x0_grouped1", [P, HALF * PACK], BF16, W2_GROUPED[0]),
         ]
         for h in range(2):
-            interleave_into(x0_grouped[h][:], x0[h][:])
-        x0_q = [quantize(x0_grouped[0], HALF, "x0_0")]
+            interleave_into(x0_grouped[h][:], x0[:, :, h * HALF : (h + 1) * HALF])
 
-        z_scales = keep.tile([P, S], U8, name="z_scales", align_bytes=64)
-
-        def gather_pair(h, pair, dest):
-            if h == 0 and pair == 0:
-                both = keep.tile([P, 2, HALF], F32, name="w2_grouped1", align_bytes=64)
-            taken = []
-            for u in range(2):
-                if h == 0 and pair == 0:
-                    picked = both[:, u, :]
-                elif h == 1 and u == 1:
-                    picked = keep.tile([P, HALF], F32, name="x1_grouped0", align_bytes=64)[:]
-                else:
-                    picked = lanes.tile(
-                        [P, HALF], F32, name=f"pick{h}_{pair}_{u}", align_bytes=64, offset=SLOT // 2 if h else u * SLOT
-                    )[:]
-                pick(PACK + 2 * pair + u, h * HALF, HALF, picked)
-                taken.append(picked)
-            width = CHUNK if h == 1 and pair == 1 else HALF
-            for off in range(0, HALF, width):
+        def gather_pair(h, pair, dests, slots):
+            taken = [pick(PACK + 2 * pair + u, h * HALF, HALF, slots[u]) for u in range(2)]
+            width = HALF // len(dests)
+            for c, dest in enumerate(dests):
                 for u in range(2):
                     i = 2 * pair + u
-                    part = slice(off, off + width)
-                    subtract(PACK + i, h * HALF + off, width, dest[:, i, part], taken[u][:, part])
+                    subtract(PACK + i, h * HALF + c * width, width, dest[:, i, :], taken[u][:, c * width : (c + 1) * width])
 
-        def product_b(c, x1_q):
+        def product_b(c, x1_q, first_bank):
             h, off = divmod(c * CHUNK, HALF)
             operands = [
                 (x0_q[h][0][:, off : off + CHUNK], x0_q[h][1][:, off : off + CHUNK]),
                 (x1_q[0][:], x1_q[1][:]),
             ]
-            banks = [bank(B_BANKS[c] + pair, [P, 2, CHUNK]) for pair in range(2)]
+            banks = [bank(first_bank + pair, [P, 2, CHUNK]) for pair in range(2)]
             for s in range(PASSES):
                 for q in range(SLICES):
                     nc.tensor.matmul_mx(
@@ -271,17 +266,20 @@ def tile_list_storm_index_cap_kernel(
                     )
             return banks
 
-        def blend_turned(c, banks, grouped):
-            first = c * CHUNK
-            b_scaled = keep.tile([P, SLICES, CHUNK], F32, name=f"w2_raw{c % 2}", align_bytes=64)
+        def scale_b(c, banks):
+            b_scaled = lane(f"b_scaled{c}", [P, SLICES, CHUNK], F32, W2_RAW[c] + 4)
             for q in range(SLICES):
                 nc.scalar.activation(
                     b_scaled[:, q, :], banks[q // 2][:, q % 2, :], ACT.Copy, scale=factor_b[:, q : q + 1]
                 )
+            return b_scaled
+
+        def blend_turned(c, b_scaled, grouped):
+            first = c * CHUNK
             words = bank(c, [P, 2, CHUNK])
             for j in range(CHUNK // P):
                 turned = bank(4 + 2 * c + j, [P, H])
-                terms = [a_scaled[0][:, :, first + j * P : first + (j + 1) * P], b_scaled[:, :, j * P : (j + 1) * P]]
+                terms = [a_scaled0[:, :, first + j * P : first + (j + 1) * P], b_scaled[:, :, j * P : (j + 1) * P]]
                 for n, term in enumerate(terms):
                     for q in range(SLICES):
                         nc.tensor.matmul(
@@ -292,7 +290,10 @@ def tile_list_storm_index_cap_kernel(
                             start=(n == 0 and q == 0),
                             stop=(n == 1 and q == SLICES - 1),
                         )
-                rounded = ring.tile([P, H], BF16, name="rounded")
+                if c == 1 and j == 1:
+                    rounded = lane("rounded_last", [P, H], BF16, LAST + 1.5)
+                else:
+                    rounded = keep.tile([P, H], BF16, name=f"rounded{2 * c + j}")
                 nc.scalar.copy(
                     rounded[:].rearrange("j (u p e) -> j u p e", u=2, e=2),
                     turned[:].rearrange("j (u e p) -> j u p e", u=2, e=2),
@@ -308,84 +309,75 @@ def tile_list_storm_index_cap_kernel(
             z = ring.tile([P, SLICES, CHUNK], BF16, name="z_slices")
             for q in range(SLICES):
                 nc.vector.scalar_tensor_tensor(
-                    z[:, q, :], banks[q // 2][:, q % 2, :], factor_b[:, q : q + 1], a_scaled[1][:, q, cols], ALU.mult, ALU.add
+                    z[:, q, :], banks[q // 2][:, q % 2, :], factor_b[:, q : q + 1], a_scaled1[q][:, cols], ALU.mult, ALU.add
                 )
-            return z
+            grouped = ring.tile([P, CHUNK * PACK], BF16, name="z_last", align_bytes=64)
+            interleave_into(grouped[:], z[:])
+            return grouped
 
-        def quantize_x1(c, grouped):
-            codes = keep.tile([P, CHUNK], U32, name=f"x1_codes{c}", align_bytes=64)
-            scales = keep.tile([P, CHUNK], U8, name=f"x1_scales{c}", align_bytes=64)
-            nc.vector.quantize_mx(codes[:].bitcast(E4M3), scales[:], grouped)
-            return codes, scales
-
-        def quantize_z(first, width, z_grouped):
-            cols = slice(first, first + width)
-            nc.vector.quantize_mx(z_codes[:, cols].bitcast(E4M3), z_scales[:, cols], z_grouped)
-
-        x1 = [keep.tile([P, PACK, HALF], F32, name="x_planes2")]
-        for pair in range(2):
-            gather_pair(0, pair, x1[0])
-        x0_q.append(
-            (
-                lanes.tile([P, HALF], U32, name="x0_1_codes", align_bytes=64, offset=3 * SLOT // 2),
-                keep.tile([P, HALF], U8, name="x0_1_scales", align_bytes=64),
-            )
-        )
-        nc.vector.quantize_mx(x0_q[1][0][:].bitcast(E4M3), x0_q[1][1][:], x0_grouped[1][:])
-        x1_q = []
-        for c, name in enumerate(("x1_grouped0", "x_planes1")):
-            grouped = interleave(x1[0][:, :, c * CHUNK : (c + 1) * CHUNK], CHUNK, keep, name)
-            x1_q.append(quantize_x1(c, grouped[:]))
-        z_words = keep.tile([P, 2 * HALF], F32, name="z_words", align_bytes=64)
-        first_banks = [product_b(c, x1_q[c]) for c in range(2)]
+        pick_slots = [(RING[0], RING[0] + 1), (RING[1], RING[1] + 1), (PAIR, PAIR + 1), (CODES + 1.5, PAIR + 3)]
+        x1a = [lane("x1a0", [P, PACK, CHUNK], F32, X1)]
+        later = []
+        for i in range(PACK):
+            taken = [pick(PACK + i, c * CHUNK, CHUNK, pick_slots[i][c]) for c in range(2)]
+            subtract(PACK + i, 0, CHUNK, x1a[0][:, i, :], taken[0][:])
+            later.append(taken[1])
+        first_grouped = [keep.tile([P, CHUNK * PACK], BF16, name=f"x1_grouped{c}", align_bytes=64) for c in range(2)]
+        interleave_into(first_grouped[0][:], x1a[0][:])
+        x0_q = [quantize(x0_grouped[0][:], HALF, "x0_0", CODES)]
+        w3_q = quantize(w3_grouped[:], H, "w3", CODES + 2)
+        x1_q = [quantize(first_grouped[0][:], CHUNK, "x1_0")]
+        x1a.append(lane("x1a1", [P, PACK, CHUNK], F32, X1 + 2))
+        for i in range(PACK):
+            subtract(PACK + i, CHUNK, CHUNK, x1a[1][:, i, :], later[i][:])
+        interleave_into(first_grouped[1][:], x1a[1][:])
+        x0_q.append(quantize(x0_grouped[1][:], HALF, "x0_1", PAIR + 1))
+        x1_q.append(quantize(first_grouped[1][:], CHUNK, "x1_1"))
+        z_words = lane("z_words", [P, 2 * HALF], F32, W2_GROUPED[1])
+        scaled = [scale_b(c, product_b(c, x1_q[c], 2 * c)) for c in range(2)]
         for c in range(2):
-            blend_turned(c, first_banks[c], z_words[:, 2 * CHUNK * c : 2 * CHUNK * (c + 1)])
-        w3_grouped = round_weight(w3_raw, keep, "tab_w1")
-        x1.append(keep.tile([P, PACK, HALF], F32, name="x_planes1", align_bytes=64))
-        for pair in range(2):
-            gather_pair(1, pair, x1[1])
+            blend_turned(c, scaled[c], z_words[:, 2 * CHUNK * c : 2 * CHUNK * (c + 1)])
+        x1b = lane("x1b", [P, PACK, HALF], F32, X1 + 4)
+        gather_pair(1, 0, [x1b[:]], (RING[0], X1 + 2))
+        gather_pair(1, 1, [x1b[:, :, 0:CHUNK], x1b[:, :, CHUNK:HALF]], (RING[0], X1 + 2))
+
+        z_q = {0: quantize(z_words[:].bitcast(BF16), HALF, "z_first")}
         banks = []
-        last_grouped = keep.tile([P, 2, CHUNK * PACK], BF16, name="w2_raw1", align_bytes=64)
         for c in (2, 3):
-            interleave_into(last_grouped[:, c - 2, :], x1[1][:, :, (c - 2) * CHUNK : (c - 1) * CHUNK])
-            banks.append(product_b(c, quantize_x1(c, last_grouped[:, c - 2, :])))
-        w3_q = (
-            lanes.tile([P, H], U32, name="w3_codes", align_bytes=64, offset=SLOT // 2),
-            keep.tile([P, H], U8, name="w3_scales", align_bytes=64),
-        )
-        nc.vector.quantize_mx(w3_q[0][:].bitcast(E4M3), w3_q[1][:], w3_grouped[:])
-        z_codes = keep.tile([P, S], U32, name="w2_raw1", align_bytes=64)
-        quantize_z(0, HALF, z_words[:].bitcast(BF16))
+            grouped = lane(f"x1_grouped{c}", [P, CHUNK * PACK], BF16, LAST + 2 * (c - 2))
+            interleave_into(grouped[:], x1b[:, :, (c - 2) * CHUNK : (c - 1) * CHUNK])
+            banks.append(product_b(c, quantize(grouped[:], CHUNK, f"x1_{c}"), 2 * c - 2))
         for c in (2, 3):
-            quantize_z(c * CHUNK, CHUNK, interleave(blend_direct(c, banks[c - 2])[:], CHUNK, ring, "z_last")[:])
+            z_q[c * CHUNK] = quantize(blend_direct(c, banks[c - 2])[:], CHUNK, f"z_{c}")
 
         out_rows = out.rearrange("(p q) j -> p q j", q=SLICES)
-        results = [keep.tile([P, SLICES, HALF], F32, name=f"a_scaled{1 - h}") for h in range(2)]
 
-        def finish(first, width):
+        def finish(first, width, q0, acc_bank, result):
             cols = slice(first, first + width)
-            h, off = divmod(first, HALF)
             per_bank = BANK // width
-            for q0 in range(0, SLICES, per_bank):
-                if h == 1:
-                    acc = bank(B_BANKS[first // CHUNK] + q0 // 2, [P, per_bank, width])
-                else:
-                    acc = bank((6 + q0) % 8, [P, per_bank, width])
-                for u in range(per_bank):
-                    q = q0 + u
-                    nc.tensor.matmul_mx(
-                        acc[:, u, :],
-                        lhsT=w3_q[0][:, P * q : P * (q + 1)].bitcast(E4M3),
-                        lhsT_scale=w3_q[1][:, P * q : P * (q + 1)],
-                        rhs=z_codes[:, cols].bitcast(E4M3),
-                        rhs_scale=z_scales[:, cols],
-                        start=True,
-                        stop=True,
-                    )
-                result = results[h][:, q0 : q0 + per_bank, off : off + width]
-                nc.vector.tensor_tensor(result, acc[:], a_raw[:, q0 : q0 + per_bank, cols], ALU.min)
-                nc.sync.dma_start(out_rows[:, q0 : q0 + per_bank, cols], result)
+            acc = bank(acc_bank, [P, per_bank, width])
+            for u in range(per_bank):
+                q = q0 + u
+                nc.tensor.matmul_mx(
+                    acc[:, u, :],
+                    lhsT=w3_q[0][:, P * q : P * (q + 1)].bitcast(E4M3),
+                    lhsT_scale=w3_q[1][:, P * q : P * (q + 1)],
+                    rhs=z_q[first][0][:].bitcast(E4M3),
+                    rhs_scale=z_q[first][1][:],
+                    start=True,
+                    stop=True,
+                )
+            nc.vector.tensor_tensor(result, acc[:], a_raw[:, q0 : q0 + per_bank, cols], ALU.min)
+            nc.sync.dma_start(out_rows[:, q0 : q0 + per_bank, cols], result)
 
-        finish(0, HALF)
-        for first in range(HALF, S, CHUNK):
-            finish(first, CHUNK)
+        for q, acc_bank in enumerate((6, 2, 3, 6)):
+            if q == 0:
+                result = keep.tile([P, 1, HALF], F32, name="result_first")
+            else:
+                result = lane(f"result{q}", [P, 1, HALF], F32, W2_RAW[q // 2] + 2 * (q % 2))
+            finish(0, HALF, q, acc_bank, result[:])
+        results = lane("results_last", [P, SLICES, HALF], F32, A0)
+        for c in (2, 3):
+            for pair in range(2):
+                off = (c - 2) * CHUNK
+                finish(c * CHUNK, CHUNK, 2 * pair, 4 * (c - 2) + pair, results[:, 2 * pair : 2 * pair + 2, off : off + CHUNK])

@@ -45,8 +45,8 @@ def tile_list_storm_index_cap_kernel(
         def lane(name, shape, dtype, kib):
             return lanes.tile(shape, dtype, name=name, align_bytes=64, offset=int(kib * KIB))
 
-        W2_RAW, RING, W1_SLOT, PAIR, X0, LAST, W2_GROUPED, A0 = (0, 8), (16, 18), 20, 22, 26, 42, (46, 50), 54
-        CODES, X1 = 62, 66
+        W2_RAW, RING, W1_SLOT, PAIR, X0, LAST, W2_GROUPED, A0 = (0, 24), (32, 34), 36, 38, 42, 58, (62, 66), 70
+        CODES, X1, A_RAW = 78, 84, 7.5
 
         list1 = lists.tile([P, S // STRIPE], U16, name="list1")
         list2 = lists.tile([P, S // STRIPE], U16, name="list2")
@@ -195,7 +195,7 @@ def tile_list_storm_index_cap_kernel(
         for s in range(PASSES):
             round_weight(w2_grouped[s], w2_raw[s])
 
-        a_raw = keep.tile([P, SLICES, S], F32, name="a_raw")
+        a_raw = lane("a_raw", [P, SLICES, S], F32, A_RAW)
         a_scaled0 = lane("a_scaled0", [P, SLICES, HALF], F32, A0)
         for h in range(2):
             for q in range(SLICES):
@@ -231,25 +231,13 @@ def tile_list_storm_index_cap_kernel(
 
         w3_grouped = keep.tile([P, H * PACK], BF16, name="tab_w1", align_bytes=64)
         round_weight(w3_grouped, w3_raw)
-        x0_grouped = [
-            keep.tile([P, HALF * PACK], BF16, name="x0_grouped0", align_bytes=64),
-            lane("x0_grouped1", [P, HALF * PACK], BF16, W2_GROUPED[0]),
-        ]
-        for h in range(2):
-            interleave_into(x0_grouped[h][:], x0[:, :, h * HALF : (h + 1) * HALF])
-
-        def gather_pair(h, pair, dests, slots):
-            taken = [pick(PACK + 2 * pair + u, h * HALF, HALF, slots[u]) for u in range(2)]
-            width = HALF // len(dests)
-            for c, dest in enumerate(dests):
-                for u in range(2):
-                    i = 2 * pair + u
-                    subtract(PACK + i, h * HALF + c * width, width, dest[:, i, :], taken[u][:, c * width : (c + 1) * width])
+        x0_grouped = lane("x0_grouped", [P, S * PACK], BF16, W2_GROUPED[0])
+        interleave_into(x0_grouped[:], x0[:])
 
         def product_b(c, x1_q, first_bank):
-            h, off = divmod(c * CHUNK, HALF)
+            cols = slice(c * CHUNK, (c + 1) * CHUNK)
             operands = [
-                (x0_q[h][0][:, off : off + CHUNK], x0_q[h][1][:, off : off + CHUNK]),
+                (x0_q[0][:, cols], x0_q[1][:, cols]),
                 (x1_q[0][:], x1_q[1][:]),
             ]
             banks = [bank(first_bank + pair, [P, 2, CHUNK]) for pair in range(2)]
@@ -267,24 +255,29 @@ def tile_list_storm_index_cap_kernel(
             return banks
 
         def scale_b(c, banks):
-            b_scaled = lane(f"b_scaled{c}", [P, SLICES, CHUNK], F32, W2_RAW[c] + 4)
+            b_scaled = lane(f"b_scaled{c}", [P, SLICES, CHUNK], F32, X0 + 4 * (c % 2))
             for q in range(SLICES):
                 nc.scalar.activation(
                     b_scaled[:, q, :], banks[q // 2][:, q % 2, :], ACT.Copy, scale=factor_b[:, q : q + 1]
                 )
             return b_scaled
 
+        a_scaled = [[a_scaled0[:, q, :] for q in range(SLICES)], [a_scaled1[q][:] for q in range(SLICES)]]
+
         def blend_turned(c, b_scaled, grouped):
-            first = c * CHUNK
-            words = bank(c, [P, 2, CHUNK])
+            words = bank((0, 1, 6)[c], [P, 2, CHUNK])
             for j in range(CHUNK // P):
-                turned = bank(4 + 2 * c + j, [P, H])
-                terms = [a_scaled0[:, :, first + j * P : first + (j + 1) * P], b_scaled[:, :, j * P : (j + 1) * P]]
+                turned = bank(4 + 2 * (c % 2) + j, [P, H])
+                first = (c % 2) * CHUNK + j * P
+                terms = [
+                    [a_scaled[c // 2][q][:, first : first + P] for q in range(SLICES)],
+                    [b_scaled[:, q, j * P : (j + 1) * P] for q in range(SLICES)],
+                ]
                 for n, term in enumerate(terms):
                     for q in range(SLICES):
                         nc.tensor.matmul(
                             turned[:, q * P : (q + 1) * P],
-                            lhsT=term[:, q, :],
+                            lhsT=term[q],
                             rhs=ident[:],
                             is_transpose=True,
                             start=(n == 0 and q == 0),
@@ -293,7 +286,7 @@ def tile_list_storm_index_cap_kernel(
                 if c == 1 and j == 1:
                     rounded = lane("rounded_last", [P, H], BF16, LAST + 1.5)
                 else:
-                    rounded = keep.tile([P, H], BF16, name=f"rounded{2 * c + j}")
+                    rounded = keep.tile([P, H], BF16, name=f"rounded{(2 * c + j) % 4}")
                 nc.scalar.copy(
                     rounded[:].rearrange("j (u p e) -> j u p e", u=2, e=2),
                     turned[:].rearrange("j (u e p) -> j u p e", u=2, e=2),
@@ -322,33 +315,50 @@ def tile_list_storm_index_cap_kernel(
             taken = [pick(PACK + i, c * CHUNK, CHUNK, pick_slots[i][c]) for c in range(2)]
             subtract(PACK + i, 0, CHUNK, x1a[0][:, i, :], taken[0][:])
             later.append(taken[1])
-        first_grouped = [keep.tile([P, CHUNK * PACK], BF16, name=f"x1_grouped{c}", align_bytes=64) for c in range(2)]
+        first_grouped = [lane(f"x1_grouped{c}", [P, CHUNK * PACK], BF16, X0 + 12 + 2 * c) for c in range(2)]
         interleave_into(first_grouped[0][:], x1a[0][:])
-        x0_q = [quantize(x0_grouped[0][:], HALF, "x0_0", CODES)]
-        w3_q = quantize(w3_grouped[:], H, "w3", CODES + 2)
+        x0_q = quantize(x0_grouped[:], S, "x0", CODES + 2)
         x1_q = [quantize(first_grouped[0][:], CHUNK, "x1_0")]
         x1a.append(lane("x1a1", [P, PACK, CHUNK], F32, X1 + 2))
         for i in range(PACK):
             subtract(PACK + i, CHUNK, CHUNK, x1a[1][:, i, :], later[i][:])
         interleave_into(first_grouped[1][:], x1a[1][:])
-        x0_q.append(quantize(x0_grouped[1][:], HALF, "x0_1", PAIR + 1))
+        taken = [pick(PACK, HALF, HALF, RING[0]), pick(PACK + 1, HALF, CHUNK, PAIR + 1)]
         x1_q.append(quantize(first_grouped[1][:], CHUNK, "x1_1"))
-        z_words = lane("z_words", [P, 2 * HALF], F32, W2_GROUPED[1])
+        z_words = lane("z_words", [P, 2 * HALF], F32, X0 + 8)
         scaled = [scale_b(c, product_b(c, x1_q[c], 2 * c)) for c in range(2)]
         for c in range(2):
             blend_turned(c, scaled[c], z_words[:, 2 * CHUNK * c : 2 * CHUNK * (c + 1)])
-        x1b = lane("x1b", [P, PACK, HALF], F32, X1 + 4)
-        gather_pair(1, 0, [x1b[:]], (RING[0], X1 + 2))
-        gather_pair(1, 1, [x1b[:, :, 0:CHUNK], x1b[:, :, CHUNK:HALF]], (RING[0], X1 + 2))
-
+        taken += [pick(PACK + i, HALF, CHUNK, X1 + i) for i in (2, 3)]
+        x1b = [lane("x1b2", [P, PACK, CHUNK], F32, X1 + 4)]
+        for i in range(PACK):
+            subtract(PACK + i, HALF, CHUNK, x1b[0][:, i, :], taken[i][:, 0:CHUNK])
+        last_grouped = [keep.tile([P, CHUNK * PACK], BF16, name="x1_grouped2", align_bytes=64)]
+        nc.gpsimd.tensor_scalar(
+            last_grouped[0][:].rearrange("p (j i) -> p j i", i=PACK),
+            x1b[0][:].rearrange("p i j -> p j i"),
+            1.0,
+            0.0,
+            ALU.mult,
+            ALU.add,
+        )
+        later = [taken[0][:, CHUNK:HALF]]
+        later += [pick(PACK + i, HALF + CHUNK, CHUNK, (PAIR + 1, X1 + 2, X1 + 3)[i - 1])[:] for i in (1, 2, 3)]
+        x1_q.append(quantize(last_grouped[0][:], CHUNK, "x1_2", CODES))
+        x1b.append(lane("x1b3", [P, PACK, CHUNK], F32, X1 + 6))
+        for i in range(PACK):
+            subtract(PACK + i, HALF + CHUNK, CHUNK, x1b[1][:, i, :], later[i])
+        scaled.append(scale_b(2, product_b(2, x1_q[2], 6)))
+        w3_q = quantize(w3_grouped[:], H, "w3", LAST + 1)
         z_q = {0: quantize(z_words[:].bitcast(BF16), HALF, "z_first")}
-        banks = []
-        for c in (2, 3):
-            grouped = lane(f"x1_grouped{c}", [P, CHUNK * PACK], BF16, LAST + 2 * (c - 2))
-            interleave_into(grouped[:], x1b[:, :, (c - 2) * CHUNK : (c - 1) * CHUNK])
-            banks.append(product_b(c, quantize(grouped[:], CHUNK, f"x1_{c}"), 2 * c - 2))
-        for c in (2, 3):
-            z_q[c * CHUNK] = quantize(blend_direct(c, banks[c - 2])[:], CHUNK, f"z_{c}")
+        last_grouped.append(lane("x1_grouped3", [P, CHUNK * PACK], BF16, CODES - 0.5))
+        interleave_into(last_grouped[1][:], x1b[1][:])
+        banks = product_b(3, quantize(last_grouped[1][:], CHUNK, "x1_3"), 2)
+        z_words2 = keep.tile([P, 2 * CHUNK], F32, name="x1_grouped2", align_bytes=64)
+        blend_turned(2, scaled[2], z_words2[:])
+        z_last = blend_direct(3, banks)
+        z_q[2 * CHUNK] = quantize(z_words2[:].bitcast(BF16), CHUNK, "z_2")
+        z_q[3 * CHUNK] = quantize(z_last[:], CHUNK, "z_3")
 
         out_rows = out.rearrange("(p q) j -> p q j", q=SLICES)
 
@@ -370,14 +380,10 @@ def tile_list_storm_index_cap_kernel(
             nc.vector.tensor_tensor(result, acc[:], a_raw[:, q0 : q0 + per_bank, cols], ALU.min)
             nc.sync.dma_start(out_rows[:, q0 : q0 + per_bank, cols], result)
 
-        for q, acc_bank in enumerate((6, 2, 3, 6)):
-            if q == 0:
-                result = keep.tile([P, 1, HALF], F32, name="result_first")
-            else:
-                result = lane(f"result{q}", [P, 1, HALF], F32, W2_RAW[q // 2] + 2 * (q % 2))
-            finish(0, HALF, q, acc_bank, result[:])
-        results = lane("results_last", [P, SLICES, HALF], F32, A0)
+        for q, acc_bank in enumerate((0, 1, 4, 5)):
+            finish(0, HALF, q, acc_bank, lane(f"result{q}", [P, 1, HALF], F32, (X1 + 6, X1 + 8, X0, X0 + 2)[q])[:])
+        results = lane("results_last", [P, SLICES, HALF], F32, W2_GROUPED[0])
         for c in (2, 3):
             for pair in range(2):
                 off = (c - 2) * CHUNK
-                finish(c * CHUNK, CHUNK, 2 * pair, 4 * (c - 2) + pair, results[:, 2 * pair : 2 * pair + 2, off : off + CHUNK])
+                finish(c * CHUNK, CHUNK, 2 * pair, (0, 1, 2, 3)[2 * (c - 2) + pair], results[:, 2 * pair : 2 * pair + 2, off : off + CHUNK])

@@ -155,7 +155,7 @@ def tile_list_storm_index_cap_kernel(
 
         def round_weight(grouped, raw):
             nc.scalar.copy(
-                grouped[:].rearrange("p (t m i) -> p m i t", t=SLICES, i=PACK),
+                grouped.rearrange("p (t m i) -> p m i t", t=SLICES, i=PACK),
                 raw[:].rearrange("p i (m t) -> p m i t", t=SLICES),
             )
 
@@ -193,7 +193,7 @@ def tile_list_storm_index_cap_kernel(
 
         w2_grouped = [lane(f"w2_grouped{s}", [P, H * PACK], BF16, W2_GROUPED[s]) for s in range(PASSES)]
         for s in range(PASSES):
-            round_weight(w2_grouped[s], w2_raw[s])
+            round_weight(w2_grouped[s][:], w2_raw[s])
 
         a_raw = lane("a_raw", [P, SLICES, S], F32, A_RAW)
         a_scaled0 = lane("a_scaled0", [P, SLICES, HALF], F32, A0)
@@ -229,8 +229,8 @@ def tile_list_storm_index_cap_kernel(
                     a_scaled1[q][:], a_raw[:, q, HALF:S], factor_a[:, q : q + 1], 0.0, ALU.mult, ALU.add
                 )
 
-        w3_grouped = keep.tile([P, H * PACK], BF16, name="tab_w1", align_bytes=64)
-        round_weight(w3_grouped, w3_raw)
+        w3_z = keep.tile([P, 2 * H * PACK], BF16, name="tab_w1", align_bytes=64)
+        round_weight(w3_z[:, 0 : H * PACK], w3_raw)
         x0_grouped = lane("x0_grouped", [P, S * PACK], BF16, W2_GROUPED[0])
         interleave_into(x0_grouped[:], x0[:])
 
@@ -305,7 +305,15 @@ def tile_list_storm_index_cap_kernel(
                     z[:, q, :], banks[q // 2][:, q % 2, :], factor_b[:, q : q + 1], a_scaled1[q][:, cols], ALU.mult, ALU.add
                 )
             grouped = ring.tile([P, CHUNK * PACK], BF16, name="z_last", align_bytes=64)
-            interleave_into(grouped[:], z[:])
+            interleave_into(grouped[:, 0 : P * PACK], z[:, :, 0:P])
+            nc.gpsimd.tensor_scalar(
+                grouped[:, P * PACK : CHUNK * PACK].rearrange("p (j i) -> p j i", i=PACK),
+                z[:, :, P:CHUNK].rearrange("p i j -> p j i"),
+                1.0,
+                0.0,
+                ALU.mult,
+                ALU.add,
+            )
             return grouped
 
         pick_slots = [(RING[0], RING[0] + 1), (RING[1], RING[1] + 1), (PAIR, PAIR + 1), (CODES + 1.5, PAIR + 3)]
@@ -325,7 +333,7 @@ def tile_list_storm_index_cap_kernel(
         interleave_into(first_grouped[1][:], x1a[1][:])
         taken = [pick(PACK, HALF, HALF, RING[0]), pick(PACK + 1, HALF, CHUNK, PAIR + 1)]
         x1_q.append(quantize(first_grouped[1][:], CHUNK, "x1_1"))
-        z_words = lane("z_words", [P, 2 * HALF], F32, X0 + 8)
+        z_words = w3_z[:, H * PACK : 2 * H * PACK].bitcast(F32)
         scaled = [scale_b(c, product_b(c, x1_q[c], 2 * c)) for c in range(2)]
         for c in range(2):
             blend_turned(c, scaled[c], z_words[:, 2 * CHUNK * c : 2 * CHUNK * (c + 1)])
@@ -349,16 +357,17 @@ def tile_list_storm_index_cap_kernel(
         for i in range(PACK):
             subtract(PACK + i, HALF + CHUNK, CHUNK, x1b[1][:, i, :], later[i])
         scaled.append(scale_b(2, product_b(2, x1_q[2], 6)))
-        w3_q = quantize(w3_grouped[:], H, "w3", LAST + 1)
-        z_q = {0: quantize(z_words[:].bitcast(BF16), HALF, "z_first")}
+        w3_q = quantize(w3_z[:], H + HALF, "w3_z", LAST - 0.5)
+        z_q = {0: (w3_q[0][:, H : H + HALF], w3_q[1][:, H : H + HALF])}
         last_grouped.append(lane("x1_grouped3", [P, CHUNK * PACK], BF16, CODES - 0.5))
         interleave_into(last_grouped[1][:], x1b[1][:])
         banks = product_b(3, quantize(last_grouped[1][:], CHUNK, "x1_3"), 2)
         z_words2 = keep.tile([P, 2 * CHUNK], F32, name="x1_grouped2", align_bytes=64)
         blend_turned(2, scaled[2], z_words2[:])
         z_last = blend_direct(3, banks)
-        z_q[2 * CHUNK] = quantize(z_words2[:].bitcast(BF16), CHUNK, "z_2")
-        z_q[3 * CHUNK] = quantize(z_last[:], CHUNK, "z_3")
+        for c, grouped in ((2, z_words2[:].bitcast(BF16)), (3, z_last[:])):
+            codes, scales = quantize(grouped, CHUNK, f"z_{c}")
+            z_q[c * CHUNK] = (codes[:], scales[:])
 
         out_rows = out.rearrange("(p q) j -> p q j", q=SLICES)
 
@@ -372,8 +381,8 @@ def tile_list_storm_index_cap_kernel(
                     acc[:, u, :],
                     lhsT=w3_q[0][:, P * q : P * (q + 1)].bitcast(E4M3),
                     lhsT_scale=w3_q[1][:, P * q : P * (q + 1)],
-                    rhs=z_q[first][0][:].bitcast(E4M3),
-                    rhs_scale=z_q[first][1][:],
+                    rhs=z_q[first][0].bitcast(E4M3),
+                    rhs_scale=z_q[first][1],
                     start=True,
                     stop=True,
                 )

@@ -45,7 +45,7 @@ def tile_list_storm_index_cap_kernel(
         def lane(name, shape, dtype, kib):
             return lanes.tile(shape, dtype, name=name, align_bytes=64, offset=int(kib * KIB))
 
-        W2_RAW, RING, W1_SLOT, PAIR, X0, LAST, W2_GROUPED, A0 = (0, 24), (32, 34), 36, 38, 42, 58, (62, 66), 70
+        W2_RAW, RING, W1_SLOT, PAIR, X0, LAST, W2_GROUPED, A0 = (0, 24), (32, 34), 36, 38, 42, 58, (62, 66), 94
         CODES, X1, A_RAW = 78, 84, 7.5
 
         list1 = lists.tile([P, S // STRIPE], U16, name="list1")
@@ -316,28 +316,32 @@ def tile_list_storm_index_cap_kernel(
             )
             return grouped
 
-        pick_slots = [(RING[0], RING[0] + 1), (RING[1], RING[1] + 1), (PAIR, PAIR + 1), (CODES + 1.5, PAIR + 3)]
         x1a = [lane("x1a0", [P, PACK, CHUNK], F32, X1)]
-        later = []
-        for i in range(PACK):
-            taken = [pick(PACK + i, c * CHUNK, CHUNK, pick_slots[i][c]) for c in range(2)]
-            subtract(PACK + i, 0, CHUNK, x1a[0][:, i, :], taken[0][:])
-            later.append(taken[1])
+        picked = pick(PACK, 0, CHUNK, RING[0])
+        taken = [pick(PACK, HALF, HALF, W1_SLOT)]
+        subtract(PACK, 0, CHUNK, x1a[0][:, 0, :], picked[:])
+        pick_slots = [(RING[1], RING[1] + 1), (PAIR, PAIR + 1), (CODES + 1.5, PAIR + 3)]
+        later = {}
+        for i in range(1, PACK):
+            pair = [pick(PACK + i, c * CHUNK, CHUNK, pick_slots[i - 1][c]) for c in range(2)]
+            subtract(PACK + i, 0, CHUNK, x1a[0][:, i, :], pair[0][:])
+            later[i] = pair[1]
         first_grouped = [lane(f"x1_grouped{c}", [P, CHUNK * PACK], BF16, X0 + 12 + 2 * c) for c in range(2)]
         interleave_into(first_grouped[0][:], x1a[0][:])
         x0_q = quantize(x0_grouped[:], S, "x0", CODES + 2)
+        later[0] = pick(PACK, CHUNK, CHUNK, CODES + 0.75)
         x1_q = [quantize(first_grouped[0][:], CHUNK, "x1_0")]
         x1a.append(lane("x1a1", [P, PACK, CHUNK], F32, X1 + 2))
-        for i in range(PACK):
+        for i in (1, 2, 3, 0):
             subtract(PACK + i, CHUNK, CHUNK, x1a[1][:, i, :], later[i][:])
         interleave_into(first_grouped[1][:], x1a[1][:])
-        taken = [pick(PACK, HALF, HALF, RING[0]), pick(PACK + 1, HALF, CHUNK, PAIR + 1)]
+        slots = (PAIR + 1, PAIR + 3, CODES + 0.75)
+        taken += [pick(PACK + i, HALF, CHUNK, slots[i - 1]) for i in (1, 2, 3)]
         x1_q.append(quantize(first_grouped[1][:], CHUNK, "x1_1"))
         z_words = w3_z[:, H * PACK : 2 * H * PACK].bitcast(F32)
         scaled = [scale_b(c, product_b(c, x1_q[c], 2 * c)) for c in range(2)]
         for c in range(2):
             blend_turned(c, scaled[c], z_words[:, 2 * CHUNK * c : 2 * CHUNK * (c + 1)])
-        taken += [pick(PACK + i, HALF, CHUNK, X1 + i) for i in (2, 3)]
         x1b = [lane("x1b2", [P, PACK, CHUNK], F32, X1 + 4)]
         for i in range(PACK):
             subtract(PACK + i, HALF, CHUNK, x1b[0][:, i, :], taken[i][:, 0:CHUNK])
@@ -351,15 +355,15 @@ def tile_list_storm_index_cap_kernel(
             ALU.add,
         )
         later = [taken[0][:, CHUNK:HALF]]
-        later += [pick(PACK + i, HALF + CHUNK, CHUNK, (PAIR + 1, X1 + 2, X1 + 3)[i - 1])[:] for i in (1, 2, 3)]
-        x1_q.append(quantize(last_grouped[0][:], CHUNK, "x1_2", CODES))
+        later += [pick(PACK + i, HALF + CHUNK, CHUNK, slots[i - 1])[:] for i in (1, 2, 3)]
+        x1_q.append(quantize(last_grouped[0][:], CHUNK, "x1_2", CODES - 0.5))
         x1b.append(lane("x1b3", [P, PACK, CHUNK], F32, X1 + 6))
         for i in range(PACK):
             subtract(PACK + i, HALF + CHUNK, CHUNK, x1b[1][:, i, :], later[i])
         scaled.append(scale_b(2, product_b(2, x1_q[2], 6)))
         w3_q = quantize(w3_z[:], H + HALF, "w3_z", LAST - 0.5)
         z_q = {0: (w3_q[0][:, H : H + HALF], w3_q[1][:, H : H + HALF])}
-        last_grouped.append(lane("x1_grouped3", [P, CHUNK * PACK], BF16, CODES - 0.5))
+        last_grouped.append(lane("x1_grouped3", [P, CHUNK * PACK], BF16, CODES - 2))
         interleave_into(last_grouped[1][:], x1b[1][:])
         banks = product_b(3, quantize(last_grouped[1][:], CHUNK, "x1_3"), 2)
         z_words2 = keep.tile([P, 2 * CHUNK], F32, name="x1_grouped2", align_bytes=64)
@@ -389,10 +393,10 @@ def tile_list_storm_index_cap_kernel(
             nc.vector.tensor_tensor(result, acc[:], a_raw[:, q0 : q0 + per_bank, cols], ALU.min)
             nc.sync.dma_start(out_rows[:, q0 : q0 + per_bank, cols], result)
 
-        for q, acc_bank in enumerate((0, 1, 4, 5)):
+        for q, acc_bank in enumerate((0, 5, 2, 3)):
             finish(0, HALF, q, acc_bank, lane(f"result{q}", [P, 1, HALF], F32, (X1 + 6, X1 + 8, X0, X0 + 2)[q])[:])
         results = lane("results_last", [P, SLICES, HALF], F32, W2_GROUPED[0])
         for c in (2, 3):
             for pair in range(2):
                 off = (c - 2) * CHUNK
-                finish(c * CHUNK, CHUNK, 2 * pair, (0, 1, 2, 3)[2 * (c - 2) + pair], results[:, 2 * pair : 2 * pair + 2, off : off + CHUNK])
+                finish(c * CHUNK, CHUNK, 2 * pair, (1, 4, 0, 5)[2 * (c - 2) + pair], results[:, 2 * pair : 2 * pair + 2, off : off + CHUNK])

@@ -184,7 +184,10 @@ def tile_list_storm_index_cap_kernel(
 
         v_w = [keep.tile([P, S], U32, name=f"v_w{s}", align_bytes=64) for s in range(PASSES)]
         for s in range(PASSES):
-            nc.vector.tensor_copy(v_w[s][:], tab_w[s][:].bitcast(U32).indirect(list1[:]))
+            for h in range(2):
+                nc.vector.tensor_copy(
+                    v_w[s][:, h * HALF : (h + 1) * HALF], tab_w[s][:].bitcast(U32).indirect(list1[:, entries(h * HALF, HALF)])
+                )
 
         w3_raw = keep.tile([P, PACK, H], F32, name="tab_w0", align_bytes=64)
         load_weight(w3_raw, w3)
@@ -219,9 +222,13 @@ def tile_list_storm_index_cap_kernel(
         a_scaled1 = []
         for s in range(PASSES):
             n = 2 + s
-            picked = pick(n, 0, S, W2_RAW[s])
+            picked = lane(f"pick{n}", [P, S], F32, W2_RAW[s])
+            halves = [slice(h * HALF, (h + 1) * HALF) for h in range(2)]
+            for cols in halves:
+                nc.vector.tensor_copy(picked[:, cols], planes[n][:].indirect(list3[:, entries(cols.start, HALF)]))
             w2_q.append(quantize(w2_grouped[s][:], H, f"w2_{s}"))
-            subtract(n, 0, S, x0[:, n, :], picked[:])
+            for cols in halves:
+                subtract(n, cols.start, HALF, x0[:, n, cols], picked[:, cols])
             for u in range(2):
                 q = 2 * s + u
                 a_scaled1.append(lane(f"a_scaled1_{q}", [P, HALF], F32, W2_RAW[s] + 2 * u))

@@ -45,7 +45,7 @@ def tile_list_storm_index_cap_kernel(
         def lane(name, shape, dtype, kib):
             return lanes.tile(shape, dtype, name=name, align_bytes=64, offset=int(kib * KIB))
 
-        W2_RAW, RING, W1_SLOT, PAIR, X0, LAST, W2_GROUPED, A0 = (0, 24), (32, 34), 36, 38, 42, 58, (62, 66), 94
+        W2_RAW, RING, W1_SLOT, PAIR, X0, LAST, W2_GROUPED, A0 = (0, 24), (32, 34), 36, 38, 42, 58, (62, 58), 94
         CODES, X1, A_RAW = 78, 84, 7.5
 
         list1 = lists.tile([P, S // STRIPE], U16, name="list1")
@@ -184,12 +184,9 @@ def tile_list_storm_index_cap_kernel(
 
         v_w = [keep.tile([P, S], U32, name=f"v_w{s}", align_bytes=64) for s in range(PASSES)]
         for s in range(PASSES):
-            for h in range(2):
-                nc.vector.tensor_copy(
-                    v_w[s][:, h * HALF : (h + 1) * HALF], tab_w[s][:].bitcast(U32).indirect(list1[:, entries(h * HALF, HALF)])
-                )
+            nc.vector.tensor_copy(v_w[s][:], tab_w[s][:].bitcast(U32).indirect(list1[:]))
 
-        w3_raw = keep.tile([P, PACK, H], F32, name="tab_w0", align_bytes=64)
+        w3_raw = lane("w3_raw", [P, PACK, H], F32, W2_GROUPED[0] + 7.5)
         load_weight(w3_raw, w3)
         for n in range(PACK, 2 * PACK):
             load_plane(n)
@@ -400,10 +397,10 @@ def tile_list_storm_index_cap_kernel(
             nc.vector.tensor_tensor(result, acc[:], a_raw[:, q0 : q0 + per_bank, cols], ALU.min)
             nc.sync.dma_start(out_rows[:, q0 : q0 + per_bank, cols], result)
 
-        for q, acc_bank in enumerate((0, 5, 2, 3)):
+        for q, acc_bank in enumerate((0, 1, 4, 5)):
             finish(0, HALF, q, acc_bank, lane(f"result{q}", [P, 1, HALF], F32, (X1 + 6, X1 + 8, X0, X0 + 2)[q])[:])
         results = lane("results_last", [P, SLICES, HALF], F32, W2_GROUPED[0])
         for c in (2, 3):
             for pair in range(2):
                 off = (c - 2) * CHUNK
-                finish(c * CHUNK, CHUNK, 2 * pair, (1, 4, 0, 5)[2 * (c - 2) + pair], results[:, 2 * pair : 2 * pair + 2, off : off + CHUNK])
+                finish(c * CHUNK, CHUNK, 2 * pair, (0, 1, 2, 3)[2 * (c - 2) + pair], results[:, 2 * pair : 2 * pair + 2, off : off + CHUNK])

from contextlib import ExitStack

import concourse.mybir as mybir
from concourse.masks import make_identity

K, H, T, S = 1024, 512, 2048, 1024
FLOPS = 2 * K * H * S * 2 + 2 * H * H * S

F32 = mybir.dt.float32
BF16 = mybir.dt.bfloat16
I32 = mybir.dt.int32
U32 = mybir.dt.uint32
U16 = mybir.dt.uint16
U8 = mybir.dt.uint8
E4M3 = mybir.dt.float8_e4m3fn_x4
E2M1 = mybir.dt.float4_e2m1fn_x4
ALU = mybir.AluOpType
ACT = mybir.ActivationFunctionType

P = 128
PACK = 4
K_PASS = P * PACK
PASSES = K // K_PASS
QUADRANTS = 4
SLICES = H // P
STRIPE = 16
HALF = 512
BANK = 512
RUN = 4
CHUNK = 256
KIB = 1024


def tile_list_storm_index_cap_kernel(
    tc, tab_words, tab_scales, w1_words, w1_scales, xT, w2, w3, lam, gain, offs, offs2, offs3, out
):
    nc = tc.nc
    with ExitStack() as ctx:
        lists = ctx.enter_context(tc.tile_pool(name="lists", bufs=1))
        keep = ctx.enter_context(tc.tile_pool(name="keep", bufs=1))
        ring = ctx.enter_context(tc.tile_pool(name="ring", bufs=2))
        lanes = ctx.enter_context(tc.tile_pool(name="lanes", bufs=1))
        psum = ctx.enter_context(tc.psum_pool(name="psum", bufs=1))

        def lane(name, shape, dtype, kib):
            return lanes.tile(shape, dtype, name=name, align_bytes=64, offset=int(kib * KIB))

        W2_RAW, RING, W1_SLOT, PAIR, X0, LAST, W2_GROUPED, A0 = (0, 24), (32, 34), 36, 38, 42, 58, (62, 58), 94
        CODES, X1, A_RAW = 78, 84, 7.5

        list1 = lists.tile([P, S // STRIPE], U16, name="list1")
        list2 = lists.tile([P, S // STRIPE], U16, name="list2")
        list3 = lists.tile([P, S // STRIPE], U16, name="list3")

        tab_s = keep.tile([P, T], U8, name="tab_s")
        w1_s = keep.tile([P, PASSES, H], U8, name="w1_s", align_bytes=64)
        v_s = keep.tile([P, PASSES, S], U8, name="v_s", align_bytes=64)
        nc.gpsimd.memset(tab_s[32:64, :].bitcast(I32), 0)
        nc.gpsimd.memset(tab_s[64:128, :].bitcast(I32), 0)
        nc.gpsimd.memset(v_s[:].rearrange("p s j -> p (s j)").bitcast(I32), 0)
        nc.gpsimd.memset(w1_s[:].rearrange("p s c -> p (s c)").bitcast(I32), 0)
        ident = keep.tile([P, P], F32, name="ident")
        make_identity(nc, ident[:])

        planes = [keep.tile([P, T], F32, name=f"plane{n}") for n in range(PASSES * PACK)]
        tab_w = [keep.tile([P, T], I32, name=f"tab_w{s}", align_bytes=64) for s in range(PASSES)]
        w1_w = keep.tile([P, PASSES, H // 2], I32, name="w1_w")
        lam_t = keep.tile([P, SLICES], F32, name="lam_t")
        gain_t = keep.tile([P, SLICES], F32, name="gain_t")
        x_rows = xT.rearrange("(s p i) t -> s i p t", s=PASSES, i=PACK)

        def load_plane(n):
            nc.sync.dma_start(planes[n][:], x_rows[n // PACK, n % PACK])

        def load_tab(s):
            nc.sync.dma_start(tab_w[s][:], tab_words[s].rearrange("p t i -> p (t i)").bitcast(I32))

        def load_weight(raw, rows):
            nc.sync.dma_start(raw[:], rows.rearrange("(p i) c -> p i c", i=PACK))

        def load_w1_scales(q):
            nc.sync.dma_start(
                w1_s[32 * q : 32 * q + 4, :, :].bitcast(I32),
                w1_scales[:, 4 * q : 4 * q + 4, :].rearrange("s r c -> r s c").bitcast(I32),
            )

        def load_channels(dest, vec):
            nc.sync.dma_start(dest[:], vec.rearrange("(p t) -> p t", t=SLICES))

        nc.sync.dma_start(list1[:], offs)
        nc.sync.dma_start(tab_s[0:32, :].bitcast(I32), tab_scales.rearrange("s g t -> (s g) t").bitcast(I32))
        load_plane(0)
        nc.sync.dma_start(list3[:], offs3)
        nc.sync.dma_start(list2[:], offs2)

        v_rows = keep.tile([P, S], U8, name="v_rows")
        nc.vector.tensor_copy(v_rows[:], tab_s[:].indirect(list1[:]))

        def place_v_scales(s, q):
            first = 4 * (QUADRANTS * s + q)
            nc.sync.dma_start(v_s[32 * q : 32 * q + 4, s, :].bitcast(I32), v_rows[first : first + 4, :].bitcast(I32))

        w2_raw = [lane(f"w2_raw{s}", [P, PACK, H], F32, W2_RAW[s]) for s in range(PASSES)]
        load_tab(0)
        nc.sync.dma_start(w1_w[:], w1_words.rearrange("s p b -> p s b").bitcast(I32))
        load_w1_scales(0)
        load_w1_scales(1)
        load_channels(lam_t, lam)
        load_tab(1)
        load_w1_scales(2)
        load_w1_scales(3)
        load_channels(gain_t, gain)
        load_plane(1)
        for q in range(QUADRANTS):
            place_v_scales(0, q)
        load_weight(w2_raw[0], w2[0:K_PASS, :])
        for q in range(QUADRANTS):
            place_v_scales(1, q)
        load_plane(2)
        load_weight(w2_raw[1], w2[K_PASS:K, :])
        load_plane(3)

        factor_a = keep.tile([P, SLICES], F32, name="factor_a")
        factor_b = keep.tile([P, SLICES], F32, name="factor_b")
        rest = keep.tile([P, SLICES], F32, name="rest")
        nc.gpsimd.tensor_tensor(factor_a[:], gain_t[:], lam_t[:], ALU.mult)
        nc.gpsimd.tensor_scalar(rest[:], lam_t[:], -1.0, 1.0, ALU.mult, ALU.add)
        nc.gpsimd.tensor_tensor(factor_b[:], gain_t[:], rest[:], ALU.mult)

        def entries(first, width):
            return slice(first // STRIPE, (first + width) // STRIPE)

        def pick(n, first, width, kib):
            picked = lane(f"pick{n}_{first}", [P, width], F32, kib)
            nc.vector.tensor_copy(picked[:], planes[n][:].indirect(list3[:, entries(first, width)]))
            return picked

        def subtract(n, first, width, dest, picked):
            nc.vector.tensor_tensor(dest, planes[n][:].indirect(list2[:, entries(first, width)]), picked, ALU.subtract)

        def interleave_into(grouped, src):
            nc.scalar.copy(
                grouped.rearrange("p (c e i) -> p c i e", e=RUN, i=PACK),
                src.rearrange("p i (c e) -> p c i e", e=RUN),
            )

        def quantize(grouped, width, name, kib=None):
            if kib is None:
                codes = keep.tile([P, width], U32, name=f"{name}_codes", align_bytes=64)
            else:
                codes = lane(f"{name}_codes", [P, width], U32, kib)
            scales = keep.tile([P, width], U8, name=f"{name}_scales", align_bytes=64)
            nc.vector.quantize_mx(codes[:].bitcast(E4M3), scales[:], grouped)
            return codes, scales

        def round_weight(grouped, raw):
            nc.scalar.copy(
                grouped.rearrange("p (t m i) -> p m i t", t=SLICES, i=PACK),
                raw[:].rearrange("p i (m t) -> p m i t", t=SLICES),
            )

        x0 = lane("x0", [P, PACK, S], F32, X0)

        def both_halves(n, slots):
            taken = [pick(n, h * HALF, HALF, slots[h]) for h in range(2)]
            for h in range(2):
                subtract(n, h * HALF, HALF, x0[:, n, h * HALF : (h + 1) * HALF], taken[h][:])

        both_halves(0, (RING[0], W1_SLOT))

        w1_codes = lane("w1_codes", [P, PASSES, H * 2], U8, W1_SLOT)
        w1_planes = keep.tile([P, PASSES, H], U8, name="w1_planes", align_bytes=64)
        nc.gpsimd.tensor_copy(
            w1_codes[:].rearrange("p s (t m b) -> p s t m b", t=SLICES, b=2),
            w1_w[:].bitcast(U8).rearrange("p s (m t b) -> p s t m b", t=SLICES, b=2),
        )
        nc.gpsimd.tensor_copy(
            w1_planes[:].rearrange("p s (t m) -> p s t m", t=SLICES),
            w1_s[:].rearrange("p s (m t) -> p s t m", t=SLICES),
        )

        def bank(n, shape):
            return psum.tile(shape, F32, name=f"bank{n}")

        v_w = [keep.tile([P, S], U32, name=f"v_w{s}", align_bytes=64) for s in range(PASSES)]
        for s in range(PASSES):
            nc.vector.tensor_copy(v_w[s][:], tab_w[s][:].bitcast(U32).indirect(list1[:]))

        w3_raw = lane("w3_raw", [P, PACK, H], F32, W2_GROUPED[0] + 7.5)
        load_weight(w3_raw, w3)
        for n in range(PACK, 2 * PACK):
            load_plane(n)

        w2_grouped = [lane(f"w2_grouped{s}", [P, H * PACK], BF16, W2_GROUPED[s]) for s in range(PASSES)]
        for s in range(PASSES):
            round_weight(w2_grouped[s][:], w2_raw[s])

        a_raw = lane("a_raw", [P, SLICES, S], F32, A_RAW)
        a_scaled0 = lane("a_scaled0", [P, SLICES, HALF], F32, A0)
        for h in range(2):
            for q in range(SLICES):
                acc = bank(q, [P, HALF])
                for s in range(PASSES):
                    nc.tensor.matmul_mx(
                        acc[:],
                        lhsT=w1_codes[:, s, 2 * P * q : 2 * P * (q + 1)].bitcast(E2M1),
                        lhsT_scale=w1_planes[:, s, P * q : P * (q + 1)],
                        rhs=v_w[s][:, (1 - h) * HALF : (2 - h) * HALF].bitcast(E4M3),
                        rhs_scale=v_s[:, s, (1 - h) * HALF : (2 - h) * HALF],
                        start=(s == 0),
                        stop=(s == PASSES - 1),
                    )
                nc.scalar.copy(a_raw[:, q, (1 - h) * HALF : (2 - h) * HALF], acc[:])
                if h == 1:
                    nc.scalar.activation(a_scaled0[:, q, :], acc[:], ACT.Copy, scale=factor_a[:, q : q + 1])

        both_halves(1, (RING[1], RING[0]))
        w2_q = []
        a_scaled1 = []
        for s in range(PASSES):
            n = 2 + s
            picked = lane(f"pick{n}", [P, S], F32, W2_RAW[s])
            halves = [slice(h * HALF, (h + 1) * HALF) for h in range(2)]
            for cols in halves:
                nc.vector.tensor_copy(picked[:, cols], planes[n][:].indirect(list3[:, entries(cols.start, HALF)]))
            w2_q.append(quantize(w2_grouped[s][:], H, f"w2_{s}"))
            for cols in halves:
                subtract(n, cols.start, HALF, x0[:, n, cols], picked[:, cols])
            for u in range(2):
                q = 2 * s + u
                a_scaled1.append(lane(f"a_scaled1_{q}", [P, HALF], F32, W2_RAW[s] + 2 * u))
                nc.gpsimd.tensor_scalar(
                    a_scaled1[q][:], a_raw[:, q, HALF:S], factor_a[:, q : q + 1], 0.0, ALU.mult, ALU.add
                )

        w3_z = keep.tile([P, 2 * H * PACK], BF16, name="tab_w1", align_bytes=64)
        round_weight(w3_z[:, 0 : H * PACK], w3_raw)
        x0_grouped = lane("x0_grouped", [P, S * PACK], BF16, W2_GROUPED[0])
        interleave_into(x0_grouped[:], x0[:])

        def product_b(c, x1_q, first_bank):
            cols = slice(c * CHUNK, (c + 1) * CHUNK)
            operands = [
                (x0_q[0][:, cols], x0_q[1][:, cols]),
                (x1_q[0][:], x1_q[1][:]),
            ]
            banks = [bank(first_bank + pair, [P, 2, CHUNK]) for pair in range(2)]
            for s in range(PASSES):
                for q in range(SLICES):
                    nc.tensor.matmul_mx(
                        banks[q // 2][:, q % 2, :],
                        lhsT=w2_q[s][0][:, P * q : P * (q + 1)].bitcast(E4M3),
                        lhsT_scale=w2_q[s][1][:, P * q : P * (q + 1)],
                        rhs=operands[s][0].bitcast(E4M3),
                        rhs_scale=operands[s][1],
                        start=(s == 0 and q % 2 == 0),
                        stop=(s == PASSES - 1 and q % 2 == 1),
                    )
            return banks

        def scale_b(c, banks):
            b_scaled = lane(f"b_scaled{c}", [P, SLICES, CHUNK], F32, X0 + 4 * (c % 2))
            for q in range(SLICES):
                nc.scalar.activation(
                    b_scaled[:, q, :], banks[q // 2][:, q % 2, :], ACT.Copy, scale=factor_b[:, q : q + 1]
                )
            return b_scaled

        a_scaled = [[a_scaled0[:, q, :] for q in range(SLICES)], [a_scaled1[q][:] for q in range(SLICES)]]

        def blend_turned(c, b_scaled, grouped):
            words = bank((0, 1, 6)[c], [P, 2, CHUNK])
            for j in range(CHUNK // P):
                turned = bank(4 + 2 * (c % 2) + j, [P, H])
                first = (c % 2) * CHUNK + j * P
                terms = [
                    [a_scaled[c // 2][q][:, first : first + P] for q in range(SLICES)],
                    [b_scaled[:, q, j * P : (j + 1) * P] for q in range(SLICES)],
                ]
                for n, term in enumerate(terms):
                    for q in range(SLICES):
                        nc.tensor.matmul(
                            turned[:, q * P : (q + 1) * P],
                            lhsT=term[q],
                            rhs=ident[:],
                            is_transpose=True,
                            start=(n == 0 and q == 0),
                            stop=(n == 1 and q == SLICES - 1),
                        )
                if c == 1 and j == 1:
                    rounded = lane("rounded_last", [P, H], BF16, LAST + 1.5)
                else:
                    rounded = keep.tile([P, H], BF16, name=f"rounded{(2 * c + j) % 4}")
                nc.scalar.copy(
                    rounded[:].rearrange("j (u p e) -> j u p e", u=2, e=2),
                    turned[:].rearrange("j (u e p) -> j u p e", u=2, e=2),
                )
                for u in range(2):
                    nc.tensor.transpose(
                        words[:, u, j * P : (j + 1) * P], rounded[:].bitcast(F32)[:, u * P : (u + 1) * P], ident[:]
                    )
            nc.scalar.copy(grouped.rearrange("p (j u) -> p j u", u=2), words[:].rearrange("p u j -> p j u"))

        def blend_direct(c, banks):
            cols = slice(c * CHUNK - HALF, (c + 1) * CHUNK - HALF)
            z = ring.tile([P, SLICES, CHUNK], BF16, name="z_slices")
            for q in range(SLICES):
                nc.vector.scalar_tensor_tensor(
                    z[:, q, :], banks[q // 2][:, q % 2, :], factor_b[:, q : q + 1], a_scaled1[q][:, cols], ALU.mult, ALU.add
                )
            grouped = ring.tile([P, CHUNK * PACK], BF16, name="z_last", align_bytes=64)
            interleave_into(grouped[:, 0 : P * PACK], z[:, :, 0:P])
            nc.gpsimd.tensor_scalar(
                grouped[:, P * PACK : CHUNK * PACK].rearrange("p (j i) -> p j i", i=PACK),
                z[:, :, P:CHUNK].rearrange("p i j -> p j i"),
                1.0,
                0.0,
                ALU.mult,
                ALU.add,
            )
            return grouped

        x1a = [lane("x1a0", [P, PACK, CHUNK], F32, X1)]
        picked = pick(PACK, 0, CHUNK, RING[0])
        taken = [pick(PACK, HALF, HALF, W1_SLOT)]
        subtract(PACK, 0, CHUNK, x1a[0][:, 0, :], picked[:])
        pick_slots = [(RING[1], RING[1] + 1), (PAIR, PAIR + 1), (CODES + 1.5, PAIR + 3)]
        later = {}
        for i in range(1, PACK):
            pair = [pick(PACK + i, c * CHUNK, CHUNK, pick_slots[i - 1][c]) for c in range(2)]
            subtract(PACK + i, 0, CHUNK, x1a[0][:, i, :], pair[0][:])
            later[i] = pair[1]
        first_grouped = [lane(f"x1_grouped{c}", [P, CHUNK * PACK], BF16, X0 + 12 + 2 * c) for c in range(2)]
        interleave_into(first_grouped[0][:], x1a[0][:])
        x0_q = quantize(x0_grouped[:], S, "x0", CODES + 2)
        later[0] = pick(PACK, CHUNK, CHUNK, CODES + 0.75)
        x1_q = [quantize(first_grouped[0][:], CHUNK, "x1_0")]
        x1a.append(lane("x1a1", [P, PACK, CHUNK], F32, X1 + 2))
        for i in (1, 2, 3, 0):
            subtract(PACK + i, CHUNK, CHUNK, x1a[1][:, i, :], later[i][:])
        interleave_into(first_grouped[1][:], x1a[1][:])
        slots = (PAIR + 1, PAIR + 3, CODES + 0.75)
        taken += [pick(PACK + i, HALF, CHUNK, slots[i - 1]) for i in (1, 2, 3)]
        x1_q.append(quantize(first_grouped[1][:], CHUNK, "x1_1"))
        z_words = w3_z[:, H * PACK : 2 * H * PACK].bitcast(F32)
        scaled = [scale_b(c, product_b(c, x1_q[c], 2 * c)) for c in range(2)]
        for c in range(2):
            blend_turned(c, scaled[c], z_words[:, 2 * CHUNK * c : 2 * CHUNK * (c + 1)])
        x1b = [lane("x1b2", [P, PACK, CHUNK], F32, X1 + 4)]
        for i in range(PACK):
            subtract(PACK + i, HALF, CHUNK, x1b[0][:, i, :], taken[i][:, 0:CHUNK])
        last_grouped = [keep.tile([P, CHUNK * PACK], BF16, name="x1_grouped2", align_bytes=64)]
        nc.gpsimd.tensor_scalar(
            last_grouped[0][:].rearrange("p (j i) -> p j i", i=PACK),
            x1b[0][:].rearrange("p i j -> p j i"),
            1.0,
            0.0,
            ALU.mult,
            ALU.add,
        )
        later = [taken[0][:, CHUNK:HALF]]
        later += [pick(PACK + i, HALF + CHUNK, CHUNK, slots[i - 1])[:] for i in (1, 2, 3)]
        x1_q.append(quantize(last_grouped[0][:], CHUNK, "x1_2", CODES - 0.5))
        x1b.append(lane("x1b3", [P, PACK, CHUNK], F32, X1 + 6))
        for i in range(PACK):
            subtract(PACK + i, HALF + CHUNK, CHUNK, x1b[1][:, i, :], later[i])
        scaled.append(scale_b(2, product_b(2, x1_q[2], 6)))
        w3_q = quantize(w3_z[:], H + HALF, "w3_z", LAST - 0.5)
        z_q = {0: (w3_q[0][:, H : H + HALF], w3_q[1][:, H : H + HALF])}
        last_grouped.append(lane("x1_grouped3", [P, CHUNK * PACK], BF16, CODES - 2))
        interleave_into(last_grouped[1][:], x1b[1][:])
        banks = product_b(3, quantize(last_grouped[1][:], CHUNK, "x1_3"), 2)
        z_words2 = keep.tile([P, 2 * CHUNK], F32, name="x1_grouped2", align_bytes=64)
        blend_turned(2, scaled[2], z_words2[:])
        z_last = blend_direct(3, banks)
        for c, grouped in ((2, z_words2[:].bitcast(BF16)), (3, z_last[:])):
            codes, scales = quantize(grouped, CHUNK, f"z_{c}")
            z_q[c * CHUNK] = (codes[:], scales[:])

        out_rows = out.rearrange("(p q) j -> p q j", q=SLICES)

        def finish(first, width, q0, acc_bank, result):
            cols = slice(first, first + width)
            per_bank = BANK // width
            acc = bank(acc_bank, [P, per_bank, width])
            for u in range(per_bank):
                q = q0 + u
                nc.tensor.matmul_mx(
                    acc[:, u, :],
                    lhsT=w3_q[0][:, P * q : P * (q + 1)].bitcast(E4M3),
                    lhsT_scale=w3_q[1][:, P * q : P * (q + 1)],
                    rhs=z_q[first][0].bitcast(E4M3),
                    rhs_scale=z_q[first][1],
                    start=True,
                    stop=True,
                )
            nc.vector.tensor_tensor(result, acc[:], a_raw[:, q0 : q0 + per_bank, cols], ALU.min)
            nc.sync.dma_start(out_rows[:, q0 : q0 + per_bank, cols], result)

        for q, acc_bank in enumerate((0, 1, 4, 5)):
            finish(0, HALF, q, acc_bank, lane(f"result{q}", [P, 1, HALF], F32, (X1 + 6, X1 + 8, X0, X0 + 2)[q])[:])
        results = lane("results_last", [P, SLICES, HALF], F32, W2_GROUPED[0])
        for c in (2, 3):
            for pair in range(2):
                off = (c - 2) * CHUNK
                finish(c * CHUNK, CHUNK, 2 * pair, (0, 1, 2, 3)[2 * (c - 2) + pair], results[:, 2 * pair : 2 * pair + 2, off : off + CHUNK])
